import numpy as np, ml_dtypes
CORES = [35,38,43,46]
N = 4
BF = ml_dtypes.bfloat16
def gentries(a):
    return np.ascontiguousarray(a.reshape(8, 16, -1).transpose(0, 2, 1)).reshape(8, -1)
def gtable(e):
    e = np.asarray(e); return np.ascontiguousarray(e.reshape(8, -1, 16).transpose(0, 2, 1)).reshape(128, -1).astype(np.int32)
V, D, SD, L, M, P, RO, ST = 2048, 4, 2, 256, 1024, 64, 3, 2
DV, E = D * V, (N - 1) * L
def wire(rng, nm, no, vd, od=None, oa=None):
    if od is None: od = np.argsort(rng.random((N, 8, DV)), axis=2)
    if oa is None: oa = np.argsort(rng.random((N, 8, DV)), axis=2)
    a = np.full((N, 8, DV), -1, np.int64); b = np.full((N, 8, DV), -1, np.int64)
    ni = np.zeros((N, 8), np.int64); nu = np.zeros((N, 8), np.int64)
    for g in range(8):
        for q in range(N):
            for h in range(N - 1):
                r = (q + h + 1) % N; m = int(nm[q, g, h]); n = m + int(no[q, g, h])
                c = DV + D * (h * L + rng.permutation(L)[:n])
                i = int(nu[q, g]); b[q, g, oa[q, g, i:i + n]] = c; nu[q, g] += n
                i = int(ni[r, g]); a[r, g, od[r, g, i:i + m]] = c[:m]; ni[r, g] += m
        for q in range(N):
            i, j = int(ni[q, g]), int(nu[q, g]); n = max(min(DV - i - int(vd[q, g]), DV - j), 0)
            sd = od[q, g, i:i + n]; sa = oa[q, g, j:j + n]; a[q, g, sd] = sa; b[q, g, sa] = sd
    return a, b
def parts(rng):
    x = rng.integers(0, 16, (N, 8, 16, V))
    nm = rng.integers(L // 2, 3 * L // 4, (N, 8, N - 1)); no = rng.integers(0, L // 8 + 1, (N, 8, N - 1))
    vd = rng.integers(M // 2, 3 * M // 2, (N, 8)); p = np.zeros((N, 8, 4 + RO), np.int64)
    p[..., 0] = rng.integers(95, 112, (N, 8)); p[..., 1] = rng.integers(112, 150, (N, 8)); p[..., 2] = rng.integers(130, 147, (N, 8))
    p[..., 3] = 2 * rng.integers(0, 1024, (N, 8)) + 1; p[..., 4:] = rng.integers(0, DV, (N, 8, RO))
    return x, nm, no, vd, p
def pack(x, ab, p):
    return {"x0": np.ascontiguousarray(x.reshape(N, 128, V)).astype(BF), "den": np.stack([gtable(c) for c in ab[0]]), "axo": np.stack([gtable(c) for c in ab[1]]), "par": p.astype(np.int32)}
def setup_inputs(rng):
    x, nm, no, vd, p = parts(rng)
    return pack(x, wire(rng, nm, no, vd), p)
def setup_inputs_caps(rng):
    x, nm, no, vd, p = parts(rng); p[..., 0] = 0; p[..., 1] = 241; p[..., 2] = 241
    nm[:] = rng.choice(np.array([0, 1, L // 2, L - 1, L]), (1, 8, N - 1)); nm[:, 3:5] = L // 2
    no[:] = np.minimum(rng.choice(np.array([0, 1, 7, L]), no.shape), L - nm); no[1, :, 0] = L - nm[1, :, 0]; no[1, 3:5, N - 2] = 5
    nm[:, 5] = 0; no[1:, 5] = L; no[0] = 0
    vd[:] = rng.choice(np.array([0, 1, M - 1, M, M + 1, 2 * M]), (N, 8)); vd[0] = np.array([M, M + 1, M - 1, 0, 1, 2 * M, M, 5])
    return pack(x, wire(rng, nm, no, vd), p)
def setup_inputs_full(rng):
    x, nm, no, vd, p = parts(rng); nm[:] = L; no[:] = 0; vd[:] = 0
    p[..., 0] = rng.integers(105, 136, (N, 8)); p[..., 1] = rng.integers(90, 242, (N, 8)); p[..., 2] = rng.integers(105, 136, (N, 8))
    return pack(x, wire(rng, nm, no, vd), p)
def setup_inputs_alike(rng):
    x, nm, no, vd, p = parts(rng)
    od = np.argsort(rng.random((N, 8, DV)), axis=2); oa = np.argsort(rng.random((N, 8, DV)), axis=2); o = np.arange(DV)
    od[:, 0] = o; oa[:, 0] = o; od[:, 1] = o[::-1]; oa[:, 2] = o[::-1]
    for q in range(N):
        od[q, 3] = (D * rng.permutation(V)[:, None] + np.arange(D)).reshape(-1); oa[q, 3] = (D * rng.permutation(V)[:, None] + np.arange(D)).reshape(-1)
    x[:, 0:4:2] = 2 * rng.integers(0, 8, (N, 2, 1, 1)) + 1; x[:, 1:4:2] = rng.integers(0, 16, (N, 2, 1, V))
    p[:, :4, 0] = 16 * rng.integers(3, 8, (N, 4)); p[:, :4, 1] = 16 * rng.integers(7, 16, (N, 4)); p[:, :4, 2] = 16 * rng.integers(8, 13, (N, 4))
    p[:, 0::4, 3] = 1; p[:, 0::4, 4:] = 0; p[:, 1::4, 3] = 2047; p[:, 1::4, 4:] = DV - 1
    return pack(x, wire(rng, nm, no, vd, od, oa), p)
def setup_inputs_bare(rng):
    x, nm, no, vd, p = parts(rng); g = rng.permutation(8); q = int(rng.integers(0, N))
    nm[:, g[0]] = 0; no[:, g[0]] = 0; vd[:, g[0]] = DV
    nm[:, g[1]] = 0; no[:, g[1]] = rng.integers(0, L + 1, (N, N - 1)); vd[:, g[1]] = M
    vd[:, g[2]] = DV
    p[:, g[3], :3] = np.array([0, 0, 241]); p[:, g[4], :3] = np.array([241, 241, 0])
    nm[q] = 0; no[q] = 0
    return pack(x, wire(rng, nm, no, vd), p)
def setup_inputs_spread(rng):
    x, nm, no, vd, p = parts(rng)
    x = np.minimum((np.exp2(4.2 * rng.random((N, 8, 1, V))) * rng.random(x.shape)).astype(np.int64), 15)
    p[..., :3] = rng.integers(0, 242, (N, 8, 3))
    nm = rng.integers(0, L + 1, nm.shape); no = ((L - nm + 1) * rng.random(nm.shape)).astype(np.int64)
    vd = np.exp2(12.9 * rng.random((N, 8))).astype(np.int64)
    return pack(x, wire(rng, nm, no, vd), p)
def ends(c):
    o = np.full((N, 8, E), -1, np.int64); n, g, i = np.nonzero(c >= DV)
    o[n, g, (c[n, g, i] - DV) >> SD] = i
    return o
def gone(c, f):
    return (c >= DV) & np.take_along_axis(f, np.maximum(c - DV, 0) >> SD, 2)
def check_inputs(d):
    bad = []
    x = np.asarray(d["x0"]).astype(np.float32); p = np.asarray(d["par"]).astype(np.int64)
    if not np.all((x >= 0) & (x <= 15) & (x == np.floor(x))): bad.append("range of x0")
    if not np.all((p[..., :3] >= 0) & (p[..., :3] <= 241)): bad.append("range of the thresholds in par")
    if not np.all((p[..., 3] >= 1) & (p[..., 3] <= 2047) & ((p[..., 3] & 1) == 1)): bad.append("K in par")
    if not np.all((p[..., 4:] >= 0) & (p[..., 4:] < DV)): bad.append("C in par")
    a = np.stack([gentries(c) for c in d["den"]]).astype(np.int64); b = np.stack([gentries(c) for c in d["axo"]]).astype(np.int64)
    out = False
    for k, c in (("den", a), ("axo", b)):
        if not np.all((c >= -1) & (c < DV + D * E) & ((c < DV) | ((c & (D - 1)) == 0))): bad.append("range of " + k); out = True
    if out: return bad
    for k, c, o in (("den", a, b), ("axo", b, a)):
        n, g, i = np.nonzero(c >= DV); key = (n * 8 + g) * E + ((c[n, g, i] - DV) >> SD)
        if np.unique(key).size != key.size: bad.append("a link that stands twice in " + k)
        n, g, i = np.nonzero((c >= 0) & (c < DV))
        if np.any(o[n, g, c[n, g, i]] != i): bad.append("twins of " + k)
    ie, oe = ends(a), ends(b)
    for r in range(N):
        for h in range(1, N):
            z = slice((h - 1) * L, h * L)
            if np.any((ie[r][:, z] >= 0) & (oe[(r - h) % N][:, z] < 0)): bad.append("a link in den that no axonal slot holds")
    return sorted(set(bad))
def reference(x0, den, axo, par):
    x = np.asarray(x0).astype(np.float32).astype(np.int32).reshape(N, 8, 16, V)
    a = np.stack([gentries(c) for c in den]).astype(np.int64); b = np.stack([gentries(c) for c in axo]).astype(np.int64); p = par.astype(np.int64)
    blocks = [(r, (r - h) % N, slice((h - 1) * L, h * L)) for r in range(N) for h in range(1, N)]
    for t in range(RO):
        oe = ends(b)
        for k in range(ST):
            new, far = [], []
            for r in range(N):
                w = [x[r]]
                for h in range(1, N):
                    q = (r - h) % N; i = oe[q][:, (h - 1) * L:h * L]
                    w.append(np.take_along_axis(x[q], np.maximum(i, 0)[:, None, :] >> SD, 2) * (i >= 0)[:, None, :])
                w = np.concatenate(w, axis=2); held = a[r] >= 0
                v = (np.take_along_axis(w, np.maximum(a[r], 0)[:, None, :] >> SD, 2) * held[:, None, :]).reshape(8, 16, V, D)
                if k == ST - 1: far.append(np.where(held.reshape(8, V, D), np.add.reduce(np.abs(v - x[r][..., None]), axis=1), -1))
                new.append((x[r] + np.add.reduce(v, axis=3)) & 15)
            x = np.stack(new).astype(np.int32)
        far = np.stack(far); s = np.add.reduce(x, axis=2)
        best = np.argmax(far, axis=3)
        kd = ((s >= p[..., 2:3])[..., None] & (far >= 0) & (np.arange(D) == best[..., None])).reshape(N, 8, DV)
        ka = ((s < p[..., 0:1])[..., None] & (np.arange(D) == t)).reshape(N, 8, DV) & (b >= 0)
        mb = np.zeros((N, 8, DV + D * E), bool); n, g, i = np.nonzero(kd); mb[n, g, a[n, g, i]] = True
        ma = np.zeros((N, 8, DV + D * E), bool); n, g, i = np.nonzero(ka); ma[n, g, b[n, g, i]] = True
        gi = np.zeros((N, 8, E), bool); go = np.zeros((N, 8, E), bool)
        for r, q, z in blocks:
            gi[r][:, z] = ma[q][:, DV::D][:, z]; go[q][:, z] = mb[r][:, DV::D][:, z]
        a = np.where(kd | ma[..., :DV] | gone(a, gi), -1, a); b = np.where(ka | mb[..., :DV] | gone(b, go), -1, b)
        oe, ie = ends(b), ends(a); opn = np.zeros((N, 8, E), bool)
        for r, q, z in blocks: opn[r][:, z] = (oe[q][:, z] >= 0) & (ie[r][:, z] < 0)
        z0 = (t % (N - 1)) * L
        for r in range(N):
            for g in range(8):
                vac = np.nonzero((a[r, g] < 0) & np.repeat(s[r, g] < p[r, g, 1], D))[0][:M]
                links = np.nonzero(opn[r, g])[0]; o = (p[r, g, 3] * np.arange(DV) + p[r, g, 4 + t]) & (DV - 1); fr = o[b[r, g][o] < 0]
                giv = np.concatenate([DV + D * links, fr]); m = min(len(vac), len(giv)); u = max(m - len(links), 0)
                a[r, g, vac[:m]] = giv[:m]
                b[r, g, fr[:u]] = vac[m - u:m]
                rest = fr[u:u + P]; free = np.nonzero(oe[r, g, z0:z0 + L] < 0)[0]; n = min(len(rest), len(free))
                b[r, g, rest[:n]] = DV + D * (z0 + free[:n])
    return {"yx": x.reshape(N, 128, V).astype(np.float32).astype(BF), "yd": np.stack([gtable(c) for c in a]).astype(np.float32), "ya": np.stack([gtable(c) for c in b]).astype(np.float32)}

@@ -1,0 +1,704 @@
+from concourse.bass import DstId, RemoteDMATransfer
+from concourse.mybir import AluOpType as A, AxisListType, ActivationFunctionType as F
+
+N, RO = 4, 3
+XW = 16 + 2048 + 768
+UAW, BWW, L1W = 10048, 14528, 2752
+NS = 7
+f32, bf, f16, i32, u16 = "float32", "bfloat16", "float16", "int32", "uint16"
+
+
+def sb(n, t):
+    return ("sbuf", [128, n], t)
+
+
+SCRATCH = {
+    "xw0": sb(XW, bf), "xw1": sb(XW, bf), "V": sb(8192, bf), "VA": sb(9280, bf), "snd": sb(768, bf),
+    "UA": sb(UAW, f32), "BW": sb(BWW, f32), "L1": sb(L1W, f32), "zer": sb(1088, f32),
+    "dT": sb(1088, f32), "dG": sb(1088, f32), "cw": sb(1088, f16), "M": sb(1088, bf),
+    "io1": sb(1088, f32), "cdat": sb(560, f32),
+    "deni": sb(512, i32), "axoi": sb(512, i32), "pari": sb(8, i32), "parf": sb(8, f32), "pc": sb(8, f32),
+    "wa": sb(560, f32), "wb": sb(560, f32), "tmpA": sb(560, f32), "AI": sb(560, i32), "Af": sb(512, f32),
+    "vacm": sb(512, bf), "off": sb(560, u16), "joff": sb(512, u16), "jio": sb(512, f32), "pj": sb(4, i32), "tab": sb(560, f32),
+    "flT": sb(560, f16), "flG": sb(560, f16), "flE": sb(768, f16), "cum": sb(576, f16), "kh": sb(256, f32), "km": sb(256, f32),
+    "BI": sb(176, f32), "Bn": sb(128, f32), "pdA": sb(176, f32), "pdL": sb(48, f32), "held": sb(48, f32), "alive": sb(48, f32),
+    "i1": sb(176, i32), "i2": sb(176, i32), "i3": sb(176, i32), "i4": sb(176, i32),
+    "f1": sb(176, f32), "f2": sb(176, f32), "f3": sb(176, f32), "f4": sb(176, f32), "f5": sb(176, f32),
+    "mx": sb(128, f32), "mg": sb(128, f32), "thr": sb(128, f32), "pdK": sb(128, f32),
+    "oK": sb(128, u16), "oA": sb(176, u16), "oL": sb(48, u16), "o1": sb(36, u16), "o2": sb(68, u16), "oT": sb(68, u16), "oG": sb(68, u16),
+    "oS": sb(68, u16), "oV": sb(68, u16), "pdV": sb(68, f32), "dumV": sb(68, f32),
+    "se": sb(36, f32), "cf": sb(68, f32), "nn": sb(136, f32), "vT": sb(68, f32), "vG": sb(68, f32), "valT": sb(136, f32), "valG": sb(136, f32),
+    "pdT": sb(68, f32), "col": sb(16, f32), "loe": sb(48, f32), "msg": sb(48, f32), "IEp": sb(48, f32),
+    "lor0": sb(48, f32), "lor1": sb(48, f32), "lor2": sb(48, f32), "lsr0": sb(48, f32), "lsr1": sb(48, f32), "lsr2": sb(48, f32),
+    "pi": sb(8, i32), "pf": sb(24, f32), "yrow": sb(144, f32), "gsel": sb(128, f32),
+    "Zb": sb(144, bf), "Zk": sb(144, bf), "Zr": sb(144, bf), "Zq": sb(144, bf), "Z1b": sb(144, bf),
+    "Zh": sb(144, f16), "Z1h": sb(144, f16), "Z16": sb(144, f16), "Z1f": sb(144, f32),
+    "Ib": sb(128, bf), "I4": sb(128, bf), "In": sb(128, bf), "If": sb(128, f32),
+    "BOh": sb(128, f16), "BOf": sb(128, f32), "TRI": sb(128, f16),
+    "Pf": sb(576, f32), "Qh": sb(576, f16), "cb": sb(1280, bf),
+    "Dc": sb(36, f32), "CL": sb(36, f32), "gam": sb(68, f32), "thg": sb(68, f32), "dumA": sb(176, f32), "dumB": sb(128, f32),
+}
+for _k in ("P0", "P1", "P2", "P3", "PK", "PS", "PX", "PY"):
+    SCRATCH[_k] = ("psum", [128, 512], f32)
+DMAS = ["ld_x", "ld_d", "ld_a", "ld_p", "bw", "bw2", "ua", "uar", "bt", "bn", "dT", "dG", "yx", "yd", "ya"]
+SEMAPHORES = ["qv", "qs", "qt", "qg"] + ["d_" + n for n in DMAS] + ["ar%d" % k for k in range(13)] + ["lo%d" % k for k in range(13)]
+
+
+def rank_program(g, core, T, topo):
+    rank = T.rank_of(core)
+    if rank is None:
+        return
+    Q = {"v": g.vector, "s": g.scalar, "t": g.tensor, "g": g, "y": g.sync}
+    cnt = {}
+    seen = {q: {} for q in Q}
+    wr, rd = {}, {}
+
+    def wait(q, toks):
+        need = {}
+        for s, n in toks:
+            need[s] = max(need.get(s, 0), cnt[s] if s[:2] == "d_" else n)
+        for s, n in need.items():
+            if seen[q].get(s, 0) < n:
+                Q[q].wait_ge(T.sem[s], n)
+                seen[q][s] = n
+
+    def deps(q, R, W):
+        toks = []
+        for r in R:
+            if r in wr:
+                toks.append(wr[r])
+        for w in W:
+            if w in wr:
+                toks.append(wr[w])
+            toks.extend(rd.get(w, []))
+        if q == "t":
+            toks = [t for t in toks if t[0] != "qt"]
+        wait(q, toks)
+
+    def done(tok, R, W):
+        for r in R:
+            rd.setdefault(r, []).append(tok)
+        for w in W:
+            wr[w] = tok
+            rd[w] = []
+
+    def op(q, ins, R, W):
+        R, W = R.split(), W.split()
+        W = W + [r for r in R if r[0] == "P" and r != "Pf"]
+        deps(q, R, W)
+        s = "q" + q
+        ins().then_inc(T.sem[s], 1)
+        cnt[s] = cnt.get(s, 0) + 1
+        done((s, cnt[s]), R, W)
+
+    def mm(out, terms, R, W, first=True, end=True):
+        def ins():
+            last = None
+            for k, (l, r) in enumerate(terms):
+                last = g.tensor.matmul(out, l, r, first and k == 0, end and k == len(terms) - 1)
+            return last
+        op("t", ins, R, W)
+
+    def dma(name, pairs, R, W, q="y"):
+        R, W = R.split(), W.split()
+        deps(q, R, W)
+        s = "d_" + name
+        for o, i in pairs:
+            Q[q].dma_start(o, i).then_inc(T.sem[s], 16)
+            cnt[s] = cnt.get(s, 0) + 16
+        done((s, cnt[s]), R, W)
+
+    def engines_of(src):
+        peers = [c for c in T.cores if c != src]
+        far = [c for c in peers if topo.chip(c) != topo.chip(src)]
+        near = [c for c in peers if topo.chip(c) == topo.chip(src)]
+        out, used = {}, set()
+        for grp in (far, near):
+            for k, c in enumerate(grp):
+                free = [e for e in topo.engines(src, c) if e not in used]
+                n = len(free) // (len(grp) - k)
+                while n & (n - 1):
+                    n -= 1
+                out[c] = free[:n]
+                used.update(free[:n])
+        return out
+
+    nx = [0]
+
+    def exchange(src, dst, d0, w, sign, R, W):
+        k = nx[0]
+        nx[0] += 1
+        deps("g", [R], [])
+        mine = engines_of(core)
+        tr, tot, arr = [], 0, 0
+        for h in range(1, N):
+            c = T.cores[(rank + sign * h) % N]
+            rid, pid = topo.addr(c)[:2]
+            tr.append(RemoteDMATransfer(dst_ids=[DstId(rid=rid, pnc=pid)], dma_engine_mask=sum(1 << e for e in mine[c]),
+                                        remote_sem=T.sem["ar%d" % k], src=src[:, (h - 1) * w:h * w], dst=dst[:, d0 + (h - 1) * w:d0 + h * w]))
+            tot += len(mine[c])
+            arr += len(engines_of(c)[core])
+        g.remote_dma_fused(tr, local_sem=T.sem["lo%d" % k])
+        cnt["lo%d" % k] = tot
+        cnt["ar%d" % k] = arr
+        done(("lo%d" % k, tot), [R], [])
+        done(("ar%d" % k, arr), [], [W])
+
+    v = g.vector
+
+    def ts(out, in0, s1, o0, R, W, s2=None, o1=None):
+        if o1 is None:
+            op("v", lambda: v.tensor_scalar(out, in0, s1, None, o0), R, W)
+        else:
+            op("v", lambda: v.tensor_scalar(out, in0, s1, s2, o0, o1), R, W)
+
+    def tt(out, a, b, o, R, W):
+        op("v", lambda: v.tensor_tensor(out, a, b, o), R, W)
+
+    def cp(out, a, R, W):
+        op("v", lambda: v.tensor_copy(out, a), R, W)
+
+    def ms(ap, c, W):
+        op("v", lambda: v.memset(ap, c), "", W)
+
+    def act(out, a, f, R, W, **kw):
+        op("s", lambda: g.scalar.activation(out, a, f, **kw), R, W)
+
+    def iota(out, pat, base, cm, W, flt=True):
+        if flt:
+            op("g", lambda: g.iota(out, pat, base, cm, allow_small_or_imprecise_dtypes=True), "", W)
+        else:
+            op("g", lambda: g.iota(out, pat, base, cm), "", W)
+
+    def conv(out, Z, rhs, R, W, more=(), first=True, end=True):
+        mm(out, list(more) + [(Z[:, 15 - r:143 - r], rhs(r)) for r in range(16)], R, W, first, end)
+
+    def run(fs):
+        for f in fs:
+            f()
+
+    xw = [T.xw0, T.xw1]
+    row = slice(0, 128, 16)
+    SH, AND = A.arith_shift_right, A.bitwise_and
+
+    dma("ld_a", [(T.axoi[:], T.axo[:])], "", "axoi")
+    dma("ld_d", [(T.deni[:], T.den[:])], "", "deni", q="s")
+    dma("ld_x", [(T.xw0[:, 16:2064], T.x0[:])], "", "x0_0 x0_1 x0_2 x0_3")
+    dma("ld_p", [(T.pari[0:8, 0:7], T.par[:])], "", "pari", q="s")
+    iota(T.pi[:, 0:1], [[0, 1]], 0, 1, "pi0", flt=False)
+    iota(T.yrow[:], [[1, 144]], 0, 0, "yrow")
+    iota(T.cdat[:], [[1, 35], [35, 16]], 0, 0, "cdat")
+    iota(T.io1[:], [[1, 1088]], 1, 0, "io1")
+    iota(T.gsel[0:8, :], [[1, 8], [0, 16]], 0, -1, "gsel")
+    iota(T.jio[:], [[1, 512]], 0, 0, "jio")
+    ms(T.zer[:], 0.0, "zer")
+    pf = T.pf
+    ts(T.pi[:, 1:2], T.pi[:, 0:1], 15, AND, "pi0", "pi1")
+    ts(T.pi[:, 2:3], T.pi[:, 0:1], 112, AND, "pi0", "pi2")
+    ts(T.pi[:, 3:4], T.pi[:, 0:1], 3, AND, "pi0", "pi3")
+    ts(T.pi[:, 4:5], T.pi[:, 0:1], 2, SH, "pi0", "pi4", 3, AND)
+    ts(T.pi[:, 5:6], T.pi[:, 0:1], 8, AND, "pi0", "pi5")
+    cp(pf[:, 0:6], T.pi[:, 0:6], "pi0 pi1 pi2 pi3 pi4 pi5", "pfa")
+    ts(pf[:, 6:7], pf[:, 2:3], 15.0, A.add, "pfa", "pf6")
+    ts(pf[:, 7:8], pf[:, 1:2], 0.0, A.is_equal, "pfa", "pf7")
+    ts(pf[:, 8:9], pf[:, 1:2], 16.0, A.add, "pfa", "pf8")
+    ts(pf[:, 9:10], pf[:, 7:8], 16.0, A.mult, "pf7", "pf9")
+    ts(pf[:, 10:11], pf[:, 1:2], 35.0, A.mult, "pfa", "pf10")
+    ms(T.flG[:, 512:560], 0.0, "flG1")
+    ms(T.flT[:, 512:560], 0.0, "flT1")
+    ms(T.cum[:, 0:1], 0.0, "cum0")
+    ms(T.wb[:, 512:560], 0.0, "wb")
+    for Z, w, n in ((T.Zh, 1.0, "Zh"), (T.Z1h, pf[:, 7:8], "Z1h"), (T.Zr, pf[:, 8:9], "Zr"), (T.Zq, pf[:, 1:2], "Zq"),
+                    (T.Z16, pf[:, 9:10], "Z16"), (T.Z1f, pf[:, 7:8], "Z1f")):
+        ts(Z[:], T.yrow[:], pf[:, 6:7], A.is_equal, "yrow pf6 pf7 pf8 pf9 pfa", n, w, A.mult)
+    ts(T.f1[:, 0:128], T.yrow[:, 0:128], pf[:, 6:7], A.is_le, "yrow pf6", "f1")
+    ts(T.f2[:, 0:128], T.yrow[:, 0:128], pf[:, 2:3], A.is_ge, "yrow pfa", "f2")
+    ts(T.f3[:, 0:128], T.yrow[:, 0:128], pf[:, 0:1], A.is_ge, "yrow pfa", "f3")
+    tt(T.BOh[:], T.f1[:, 0:128], T.f2[:, 0:128], A.mult, "f1 f2", "BOh")
+    tt(T.TRI[:], T.f1[:, 0:128], T.f3[:, 0:128], A.mult, "f1 f3", "TRI")
+    ts(T.Dc[:], T.yrow[:, 0:36], pf[:, 10:11], A.add, "yrow pf10", "Dc", 1089.0, A.add)
+    ts(T.gam[:], T.yrow[:, 0:68], 16.0, A.mult, "yrow pfa", "gam", pf[:, 1:2], A.add)
+
+    def clear_l1():
+        act(T.L1[:, 0:1088], T.zer[:], F.Copy, "zer", "L1")
+    clear_l1()
+    act(T.dT[:], T.zer[:], F.Copy, "zer", "dT")
+    act(T.dG[:], T.zer[:], F.Copy, "zer", "dG")
+    for b, c0 in enumerate((8384, 10432)):
+        act(T.BW[:, c0:c0 + 768], T.zer[:, 0:768], F.Identity, "zer", "Bg%d" % b, bias=63.0)
+    for k in range(3):
+        act(T.BW[:, 1024 * k:1024 * k + 1024], T.zer[:, 0:1024], F.Copy, "zer", "Bi%d" % k)
+    for k in range(3, 8):
+        iota(T.BW[:, 1024 * k:1024 * k + 1024], [[0, 1024]], 0, 0, "Bi%d" % k)
+    for k in range(4):
+        iota(T.BW[:, 8192 + 2048 * k:8384 + 2048 * k], [[0, 192]], 64, 0, "BL")
+
+    def compact(fl, fn, no, clamp, h1=(), h2=(), h3=()):
+        n = 16 * no
+        conv(T.PX[:, 0:36], T.Zh, lambda r: T.cum[:, 35 * r:35 * r + 36], "Zh cum cum0", "PX")
+        mm(T.P0[:], [(T.BOh[:], T.cum[:, 0:512]), (T.TRI[:], fl[:, 0:512])], "BOh TRI cum cum0 " + fn, "P0")
+        mm(T.P1[:, 0:48], [(T.BOh[:], T.cum[:, 512:560]), (T.TRI[:], fl[:, 512:560])], "BOh TRI cum " + fn, "P1")
+        run(h1)
+        if clamp:
+            tt(T.se[:], T.PX[:, 0:36], T.CL[:], A.min, "PX CL", "se")
+        else:
+            ts(T.se[:], T.PX[:, 0:36], 1088.0, A.min, "PX", "se")
+        tt(T.f1[:, 0:35], T.se[:, 1:36], T.se[:, 0:35], A.is_le, "se", "f1")
+        tt(T.f1[:, 0:35], T.f1[:, 0:35], T.Dc[:, 0:35], A.mult, "f1 Dc", "f1")
+        tt(T.f1[:, 0:35], T.f1[:, 0:35], T.se[:, 0:35], A.add, "f1 se", "f1")
+        cp(T.o1[:, 0:35], T.f1[:, 0:35], "f1", "o1")
+        cp(T.L1[:].indirect(T.o1[:, 0:35]), T.cdat[:], "o1 cdat", "L1")
+        run(h2)
+        op("v", lambda: v.tensor_tensor_scan(T.cw[:, 0:n], T.L1[:, 0:n], T.L1[:, 0:n], 0.0, A.max, A.max), "L1", "cw")
+        conv(T.PX[:, 64:64 + no], T.Z1h, lambda r: T.cw[:, r:n:16], "Z1h cw", "PX")
+        conv(T.PY[:, 128:128 + no], T.Z16, lambda r: T.cw[:, no * r:no * r + no], "Z16 cw", "PY", end=False)
+        run(h3)
+        tt(T.tab[:, 0:512], T.P0[:], fl[:, 0:512], A.mult, "P0 " + fn, "tab0")
+        tt(T.tab[:, 512:560], T.P1[:, 0:48], fl[:, 512:560], A.mult, "P1 " + fn, "tab1")
+        cp(T.o2[:, 0:no], T.PX[:, 64:64 + no], "PX", "o2")
+        ts(T.cf[:, 0:no], T.PX[:, 64:64 + no], 16.0, A.mult, "PX", "cf", -16.0, A.add)
+        tt(T.M[:, 0:n], T.tab[:].indirect(T.o2[:, 0:no]), T.io1[:, 0:n], A.is_equal, "tab0 tab1 o2 io1", "M rr0 rr1")
+        conv(T.PY[:, 128:128 + no], T.Zq, lambda r: T.M[:, no * r:no * r + no], "Zq M", "PY", first=False)
+        conv(T.PX[:, 192:192 + no], T.Zr, lambda r: T.M[:, r:n:16], "Zr M", "PX")
+
+    def scan(fl, fn, a, b, init, R=""):
+        op("v", lambda: v.tensor_tensor_scan(T.cum[:, a + 1:b + 1], fl[:, a:b], fl[:, a:b], init, A.add, A.max), fn + " " + R, "cum")
+
+    def invert(src, sn, c0, gn, d, dn, ol, on, bank, h1=(), h2=(), h3=()):
+        ts(T.flG[:, 0:512], src[:], 8192.0, A.is_ge, sn, "flG0")
+        scan(T.flG, "flG0 flG1", 0, 560, 0.0)
+        ts(T.wb[:, 0:512], src[:], -8192.0, A.add, sn, "wb", 0.25, A.mult)
+        compact(T.flG, "flG0 flG1", 48, False, h1, h2, h3)
+        clear_l1()
+        tt(T.flE[:], T.wb[:].indirect(T.o2[:, 0:48]), T.M[:, 0:768], A.mult, "wb o2 M", "Eh")
+        act(T.valT[:, 0:48], T.PY[:, 128:176], F.Identity, "PY", "valT", bias=64.0)
+        dma(dn, [(d[row, 0:768], T.valT[:, 0:48])], "valT", dn)
+        conv(T.PK[:, 0:48], T.Zh, lambda r: T.flE[:, r:768:16], "Zh Eh", "PK")
+        ts(T.f1[:, 0:48], T.PX[:, 192:240], 16.0, A.is_ge, "PX", "f1")
+        ts(T.f3[:, 0:48], T.gam[:, 0:48], 768.0, A.add, "gam", "f3")
+        tt(T.f2[:, 0:48], T.PK[:, 0:48], T.f3[:, 0:48], A.subtract, "PK f3", "f2")
+        tt(T.f2[:, 0:48], T.f2[:, 0:48], T.f1[:, 0:48], A.mult, "f1 f2", "f2")
+        tt(T.f2[:, 0:48], T.f2[:, 0:48], T.f3[:, 0:48], A.add, "f2 f3", "f2")
+        cp(ol, T.f2[:, 0:48], "f2", on)
+        return (lambda: act(T.BW[:, c0:c0 + 1536].indirect(ol), d[:, 0:768], F.Silu, on + " " + dn, gn),
+                lambda: conv(T[bank][:, 0:48], T.Z1f, lambda r: T.BW[:, c0 + r:c0 + 768:16], "Z1f " + gn, bank))
+
+    def pos_b(I, In, n, dum, dn, out, on):
+        ts(T.i2[:, 0:n], I, 15, AND, In, "i2")
+        ts(T.i3[:, 0:n], I, 4, SH, In, "i3", 1023, AND)
+        ts(T.f1[:, 0:n], T.i2[:, 0:n], 512.0, A.mult, "i2", "f1")
+        ts(T.f2[:, 0:n], T.i3[:, 0:n], 512.0, A.is_ge, "i3", "f2", 7680.0, A.mult)
+        tt(T.f1[:, 0:n], T.f1[:, 0:n], T.i3[:, 0:n], A.add, "f1 i3", "f1")
+        tt(T.f2[:, 0:n], T.f2[:, 0:n], dum, A.subtract, "f2 " + dn, "f2")
+        tt(out, T.f1[:, 0:n], T.f2[:, 0:n], A.add, "f1 f2", on)
+
+    def pos_a(I, In, n, out, on):
+        ts(T.i2[:, 0:n], I, 2, SH, In, "i2", 15, AND)
+        ts(T.i3[:, 0:n], I, 3, AND, In, "i3")
+        ts(T.i4[:, 0:n], I, 6, SH, In, "i4")
+        ts(T.f1[:, 0:n], T.i2[:, 0:n], 560.0, A.mult, "i2", "f1")
+        ts(T.f2[:, 0:n], T.i3[:, 0:n], 128.0, A.mult, "i3", "f2")
+        ts(T.f3[:, 0:n], T.i4[:, 0:n], 128.0, A.is_ge, "i4", "f3", 384.0, A.mult)
+        tt(T.f1[:, 0:n], T.f1[:, 0:n], T.i4[:, 0:n], A.add, "f1 i4", "f1")
+        tt(T.f2[:, 0:n], T.f2[:, 0:n], T.dumA[:, 0:n], A.subtract, "f2 dumA", "f2")
+        tt(T.f1[:, 0:n], T.f1[:, 0:n], T.f3[:, 0:n], A.add, "f1 f3", "f1")
+        tt(out, T.f1[:, 0:n], T.f2[:, 0:n], A.add, "f1 f2", on)
+
+    def pick(out, on, pd, pn, flag, fn, dum, dn, n):
+        t = T.f4[:, 0:n]
+        tt(t, pd, flag, A.mult, pn + " " + fn, "f4")
+        tt(t, t, dum, A.add, "f4 " + dn, "f4")
+        cp(out, t, "f4", on)
+
+    def xn(b):
+        return " ".join("x%d_%d" % (b, q) for q in range(4))
+
+    def send_values(b):
+        act(T.snd[:], xw[b][:, 0:2064].indirect(T.off[:, 512:560]), F.Copy, "offL vac " + xn(b), "snd")
+        exchange(T.snd, xw[b], 2064, 256, 1, "snd", "xl%d" % b)
+
+    def own(hq):
+        return T.VA[:, 5120 + 3072 * hq:6144 + 3072 * hq]
+
+    def own_values(b, vec):
+        for hq in range(2):
+            src = xw[b][:, 16 + 1024 * hq:1040 + 1024 * hq]
+            if vec:
+                cp(own(hq), src, xn(b), "W%d1" % (2 + 2 * hq))
+            else:
+                act(own(hq), src, F.Copy, xn(b), "W%d1" % (2 + 2 * hq))
+
+    put, fin = invert(T.axoi, "axoi", 8384, "Bg0", T.dT, "dT", T.oL[:], "oL", "PS")
+    put()
+    ms(T.xw0[:, 0:16], -16.0, "vac")
+    ms(T.xw1[:, 0:16], -16.0, "vac")
+    tt(pf[:, 12:13], pf[:, 2:3], pf[:, 4:5], A.add, "pfa", "pf12")
+    ts(pf[:, 13:14], pf[:, 3:4], 4.0, A.mult, "pfa", "pf13", pf[:, 2:3], A.add)
+    for j in range(4):
+        ts(pf[:, 14 + j:15 + j], pf[:, 3:4], float(j), A.is_equal, "pfa", "pm%d" % j)
+        ts(pf[:, 18 + j:19 + j], pf[:, 4:5], float(j), A.is_equal, "pfa", "pn%d" % j)
+    ts(pf[:, 12:13], pf[:, 12:13], 12.0, A.add, "pf12", "pf12")
+    ts(pf[:, 13:14], pf[:, 13:14], 3.0, A.add, "pf13", "pf13")
+    for j in range(4):
+        ts(T.Pf[:, 144 * j:144 * j + 144], T.yrow[:], pf[:, 12:13], A.is_equal, "yrow pf12 pm%d" % j, "Pf", pf[:, 14 + j:15 + j], A.mult)
+    cp(T.wa[:, 0:512], T.deni[:], "deni", "wa")
+    ts(T.tmpA[:, 0:512], T.axoi[:], 64.0, A.add, "axoi", "tmpA")
+    dma("bw2", [(T.BW[row, 0:8192], T.tmpA[:, 0:512])], "tmpA", "BW " + " ".join("Bi%d" % k for k in range(8)))
+
+    def to_planes(j):
+        mm(T.P2[:, 128 * j:128 * j + 128], [(T.Pf[:, 144 * j + 12 - 4 * b:144 * j + 140 - 4 * b], T.wa[:, b:512:4]) for b in range(4)], "Pf wa", "P2")
+    to_planes(0)
+
+    def first_values():
+        ts(T.off[:, 512:560], T.PS[:, 0:48], 0.25, A.mult, "PS", "offL", -0.375, A.add)
+        ts(T.AI[:, 512:560], T.PS[:, 0:48], -64.0, A.add, "PS", "AIL")
+        send_values(0)
+        own_values(0, False)
+    put, fin = invert(T.deni, "deni", 10432, "Bg1", T.dG, "dG", T.oA[:, 128:176], "oA2", "PY",
+                      [fin, lambda: to_planes(1)], [first_values], [lambda: to_planes(2)])
+    to_planes(3)
+    for Z, w, n in ((T.Zb, 1.0, "Zb"), (T.Zk, 65536.0, "Zk"), (T.Z1b, pf[:, 7:8], "Z1b")):
+        ts(Z[:], T.yrow[:], pf[:, 6:7], A.is_equal, "yrow pf6 pf7", n, w, A.mult)
+    ts(T.off[:, 0:512], T.P2[:], 0.25, A.mult, "P2", "off", 15.625, A.add)
+    cp(T.AI[:, 0:512], T.P2[:], "P2", "AI")
+    for I, w, n in ((T.Ib, 1.0, "Ib"), (T.I4, 4.0, "I4"), (T.In, -1.0, "In"), (T.If, 1.0, "If")):
+        ts(I[:], T.yrow[:, 0:128], pf[:, 0:1], A.is_equal, "yrow pfa", n, w, A.mult)
+    ms(T.cb[0:32, 0:640], 1.0, "cb0")
+    ms(T.cb[0:32, 640:768], 3072.0, "cb1")
+    for j in range(4):
+        ms(T.cb[0:32, 768 + 128 * j:896 + 128 * j], 16384.0 * (4 - j), "cb%d" % (2 + j))
+
+    def late_constants():
+        put()
+        cp(T.parf[0:8, 0:7], T.pari[0:8, 0:7], "pari", "parf")
+        ts(T.gsel[0:8, :], T.gsel[0:8, :], 0.0, A.is_equal, "gsel", "gsel")
+        mm(T.PY[:, 0:7], [(T.gsel[0:8, :], T.parf[0:8, 0:7])], "gsel parf", "PY")
+        ts(T.wa[:], T.AI[:], 64.0, A.add, "AI AIL", "wa")
+        dma("ua", [(T.UA[row, 0:8960], T.wa[:])], "wa", "UA")
+        cp(T.pc[:, 0:7], T.PY[:, 0:7], "PY", "pc")
+        for b in range(4):
+            ts(T.Qh[:, 144 * b:144 * b + 144], T.yrow[:], pf[:, 13:14], A.is_equal, "yrow pf13 pn%d" % b, "Qh", pf[:, 18 + b:19 + b], A.mult)
+        cp(T.BOf[:], T.BOh[:], "BOh", "BOf")
+        ts(T.CL[:], T.Dc[:], 1089.0 + 512.5, A.is_ge, "Dc", "CL", 64.0, A.mult)
+        ts(T.CL[:], T.CL[:], 1024.0, A.add, "CL", "CL")
+        ts(T.thg[:], T.gam[:], 1024.0, A.is_ge, "gam", "thg", 8300.0, A.mult)
+        ts(T.thg[:], T.thg[:], -92.0, A.add, "thg", "thg")
+        ts(pf[:, 22:23], pf[:, 1:2], 68.0, A.mult, "pfa", "pf22", 8960.0, A.add)
+        ts(pf[:, 11:12], pf[:, 1:2], 128.0, A.mult, "pfa", "pf11", 8384.0, A.add)
+        ts(pf[:, 23:24], pf[:, 5:6], 128.0, A.mult, "pfa pf11", "pf23", pf[:, 11:12], A.add)
+        for c0, n in ((0, 68), (68, 68), (136, 40)):
+            ts(T.dumA[:, c0:c0 + n], T.yrow[:, 0:n], pf[:, 22:23], A.add, "yrow pf22", "dumA")
+        ts(T.dumV[:], T.dumA[:, 0:68], -768.0, A.add, "dumA", "dumV")
+        ts(T.dumB[:], T.yrow[:, 0:128], pf[:, 23:24], A.add, "yrow pf23", "dumB")
+
+    lo, th, hi, K = (T.pc[:, k:k + 1] for k in range(4))
+    Pq = [T.P0, T.P1, T.P2, T.P3]
+
+    def read_plane(t):
+        dma("bt", [(T.BI[a:128:4, 0:128], T.BW[row, 512 * (4 * a + t):512 * (4 * a + t) + 512]) for a in range(4)], "BW", "Bt")
+
+    def j_list(t):
+        ts(T.pj[:, 0:1], pf[:, 1:2], K, A.mult, "pfa pc", "pj0", T.pc[:, 4 + t:5 + t], A.add)
+        ts(T.pj[:, 1:2], T.pj[:, 0:1], 15, AND, "pj0", "pj1")
+        ts(T.pj[:, 2:3], T.pj[:, 0:1], 4, SH, "pj0", "pj2")
+        ts(T.col[:, 8:9], T.pj[:, 1:2], 512.0, A.mult, "pj1", "c8")
+        cp(T.col[:, 9:10], T.pj[:, 2:3], "pj2", "c9")
+        ts(T.deni[:], T.jio[:], K, A.mult, "jio pc c9", "deni", T.col[:, 9:10], A.add)
+        ts(T.deni[:], T.deni[:], 511, AND, "deni", "deni")
+        ts(T.joff[:], T.deni[:], T.col[:, 8:9], A.add, "deni c8", "joff")
+
+    def floor16(q):
+        act(T.M[:, 512 * (q % 2):512 * (q % 2) + 512], Pq[q][:], F.Identity, "P%d" % q, "M rr%d" % (q % 2), bias=-7.5)
+
+    def mod16(b, q):
+        tt(xw[b][:, 16 + 512 * q:528 + 512 * q], Pq[q][:], T.M[:, 512 * (q % 2):512 * (q % 2) + 512], A.subtract,
+           "P%d rr%d" % (q, q % 2), "x%d_%d" % (b, q))
+
+    def link_conv(bank):
+        conv(T[bank][:, 320:368], T.Z1f, lambda r: T.BW[:, 8192 + 2048 * (r % 4) + r // 4:8384 + 2048 * (r % 4):4], "Z1f BW", bank)
+
+    WALL = " ".join("W%d%d" % (j, h) for j in range(4) for h in range(2))
+    one = (T.cb[0:1, 640:768], T.cb[0:1, 0:512])
+
+    for t in range(RO):
+        last = t == RO - 1
+        C = T.pc[:, 4 + t:5 + t]
+        win = "vac xl0 off " + xn(0)
+        for hq in range(2 if t == 0 else 0):
+            c0 = 1024 * hq
+
+            def o(j):
+                return T.xw0[:].indirect(T.off[:, 128 * j + 64 * hq:128 * j + 64 * hq + 64])
+            tt(T.V[:, c0:c0 + 1024], o(0), own(hq), A.add, win + " W%d1" % (2 + 2 * hq), "V0%d" % hq)
+            act(T.V[:, 4096 + c0:5120 + c0], o(2), F.Copy, win, "V2%d" % hq)
+            tt(T.V[:, 2048 + c0:3072 + c0], o(1), T.V[:, c0:c0 + 1024], A.add, win + " V0%d" % hq, "V1%d" % hq)
+            act(T.V[:, 6144 + c0:7168 + c0], o(3), F.Copy, win, "V3%d" % hq)
+            for k, j in enumerate((2, 1, 3)):
+                for q in (2 * hq, 2 * hq + 1):
+                    mm(Pq[q][:], [one] * (k == 0) + [(T.Ib[:], T.V[:, 2048 * j + 512 * q:2048 * j + 512 * q + 512])],
+                       "cb0 cb1 Ib V%d%d" % (j, hq), "P%d" % q, k == 0, k == 2)
+        for q in range(4):
+            if t > 0:
+                mm(Pq[q][:], [(T.Ib[:], T.VA[:, 2048 * j + 512 * q:2048 * j + 512 * q + 512]) for j in range(4)], "Ib " + WALL, "P%d" % q, False, True)
+                if q == 3:
+                    ts(T.off[:], T.tmpA[:], 0.25, A.mult, "tmpA tmpL", "off offL", -0.375, A.add)
+            floor16(q)
+            mod16(1, q)
+        send_values(1)
+        if t > 0:
+            act(T.BW[:].indirect(T.oG[:]), T.dT[:], F.Silu, "oG dT", "BW")
+            read_plane(t)
+        own_values(1, t > 0)
+        if t == 0:
+            late_constants()
+            read_plane(0)
+        else:
+            ts(T.AI[:], T.tmpA[:], -64.0, A.add, "tmpA tmpL", "AI AIL", -1.0, A.max)
+        ts(T.i1[:, 0:48], T.AI[:, 512:560], 3, AND, "AIL", "i1")
+        ts(T.loe[:], T.i1[:, 0:48], float(t), A.is_equal, "i1 pc", "loe", lo, A.mult)
+        lor, lsr = T["lor%d" % t], T["lsr%d" % t]
+        exchange(T.loe, lor, 0, 16, 1, "loe", "lor")
+        cp(T.Af[:], T.AI[:, 0:512], "AI", "Af")
+        act(T.vacm[:], T.Af[:], F.Relu, "Af", "vacm", scale=-67108864.0)
+        pos_b(T.AI[:, 512:560], "AIL", 48, T.dumB[:, 0:48], "dumB", T.pdL[:], "pdL")
+        j_list(t)
+        win = "vac xl1 off " + xn(1)
+
+        def keys(j, hq):
+            k = slice(128 * j + 64 * hq, 128 * j + 64 * hq + 64)
+            c0 = 2048 * j + 1024 * hq
+            conv(T.PK[:, k], T.Zk, lambda r: T.VA[:, c0 + r:c0 + 1024:16], "Zk If In Af vacm cb0 cb%d W%d%d" % (2 + j, j, hq), "PK",
+                 [(T.If[:], T.Af[:, k]), (T.In[:], T.vacm[:, k]), (T.cb[0:1, 0:128], T.cb[0:1, 768 + 128 * j:832 + 128 * j])])
+        for q in range(4):
+            mm(Pq[q][:], [one, (T.I4[:], T.xw1[:, 16 + 512 * q:528 + 512 * q])], "cb0 cb1 I4 x1_%d" % q, "P%d" % q, True, False)
+        if t == 0:
+            fin()
+        else:
+            link_conv("PY")
+
+        def fourth(hq):
+            act(T.V[:, 6144 + 1024 * hq:7168 + 1024 * hq], T.xw1[:].indirect(T.off[:, 384 + 64 * hq:448 + 64 * hq]), F.Copy, win, "V3%d" % hq)
+            for q in (2 * hq, 2 * hq + 1):
+                c = slice(6144 + 512 * q, 6656 + 512 * q)
+                bank = ("PS", "PX")[q % 2]
+                mm(T[bank][:], [(T.Ib[:], T.V[:, c]), (T.In[:], T.xw1[:, 16 + 512 * q:528 + 512 * q])], "Ib In V3%d x1_%d" % (hq, q), bank)
+                mm(Pq[q][:], [(T.Ib[:], T.V[:, c])], "Ib V3%d" % hq, "P%d" % q, False, False)
+
+        def fourth_keys(hq):
+            for q in (2 * hq, 2 * hq + 1):
+                bank = ("PS", "PX")[q % 2]
+                act(T.VA[:, 6144 + 512 * q:6656 + 512 * q], T[bank][:], F.Abs, bank, "W3%d" % hq)
+            keys(3, hq)
+        fourth(0)
+        for hq, j in ((0, 0), (0, 1), (0, 2), (1, 0), (1, 1), (1, 2)):
+            c0 = 1024 * hq
+            c = slice(2048 * j + c0, 2048 * j + c0 + 1024)
+            n = "%d%d" % (j, hq)
+            tt(T.V[:, c], T.xw1[:].indirect(T.off[:, 128 * j + 64 * hq:128 * j + 64 * hq + 64]), own(hq),
+               A.subtract, win + " W%d1" % (2 + 2 * hq), "V" + n)
+            for q in (2 * hq, 2 * hq + 1):
+                mm(Pq[q][:], [(T.Ib[:], T.V[:, 2048 * j + 512 * q:2048 * j + 512 * q + 512])], "Ib V" + n, "P%d" % q, False, j == 2)
+            if (hq, j) == (1, 2):
+                break
+            act(T.VA[:, c], T.V[:, c], F.Abs, "V" + n, "W" + n)
+            keys(j, hq)
+            if (hq, j) == (0, 0):
+                fourth_keys(0)
+            if (hq, j) == (0, 2):
+                fourth(1)
+            if (hq, j) == (1, 0):
+                fourth_keys(1)
+            if (hq, j) == (1, 1):
+                floor16(0)
+                floor16(1)
+        if t == 0:
+            cp(T.BI[:, 128:176], T.PY[:, 0:48], "PY", "IE")
+        else:
+            tt(T.f5[:, 0:48], T.PY[:, 320:368], T.held[:], A.mult, "PY held", "f5")
+            tt(T.BI[:, 128:176], T.f5[:, 0:48], T.IEp[:], A.add, "f5 IEp", "IE")
+        ts(T.i1[:], T.BI[:], -64.0, A.add, "Bt IE", "i1")
+        pos_a(T.i1[:], "i1", 176, T.pdA[:], "pdA")
+        ts(T.f5[:], T.BI[:], 63.5, A.is_ge, "Bt IE", "f5")
+        tt(T.pdA[:], T.pdA[:], T.f5[:], A.mult, "pdA f5", "pdA")
+        cp(T.held[:], T.f5[:, 128:176], "f5", "held")
+        for q in range(4):
+            if q >= 2:
+                floor16(q)
+            mod16(0, q)
+            mm(T.PS[:, 128:256], [(T.Zb[:, 15 - r:143 - r], T.xw0[:, 16 + 512 * q + r % 4:528 + 512 * q:4]) for r in range(4 * q, 4 * q + 4)],
+               "Zb x0_%d" % q, "PS", q == 0, q == 3)
+        act(T.VA[:, 5120:6144], T.V[:, 5120:6144], F.Abs, "V21", "W21")
+        act(T.kh[:], T.PK[:, 0:256], F.Copy, "PK", "kh")
+        keys(2, 1)
+        conv(T.PY[:, 256:384], T.Zb, lambda r: T.xw0[:, 16 + r:2064:16], "Zb " + xn(0), "PY")
+        send_values(0)
+        ts(T.f5[:, 0:128], T.PS[:, 128:256], lo, A.is_ge, "PS pc", "f5")
+        ts(T.f3[:, 0:128], T.PS[:, 128:256], lo, A.is_lt, "PS pc", "f3")
+        tt(T.Bn[:], T.BI[:, 0:128], T.f5[:, 0:128], A.mult, "Bt f5", "Bn")
+        dma("bn", [(T.BW[row, 512 * (4 * a + t):512 * (4 * a + t) + 512], T.Bn[a:128:4, :]) for a in range(4)], "Bn", "BW")
+        if last:
+            dma("yx", [(T.yx[:], T.xw0[:, 16:2064])], xn(0), "")
+        pick(T.oA[:, 0:128], "oA", T.pdA[:, 0:128], "pdA", T.f3[:, 0:128], "f3", T.dumA[:, 0:128], "dumA", 128)
+        for k in range(2):
+            act(T.UA[:].indirect(T.oA[:, 64 * k:64 * k + 64]), T.zer[:, 0:1024], F.Silu, "oA zer", "UA")
+        tt(T.km[:], T.PK[:, 256:512], T.kh[:], A.max, "PK kh", "km")
+        ts(T.f5[:, 0:128], T.PY[:, 256:384], hi, A.is_ge, "PY pc", "f5")
+        tt(T.mx[:], T.km[:, 0:128], T.km[:, 128:256], A.max, "km", "mx")
+        cp(T.i1[:, 0:128], T.mx[:], "mx", "i1")
+        ts(T.mx[:], T.mx[:], 0.0, A.max, "mx", "mx")
+        pos_b(T.i1[:, 0:128], "i1", 128, T.dumB[:], "dumB", T.pdK[:], "pdK")
+        tt(T.mg[:], T.mx[:], T.f5[:, 0:128], A.mult, "mx f5", "mg")
+        ts(T.f5[:, 0:128], T.mg[:], 0.0, A.is_gt, "mg", "f5")
+        pick(T.oK[:], "oK", T.pdK[:], "pdK", T.f5[:, 0:128], "f5", T.dumB[:], "dumB", 128)
+        conv(T.PS[:, 256:304], T.Zb, lambda r: T.xw0[:, 2064 + r:XW:16], "Zb xl0", "PS")
+        cp(T.BW[:].indirect(T.oK[:, 0:64]), T.zer[:, 0:1024], "oK zer", "BW Bg0 Bg1 BL")
+        tt(T.alive[:], T.PS[:, 256:304], lor[:], A.is_ge, "PS lor", "alive")
+        ts(T.f5[:, 0:48], T.alive[:], 0.0, A.is_equal, "alive", "f5")
+        pick(T.oA[:, 128:176], "oA2", T.pdA[:, 128:176], "pdA", T.f5[:, 0:48], "f5", T.dumA[:, 128:176], "dumA", 48)
+        act(T.UA[:].indirect(T.oA[:, 128:176]), T.zer[:, 0:768], F.Silu, "oA2 zer", "UA")
+        dma("uar", [(T.tmpA[:], T.UA[row, 0:8960])], "UA", "tmpA tmpL")
+        cp(T.BW[:].indirect(T.oK[:, 64:128]), T.zer[:, 0:1024], "oK zer", "BW")
+        link_conv("PS")
+        ts(T.thr[:], T.PY[:, 256:384], th, A.is_lt, "PY pc", "thr", 63.5, A.mult)
+        for j in range(4):
+            tt(T.wb[:, 128 * j:128 * j + 128], T.PK[:, 128 * j:128 * j + 128], T.mg[:], A.not_equal, "PK mg", "wb")
+        tt(T.flG[:, 0:48], T.alive[:], T.held[:], A.is_gt, "alive held", "flG0")
+        op("v", lambda: v.tensor_reduce(T.col[:, 0:1], T.flG[:, 0:48], AxisListType.X, A.add), "flG0", "c0")
+        mm(T.PY[:, 0:1], [(T.BOf[:], T.col[:, 0:1])], "BOf c0", "PY")
+        ts(T.f5[:, 0:48], T.PS[:, 320:368], 63.5, A.is_lt, "PS", "f5")
+        tt(T.msg[:], T.f5[:, 0:48], T.held[:], A.mult, "f5 held", "msg")
+        exchange(T.msg, lsr, 0, 16, -1, "msg", "lsr")
+        if not last:
+            tt(T.f5[:, 0:48], T.alive[:], T.msg[:], A.is_gt, "alive msg", "f5")
+            tt(T.f5[:, 0:48], T.f5[:, 0:48], T.held[:], A.mult, "held f5", "f5")
+            tt(T.IEp[:], T.BI[:, 128:176], T.f5[:, 0:48], A.mult, "IE f5", "IEp")
+        cp(T.col[:, 1:2], T.PY[:, 0:1], "PY", "c1")
+        tt(T.tmpA[:, 0:512], T.tmpA[:, 0:512], T.wb[:, 0:512], A.mult, "tmpA wb", "tmpA")
+        for j in range(4):
+            tt(T.flE[:, 128 * j:128 * j + 128], T.tmpA[:, 128 * j:128 * j + 128], T.thr[:], A.is_lt, "tmpA thr", "Eh flP%d" % j)
+        for b in range(4):
+            mm(T.P2[:, b:512:4], [(T.Qh[:, 144 * b + 3 - j:144 * b + 131 - j], T.flE[:, 128 * j:128 * j + 128]) for j in range(4)],
+               "Qh Eh flP0 flP1 flP2 flP3", "P2")
+        pick(T.oL[:], "oL", T.pdL[:], "pdL", lsr[:], "lsr", T.dumB[:, 0:48], "dumB", 48)
+        act(T.BW[:].indirect(T.oL[:]), T.zer[:, 0:768], F.Silu, "oL zer", "BW")
+
+        def jchunk(k, eng):
+            c = slice(1024 * k, 1024 * k + 1024)
+            n = "V%d%d" % (k // 2, k % 2)
+            src = T.BW[:, 0:8192].indirect(T.joff[:, 64 * k:64 * k + 64])
+            if eng == "s":
+                act(T.V[:, c], src, F.Sign, "BW joff", n, scale=-1.0, bias=63.5)
+            else:
+                ts(T.V[:, c], src, 63.5, A.is_lt, "BW joff", n)
+            return lambda: conv(T.P3[:, 64 * k:64 * k + 64], T.Z1b, lambda r: T.V[:, 1024 * k + r:1024 * k + 1024:16], "Z1b " + n, "P3")
+        jc = [jchunk(k, "s") for k in range(NS)]
+        if last:
+            dma("bw", [(T.wb[:, 0:512], T.BW[row, 0:8192])], "BW", "wb")
+        ts(T.f5[:, 0:48], lsr[:], -1.0, A.mult, "lsr", "f5", 1.0, A.add)
+        tt(T.tmpA[:, 512:560], T.tmpA[:, 512:560], T.f5[:, 0:48], A.mult, "tmpL f5", "tmpL")
+        ts(T.flT[:, 513:529], T.tmpA[:, 512 + 16 * t:528 + 16 * t], 63.5, A.is_lt, "tmpL", "flT1")
+        if not last:
+            dma("ua", [(T.UA[row, 0:8960], T.tmpA[:])], "tmpA tmpL", "UA")
+        cp(T.flT[:, 0:512], T.P2[:], "P2", "flT0")
+        scan(T.flT, "flT0", 0, 512, 0.0)
+        mm(T.PY[:, 0:1], [(T.BOh[:], T.cum[:, 512:513])], "BOh cum", "PY")
+        if last:
+            ts(T.AI[:, 0:512], T.tmpA[:, 0:512], -64.0, A.add, "tmpA", "AI", -1.0, A.max)
+            cp(T.Pf[:], T.Qh[:], "Qh", "Pf")
+            cp(T.Af[:], T.AI[:, 0:512], "AI", "Af")
+        else:
+            ts(T.off[:, 0:512], T.tmpA[:, 0:512], 0.25, A.mult, "tmpA", "off", -0.375, A.add)
+        ts(T.col[:, 2:3], T.PY[:, 0:1], 1024.0, A.min, "PY c1", "c2", T.col[:, 1:2], A.max)
+        ts(T.col[:, 3:4], T.PY[:, 0:1], 1024.0, A.min, "PY", "c3")
+        ts(T.col[:, 4:5], T.col[:, 2:3], pf[:, 7:8], A.mult, "c2 pf7", "c4")
+        ts(T.col[:, 5:6], T.col[:, 2:3], 64.0, A.add, "c2", "c5")
+        cp(T.cum[:, 513:514], T.col[:, 4:5], "c4", "cum")
+        scan(T.flT, "flT1", 513, 560, T.col[:, 4:5], "c4")
+        nat = [lambda b=b: mm(T.P2[:, b:512:4], [(T.Pf[:, 144 * b + 3 - j:144 * b + 131 - j], T.Af[:, 128 * j:128 * j + 128]) for j in range(4)],
+                              "Pf Af", "P2") for b in range(4) if last]
+        compact(T.flT, "flT0 flT1", 68, True, nat[0:3], jc[0:1], jc[1:2] + nat[3:])
+        run(jc[2:NS - 1])
+        cp(T.nn[:, 68:136], T.PY[:, 128:196], "PY", "nn1")
+        tt(T.nn[:, 0:68], T.PX[:, 192:260], T.cf[:], A.add, "PX cf", "nn0")
+        ts(T.vT[:], T.PX[:, 192:260], 16.0, A.is_ge, "PX", "vT")
+        ts(T.f1[:, 0:136], T.nn[:], 3.0, A.mult, "nn0 nn1", "f1", float(8192 + 1024 * t - 64 * 513), A.add)
+        ts(T.f2[:, 0:136], T.nn[:], 8208.0, A.is_ge, "nn0 nn1", "f2")
+        tt(T.f3[:, 0:68], T.nn[:, 0:68], T.thg[:], A.is_ge, "nn0 thg", "f3")
+        tt(T.f1[:, 0:136], T.f1[:, 0:136], T.f2[:, 0:136], A.mult, "f1 f2", "f1")
+        ts(T.f4[:, 0:68], T.gam[:], T.col[:, 5:6], A.is_lt, "gam c5", "f4")
+        tt(T.vT[:], T.vT[:], T.f3[:, 0:68], A.mult, "vT f3", "vT")
+        tt(T.valT[:], T.f1[:, 0:136], T.nn[:], A.add, "f1 nn0 nn1", "valT")
+        tt(T.vT[:], T.vT[:], T.f4[:, 0:68], A.mult, "vT f4", "vT")
+        if not last:
+            ts(T.valT[:, 68:136], T.valT[:, 68:136], 64.0, A.add, "valT", "valT")
+        dma("dT", [(T.dT[row, :], T.valT[:, 68:136])], "valT", "dT")
+        cp(T.i1[:, 0:68], T.valT[:, 0:68], "valT", "i1")
+        if last:
+            pos_b(T.i1[:, 0:68], "i1", 68, T.dumA[:, 0:68], "dumA", T.pdT[:], "pdT")
+            ts(T.f3[:, 0:68], T.valT[:, 0:68], 8192.0, A.is_lt, "valT", "f3")
+            tt(T.pdT[:], T.pdT[:], T.f3[:, 0:68], A.mult, "pdT f3", "pdT")
+        else:
+            pos_a(T.i1[:, 0:68], "i1", 68, T.pdT[:], "pdT")
+            ts(T.i2[:, 0:68], T.i1[:, 0:68], 2, SH, "i1", "i2")
+            ts(T.f1[:, 0:68], T.i3[:, 0:68], 2048.0, A.mult, "i3", "f1")
+            tt(T.f2[:, 0:68], T.i2[:, 0:68], T.dumV[:], A.subtract, "i2 dumV", "f2")
+            ts(T.f3[:, 0:68], T.valT[:, 0:68], 8192.0, A.is_lt, "valT", "f3")
+            tt(T.f1[:, 0:68], T.f1[:, 0:68], T.f2[:, 0:68], A.add, "f1 f2", "f1")
+            tt(T.pdV[:], T.f1[:, 0:68], T.f3[:, 0:68], A.mult, "f1 f3", "pdV")
+        jc += [jchunk(k, "v") for k in range(NS, 8)]
+        run(jc[NS - 1:])
+        clear_l1()
+        if not last:
+            for k in range(8):
+                act(T.VA[:, 1024 * k:1024 * k + 1024], T.xw0[:].indirect(T.off[:, 64 * k:64 * k + 64]), F.Copy,
+                    "vac xl0 off " + xn(0), "W%d%d" % (k // 2, k % 2))
+        ts(T.flG[:, 48:560], T.P3[:], 0.0, A.max, "P3", "flG1")
+        scan(T.flG, "flG0 flG1", 0, 560, 0.0)
+
+        def to_natural():
+            act(T.wa[:, 0:512], T.P2[:], F.Copy, "P2", "wa")
+            dma("ua", [(T.UA[row, 0:8192], T.wa[:, 0:512])], "wa", "UA")
+
+        def plain_entries():
+            ts(T.deni[:], T.wb[:, 0:512], -64.0, A.add, "wb", "deni", -1.0, A.max)
+            cp(T.wb[:, 0:512], T.deni[:], "deni", "wb")
+            dma("bw2", [(T.BW[row, 0:8192], T.wb[:, 0:512])], "wb", "BW")
+        compact(T.flG, "flG0 flG1", 68, False, [to_natural] if last else (), (), [plain_entries] if last else ())
+        if not last:
+            for q in range(4):
+                mm(Pq[q][:], [one, (T.Ib[:], T.xw0[:, 16 + 512 * q:528 + 512 * q])], "cb0 cb1 Ib x0_%d" % q, "P%d" % q, True, False)
+            ts(T.f5[:, 0:48], T.tab[:, 0:48], T.col[:, 3:4], A.is_le, "tab0 c3", "f5")
+            tt(T.held[:], T.f5[:, 0:48], T.flG[:, 0:48], A.mult, "f5 flG0", "held")
+        cp(T.nn[:, 68:136], T.PY[:, 128:196], "PY", "nn1")
+        tt(T.nn[:, 0:68], T.PX[:, 192:260], T.cf[:], A.add, "PX cf", "nn0")
+        ts(T.f1[:, 0:136], T.nn[:], -768.0, A.add, "nn0 nn1 pc", "f1", K, A.mult)
+        ts(T.f2[:, 0:136], T.nn[:], 768.0, A.is_lt, "nn0 nn1", "f2")
+        ts(T.i1[:, 0:136], T.f1[:, 0:136], C, A.add, "f1 pc", "i1")
+        ts(T.f3[:, 0:136], T.nn[:], 4.0, A.mult, "nn0 nn1", "f3", 8192.0, A.add)
+        ts(T.i1[:, 0:136], T.i1[:, 0:136], 8191, AND, "i1", "i1")
+        ts(T.vG[:], T.PX[:, 192:260], 16.0, A.is_ge, "PX", "vG")
+        tt(T.f3[:, 0:136], T.f3[:, 0:136], T.i1[:, 0:136], A.subtract, "f3 i1", "f3")
+        tt(T.f3[:, 0:136], T.f3[:, 0:136], T.f2[:, 0:136], A.mult, "f3 f2", "f3")
+        tt(T.valG[:], T.f3[:, 0:136], T.i1[:, 0:136], A.add, "f3 i1", "valG")
+        if not last:
+            ts(T.valG[:, 68:136], T.valG[:, 68:136], 64.0, A.add, "valG", "valG")
+        dma("dG", [(T.dG[row, :], T.valG[:, 68:136])], "valG", "dG")
+        tt(T.vG[:], T.vG[:], T.vT[:], A.mult, "vG vT", "vG")
+        cp(T.i1[:, 0:68], T.valG[:, 0:68], "valG", "i1")
+        pick(T.oT[:], "oT", T.pdT[:], "pdT", T.vG[:], "vG", T.dumA[:, 0:68], "dumA", 68)
+        if not last:
+            act(T.UA[:].indirect(T.oT[:]), T.dG[:], F.Silu, "oT dG", "UA")
+            dma("uar", [(T.tmpA[:], T.UA[row, 0:8960])], "UA", "tmpA tmpL")
+            ts(T.oS[:], T.valG[:, 0:68], 0.25, A.mult, "valG", "oS", 15.625, A.add)
+            pick(T.oV[:], "oV", T.pdV[:], "pdV", T.vG[:], "vG", T.dumV[:], "dumV", 68)
+            cp(T.M[:], T.xw0[:].indirect(T.oS[:]), "oS vac xl0 " + xn(0), "M rr0 rr1")
+            cp(T.VA[:].indirect(T.oV[:]), T.M[:], "oV M rr0 rr1", WALL + " W41")
+            clear_l1()
+        pos_b(T.i1[:, 0:68], "i1", 68, T.dumB[:, 0:68], "dumB", T.pdT[:], "pdT")
+        pick(T.oG[:], "oG", T.pdT[:], "pdT", T.vG[:], "vG", T.dumB[:, 0:68], "dumB", 68)
+        if last:
+            cp(T.BW[:].indirect(T.oG[:]), T.dT[:], "oG dT", "BW")
+            dma("ya", [(T.ya[:], T.BW[row, 0:8192])], "BW", "")
+            cp(T.UA[:].indirect(T.oT[:]), T.dG[:], "oT dG", "UA")
+            dma("yd", [(T.yd[:], T.UA[row, 0:8192])], "UA", "", q="s")
+    wait("g", list(cnt.items()))

@@ -1,10 +1,14 @@
+import numpy as np
 from concourse.bass import DstId, RemoteDMATransfer
-from concourse.mybir import AluOpType as A, AxisListType, ActivationFunctionType as F
+from concourse.mybir import AluOpType as A, ActivationFunctionType as F
 
 N, RO = 4, 3
-XW = 16 + 2048 + 768
-UAW, BWW, L1W = 10048, 14528, 2752
-NS = 7
+W0, W1 = 4912, 2832
+PL = 2064
+UAW, AXW, L1W = 11264, 11328, 1680
+MODE = {(0, 0): "vr", (1, 0): "va", (2, 0): "va", (3, 0): "s", (0, 1): "va", (1, 1): "va", (2, 1): "va", (3, 1): "s"}
+PASSES = 3000
+HEAT = 0.3
 f32, bf, f16, i32, u16 = "float32", "bfloat16", "float16", "int32", "uint16"
 
 
@@ -13,35 +17,103 @@ def sb(n, t):
 
 
 SCRATCH = {
-    "xw0": sb(XW, bf), "xw1": sb(XW, bf), "V": sb(8192, bf), "VA": sb(9280, bf), "snd": sb(768, bf),
-    "UA": sb(UAW, f32), "BW": sb(BWW, f32), "L1": sb(L1W, f32), "zer": sb(1088, f32),
-    "dT": sb(1088, f32), "dG": sb(1088, f32), "cw": sb(1088, f16), "M": sb(1088, bf),
-    "io1": sb(1088, f32), "cdat": sb(560, f32),
-    "deni": sb(512, i32), "axoi": sb(512, i32), "pari": sb(8, i32), "parf": sb(8, f32), "pc": sb(8, f32),
-    "wa": sb(560, f32), "wb": sb(560, f32), "tmpA": sb(560, f32), "AI": sb(560, i32), "Af": sb(512, f32),
-    "vacm": sb(512, bf), "off": sb(560, u16), "joff": sb(512, u16), "jio": sb(512, f32), "pj": sb(4, i32), "tab": sb(560, f32),
-    "flT": sb(560, f16), "flG": sb(560, f16), "flE": sb(768, f16), "cum": sb(576, f16), "kh": sb(256, f32), "km": sb(256, f32),
-    "BI": sb(176, f32), "Bn": sb(128, f32), "pdA": sb(176, f32), "pdL": sb(48, f32), "held": sb(48, f32), "alive": sb(48, f32),
-    "i1": sb(176, i32), "i2": sb(176, i32), "i3": sb(176, i32), "i4": sb(176, i32),
-    "f1": sb(176, f32), "f2": sb(176, f32), "f3": sb(176, f32), "f4": sb(176, f32), "f5": sb(176, f32),
-    "mx": sb(128, f32), "mg": sb(128, f32), "thr": sb(128, f32), "pdK": sb(128, f32),
-    "oK": sb(128, u16), "oA": sb(176, u16), "oL": sb(48, u16), "o1": sb(36, u16), "o2": sb(68, u16), "oT": sb(68, u16), "oG": sb(68, u16),
-    "oS": sb(68, u16), "oV": sb(68, u16), "pdV": sb(68, f32), "dumV": sb(68, f32),
-    "se": sb(36, f32), "cf": sb(68, f32), "nn": sb(136, f32), "vT": sb(68, f32), "vG": sb(68, f32), "valT": sb(136, f32), "valG": sb(136, f32),
-    "pdT": sb(68, f32), "col": sb(16, f32), "loe": sb(48, f32), "msg": sb(48, f32), "IEp": sb(48, f32),
-    "lor0": sb(48, f32), "lor1": sb(48, f32), "lor2": sb(48, f32), "lsr0": sb(48, f32), "lsr1": sb(48, f32), "lsr2": sb(48, f32),
-    "pi": sb(8, i32), "pf": sb(24, f32), "yrow": sb(144, f32), "gsel": sb(128, f32),
-    "Zb": sb(144, bf), "Zk": sb(144, bf), "Zr": sb(144, bf), "Zq": sb(144, bf), "Z1b": sb(144, bf),
-    "Zh": sb(144, f16), "Z1h": sb(144, f16), "Z16": sb(144, f16), "Z1f": sb(144, f32),
-    "Ib": sb(128, bf), "I4": sb(128, bf), "In": sb(128, bf), "If": sb(128, f32),
-    "BOh": sb(128, f16), "BOf": sb(128, f32), "TRI": sb(128, f16),
-    "Pf": sb(576, f32), "Qh": sb(576, f16), "cb": sb(1280, bf),
-    "Dc": sb(36, f32), "CL": sb(36, f32), "gam": sb(68, f32), "thg": sb(68, f32), "dumA": sb(176, f32), "dumB": sb(128, f32),
+    "xw0": sb(W0, bf), "xw1": sb(W1, bf), "V": sb(8192, bf), "VA": sb(8192, bf), "snd": sb(1536, bf),
+    "UA": sb(UAW, f32), "AX": sb(AXW, f32), "La": sb(L1W, f32), "Lb": sb(L1W, f32), "zer": sb(1024, f32),
+    "dT": sb(1088, f32), "dG": sb(1088, f32), "cwa": sb(1088, f16), "cwb": sb(1088, f16), "DEC": sb(1088, bf),
+    "wa": sb(592, f32), "wb": sb(592, f32), "D": sb(704, f32), "AI": sb(704, i32), "isT": sb(704, bf), "vacm": sb(704, bf),
+    "off": sb(704, u16), "ofp": sb(512, u16), "M": sb(1024, bf), "msR": sb(768, bf), "TG": sb(1024, bf),
+    "Fb": sb(512, f32), "Eb": sb(512, f32), "RV": sb(2048, bf),
+    "axoi": sb(512, i32), "pari": sb(8, i32), "parf": sb(8, f32), "pc": sb(16, f32),
+    "flT": sb(592, f16), "flG": sb(560, f16), "flE": sb(576, f16), "cumT": sb(608, f16), "cumG": sb(576, f16),
+    "km": sb(256, f32), "held": sb(48, f32), "alive": sb(48, f32),
+    "i1": sb(136, i32), "i2": sb(136, i32), "j1": sb(136, i32), "j2": sb(136, i32),
+    "f1": sb(256, f32), "f2": sb(136, f32), "f3": sb(136, f32), "f4": sb(136, f32), "f5": sb(136, f32), "g1": sb(136, f32), "g2": sb(136, f32),
+    "mg": sb(128, f32), "thr": sb(128, f32), "hiF": sb(128, f32), "lostB": sb(128, bf), "keepB": sb(128, f32),
+    "oK": sb(128, u16), "oL": sb(48, u16), "oN": sb(48, u16), "oa": sb(40, u16), "ob": sb(40, u16), "oT": sb(68, u16), "oG": sb(68, u16),
+    "oS": sb(64, u16), "oE": sb(128, u16), "oJ": sb(64, u16), "lpre": sb(64, u16), "lpost": sb(32, u16),
+    "sea": sb(80, f32), "seb": sb(80, f32), "posT": sb(68, f32), "valT": sb(68, f32), "valG": sb(68, f32),
+    "inv": sb(136, f32), "dA": sb(68, f32), "dX": sb(68, f32), "isL": sb(136, f32), "pre": sb(64, f32),
+    "col": sb(24, f32), "pi": sb(8, i32), "pf": sb(28, f32), "yrow": sb(144, f32),
+    "Zb": sb(144, bf), "Zk": sb(144, bf), "Zr": sb(144, bf), "Zn": sb(144, bf), "Zq": sb(144, bf),
+    "Zh": sb(144, f16), "Zc": sb(144, f16), "Zt": sb(144, f16),
+    "Ib": sb(128, bf), "I4": sb(128, bf), "In": sb(128, bf), "Ig": sb(128, bf), "If": sb(128, f32),
+    "BOh": sb(128, f16), "TRI": sb(128, f16), "TRp": sb(128, f16), "TRs": sb(128, f16), "TRe": sb(128, f16), "Ie": sb(128, f16),
+    "Wv": sb(256, f16), "Pf": sb(576, f32), "Qh": sb(576, f16), "cb": sb(976, bf), "ch": sb(832, f16), "Ut": sb(16, bf),
+    "Dc": sb(40, f32), "CL": sb(80, f32), "gam": sb(136, f32), "dumA": sb(144, f32), "dumK": sb(144, f32),
 }
 for _k in ("P0", "P1", "P2", "P3", "PK", "PS", "PX", "PY"):
     SCRATCH[_k] = ("psum", [128, 512], f32)
-DMAS = ["ld_x", "ld_d", "ld_a", "ld_p", "bw", "bw2", "ua", "uar", "bt", "bn", "dT", "dG", "yx", "yd", "ya"]
-SEMAPHORES = ["qv", "qs", "qt", "qg"] + ["d_" + n for n in DMAS] + ["ar%d" % k for k in range(13)] + ["lo%d" % k for k in range(13)]
+SEMAPHORES = ["qv", "qs", "qt", "qg"] + ["d%d" % k for k in range(40)] + ["ar%d" % k for k in range(10)] + ["lo%d" % k for k in range(10)]
+CY, GA, SC, PE, WAKE, NEAR = 0.9e-3, 1.56, 3.8, 0.5e-3, 0.12, 0.05
+PLAN = {}
+
+
+def schedule(ops):
+    n = len(ops)
+    pred, succ = [o[0] for o in ops], [[] for _ in ops]
+    for i in range(n):
+        for p in pred[i]:
+            succ[p].append(i)
+    level = [0.0] * n
+    for i in range(n - 1, -1, -1):
+        level[i] = min(b + l for b, l in ops[i][1].values()) + max([level[s] + WAKE for s in succ[i]], default=0.0)
+
+    def one(prio, pen, pre, suc, fixed):
+        left = [len(p) for p in pre]
+        fin, where, gaps = [0.0] * n, [""] * n, {q: [[0.0, 1e9]] for q in "vstgy"}
+        ready = sorted((prio[i], i) for i in range(n) if not left[i])
+        while ready:
+            i = ready.pop()[1]
+            top = None
+            for q, (b, l) in ops[i][1].items():
+                if fixed and q != fixed[i]:
+                    continue
+                est, near = 0.0, 0.0 if q == "t" else NEAR
+                for p in pre[i]:
+                    e = fin[p] + (near if where[p] == q else WAKE)
+                    if e > est:
+                        est = e
+                if fixed:
+                    est += l
+                gq = gaps[q]
+                k = len(gq) - 1
+                while k > 0 and gq[k - 1][1] >= est + b:
+                    k -= 1
+                while gq[k][1] < max(gq[k][0], est) + b:
+                    k += 1
+                st = max(gq[k][0], est)
+                key = st + b * (1 + pen[i] * (q == "v"))
+                if top is None or key < top[0]:
+                    top = (key, q, k, st, b, 0.0 if fixed else l)
+            key, q, k, st, b, l = top
+            a, z = gaps[q][k]
+            gaps[q][k:k + 1] = [x for x in ([a, st], [st + b, z]) if x[1] - x[0] > 0.03]
+            fin[i], where[i] = st + b + l, q
+            new = False
+            for s in suc[i]:
+                left[s] -= 1
+                if not left[s]:
+                    ready.append((prio[s], s))
+                    new = True
+            if new:
+                ready.sort()
+        return max(fin), fin, where
+    rng = np.random.default_rng(1)
+    prio, pen = level, [0.5] * n
+    best = now = one(prio, pen, pred, succ, None)
+    for k in range(PASSES):
+        base = one(now[1], pen, succ, pred, now[2])[1] if k % 4 == 0 else prio
+        t0 = rng.random() * now[0]
+        near = (np.abs(np.array(now[1]) - t0) < 8.0) * (rng.random(n) < 0.3)
+        p2 = (np.array(base) + near * rng.normal(0.0, (0.4, 1.2)[k % 2], n)).tolist()
+        e2 = np.where(near * (rng.random(n) < 0.4), rng.random(n) * 3.0 - 0.5, pen).tolist()
+        got = one(p2, e2, pred, succ, None)
+        if got[0] <= now[0] + HEAT * (1.0 - k / PASSES):
+            now, prio, pen = got, p2, e2
+            if got[0] < best[0]:
+                best = got
+    best = (best[0], [(best[1][i] - sum(ops[i][1][best[2][i]]), i, best[2][i]) for i in range(n)])
+    return [(i, q) for st, i, q in sorted(best[1])]
 
 
 def rank_program(g, core, T, topo):
@@ -49,64 +121,123 @@ def rank_program(g, core, T, topo):
     if rank is None:
         return
     Q = {"v": g.vector, "s": g.scalar, "t": g.tensor, "g": g, "y": g.sync}
-    cnt = {}
-    seen = {q: {} for q in Q}
+    ops, calls = [], []
     wr, rd = {}, {}
 
-    def wait(q, toks):
-        need = {}
-        for s, n in toks:
-            need[s] = max(need.get(s, 0), cnt[s] if s[:2] == "d_" else n)
-        for s, n in need.items():
-            if seen[q].get(s, 0) < n:
-                Q[q].wait_ge(T.sem[s], n)
-                seen[q][s] = n
-
-    def deps(q, R, W):
-        toks = []
-        for r in R:
-            if r in wr:
-                toks.append(wr[r])
-        for w in W:
-            if w in wr:
-                toks.append(wr[w])
-            toks.extend(rd.get(w, []))
-        if q == "t":
-            toks = [t for t in toks if t[0] != "qt"]
-        wait(q, toks)
-
-    def done(tok, R, W):
-        for r in R:
-            rd.setdefault(r, []).append(tok)
-        for w in W:
-            wr[w] = tok
-            rd[w] = []
-
-    def op(q, ins, R, W):
+    def record(alts, R, W, any_order=""):
         R, W = R.split(), W.split()
         W = W + [r for r in R if r[0] == "P" and r != "Pf"]
-        deps(q, R, W)
-        s = "q" + q
-        ins().then_inc(T.sem[s], 1)
-        cnt[s] = cnt.get(s, 0) + 1
-        done((s, cnt[s]), R, W)
+        i, pre = len(ops), set()
+        for r in R:
+            if r in wr:
+                pre.add(wr[r])
+        for w in W:
+            if w in wr:
+                pre.add(wr[w])
+            pre.update(rd.get(w, []))
+        if any_order:
+            pre.add(wr[any_order])
+            R = R + [any_order]
+        for r in R:
+            rd.setdefault(r, []).append(i)
+        for w in W:
+            wr[w] = i
+            rd[w] = []
+        ops.append((sorted(pre), {q: a[:2] for q, a in alts.items()}))
+        calls.append({q: a[2] for q, a in alts.items()})
 
-    def mm(out, terms, R, W, first=True, end=True):
-        def ins():
-            last = None
-            for k, (l, r) in enumerate(terms):
-                last = g.tensor.matmul(out, l, r, first and k == 0, end and k == len(terms) - 1)
+    def ap(x):
+        return x[0].indirect(x[1]) if isinstance(x, tuple) else x
+
+    def cost(q, out, a, other=None, two=False):
+        if isinstance(out, tuple):
+            return 0.06 + 16 * out[1].shape[1] * SC * CY
+        if isinstance(a, tuple):
+            return 0.06 + 16 * a[1].shape[1] * GA * CY
+        n = out.shape[1]
+        if q == "s":
+            return 0.07 + n * CY
+        if two:
+            n *= 1 if "P" in (a.name[0], other.name[0]) else 2
+        elif all("16" in str(x.dtype) for x in (out, a, other) if x is not None):
+            n *= 0.5
+        return max(n, 64) * CY
+
+    v = g.vector
+
+    def TS(out, a, s1, o0, s2=None, o1=None):
+        if o1 is None:
+            return {"v": (cost("v", out, a), 0.0, lambda: v.tensor_scalar(ap(out), ap(a), s1, None, o0))}
+        return {"v": (cost("v", out, a), 0.0, lambda: v.tensor_scalar(ap(out), ap(a), s1, s2, o0, o1))}
+
+    def CP(out, a):
+        return {"v": (cost("v", out, a), 0.0, lambda: v.tensor_copy(ap(out), ap(a)))}
+
+    def ACT(out, a, f, **kw):
+        return {"s": (cost("s", out, a), 0.0, lambda: g.scalar.activation(ap(out), ap(a), f, **kw))}
+
+    def ts(out, a, s1, o0, R, W, s2=None, o1=None):
+        record(TS(out, a, s1, o0, s2, o1), R, W)
+
+    def tt(out, a, b, o, R, W):
+        record({"v": (cost("v", out, a, b, True), 0.0, lambda: v.tensor_tensor(ap(out), ap(a), b, o))}, R, W)
+
+    def cp(out, a, R, W):
+        record(CP(out, a), R, W)
+
+    def act(out, a, f, R, W, **kw):
+        record(ACT(out, a, f, **kw), R, W)
+
+    def either(x, y, R, W):
+        record({**x, **y}, R, W)
+
+    def move(out, a, R, W):
+        either(CP(out, a), ACT(out, a, F.Silu if isinstance(out, tuple) else F.Copy), R, W)
+
+    def copy3(out, a, R, W):
+        n = out.shape[1]
+        record({**CP(out, a), **ACT(out, a, F.Copy), "g": (0.17 + 2 * n * CY, 0.0, lambda: g.affine_select(out, a, [[0, n]], A.is_ge, 0.0, 0, 0))}, R, W)
+
+    def plus(out, a, c, R, W):
+        either(TS(out, a, c, A.add), ACT(out, a, F.Identity, bias=c), R, W)
+
+    def ms(a, c, W):
+        record({"v": (cost("v", a, a), 0.0, lambda: v.memset(a, c))}, "", W)
+
+    def scan(out, a, b, init, o0, o1, R, W):
+        record({"v": (cost("v", out, a, b), 0.0, lambda: v.tensor_tensor_scan(out, a, b, init, o0, o1))}, R, W)
+
+    def iota(out, pat, base, cm, W, flt=True):
+        kw = {"allow_small_or_imprecise_dtypes": True} if flt else {}
+        record({"g": (0.13 + 2 * out.shape[1] * CY, 0.0, lambda: g.iota(out, pat, base, cm, **kw))}, "", W)
+
+    def mms(items, R, W, left=None):
+        def call():
+            if left:
+                left[0] -= 1
+            for k, it in enumerate(items):
+                last = g.tensor.matmul(*it[:4], it[4] if not left else left[0] == 0 and k == len(items) - 1)
             return last
-        op("t", ins, R, W)
+        c = sum(max(64, it[2].shape[1]) * (4 if "32" in str(it[1].dtype) else 1) for it in items) * PE
+        record({"t": (c, 0.0, call)}, R, "" if left else W, W if left else "")
 
-    def dma(name, pairs, R, W, q="y"):
-        R, W = R.split(), W.split()
-        deps(q, R, W)
-        s = "d_" + name
-        for o, i in pairs:
-            Q[q].dma_start(o, i).then_inc(T.sem[s], 16)
-            cnt[s] = cnt.get(s, 0) + 16
-        done((s, cnt[s]), R, W)
+    def mm(out, tl, R, W, first=True, end=True):
+        mms([(out, l, r, first and k == 0, end and k == len(tl) - 1) for k, (l, r) in enumerate(tl)], R, W)
+
+    def more(out, tl, R, W, left):
+        mms([(out, l, r, False, False) for l, r in tl], R, W, left)
+
+    nd, nx = [0], [0]
+
+    def dma(pairs, R, W, kb, q="y"):
+        s = "d%d" % nd[0]
+        nd[0] += 1
+
+        def call():
+            for o, i in pairs:
+                Q[q].dma_start(o, i).then_inc(T.sem[s], 16)
+            return [(s, 16 * len(pairs))]
+        record({q: (0.05 * len(pairs), 2.0 + kb / 200.0, call)}, R, W)
 
     def engines_of(src):
         peers = [c for c in T.cores if c != src]
@@ -123,582 +254,598 @@ def rank_program(g, core, T, topo):
                 used.update(free[:n])
         return out
 
-    nx = [0]
-
-    def exchange(src, dst, d0, w, sign, R, W):
+    def exchange(src, s0, dst, d0, sign, R, W):
         k = nx[0]
         nx[0] += 1
-        deps("g", [R], [])
-        mine = engines_of(core)
-        tr, tot, arr = [], 0, 0
-        for h in range(1, N):
-            c = T.cores[(rank + sign * h) % N]
-            rid, pid = topo.addr(c)[:2]
-            tr.append(RemoteDMATransfer(dst_ids=[DstId(rid=rid, pnc=pid)], dma_engine_mask=sum(1 << e for e in mine[c]),
-                                        remote_sem=T.sem["ar%d" % k], src=src[:, (h - 1) * w:h * w], dst=dst[:, d0 + (h - 1) * w:d0 + h * w]))
-            tot += len(mine[c])
-            arr += len(engines_of(c)[core])
-        g.remote_dma_fused(tr, local_sem=T.sem["lo%d" % k])
-        cnt["lo%d" % k] = tot
-        cnt["ar%d" % k] = arr
-        done(("lo%d" % k, tot), [R], [])
-        done(("ar%d" % k, arr), [], [W])
 
-    v = g.vector
+        def call():
+            mine = engines_of(core)
+            tr, tot, arr = [], 0, 0
+            for h in range(1, N):
+                c = T.cores[(rank + sign * h) % N]
+                rid, pid = topo.addr(c)[:2]
+                tr.append(RemoteDMATransfer(dst_ids=[DstId(rid=rid, pnc=pid)], dma_engine_mask=sum(1 << e for e in mine[c]), remote_sem=T.sem["ar%d" % k],
+                                            src=src[:, s0 + (h - 1) * 256:s0 + h * 256], dst=dst[:, d0 + (h - 1) * 256:d0 + h * 256]))
+                tot += len(mine[c])
+                arr += len(engines_of(c)[core])
+            g.remote_dma_fused(tr, local_sem=T.sem["lo%d" % k])
+            return [("lo%d" % k, tot), ("ar%d" % k, arr)]
+        record({"g": (0.6 + 3.0 * (k == 0), 4.5, call)}, R, W)
 
-    def ts(out, in0, s1, o0, R, W, s2=None, o1=None):
-        if o1 is None:
-            op("v", lambda: v.tensor_scalar(out, in0, s1, None, o0), R, W)
-        else:
-            op("v", lambda: v.tensor_scalar(out, in0, s1, s2, o0, o1), R, W)
+    def terms(Z, rhs):
+        return [(Z[:, 15 - r:143 - r], rhs(r)) for r in range(16)]
 
-    def tt(out, a, b, o, R, W):
-        op("v", lambda: v.tensor_tensor(out, a, b, o), R, W)
+    def conv(out, Z, rhs, R, W):
+        mm(out, terms(Z, rhs), R, W)
 
-    def cp(out, a, R, W):
-        op("v", lambda: v.tensor_copy(out, a), R, W)
-
-    def ms(ap, c, W):
-        op("v", lambda: v.memset(ap, c), "", W)
-
-    def act(out, a, f, R, W, **kw):
-        op("s", lambda: g.scalar.activation(out, a, f, **kw), R, W)
-
-    def iota(out, pat, base, cm, W, flt=True):
-        if flt:
-            op("g", lambda: g.iota(out, pat, base, cm, allow_small_or_imprecise_dtypes=True), "", W)
-        else:
-            op("g", lambda: g.iota(out, pat, base, cm), "", W)
-
-    def conv(out, Z, rhs, R, W, more=(), first=True, end=True):
-        mm(out, list(more) + [(Z[:, 15 - r:143 - r], rhs(r)) for r in range(16)], R, W, first, end)
-
-    def run(fs):
-        for f in fs:
-            f()
-
-    xw = [T.xw0, T.xw1]
-    row = slice(0, 128, 16)
+    row, row1 = slice(0, 128, 16), slice(1, 128, 16)
     SH, AND = A.arith_shift_right, A.bitwise_and
-
-    dma("ld_a", [(T.axoi[:], T.axo[:])], "", "axoi")
-    dma("ld_d", [(T.deni[:], T.den[:])], "", "deni", q="s")
-    dma("ld_x", [(T.xw0[:, 16:2064], T.x0[:])], "", "x0_0 x0_1 x0_2 x0_3")
-    dma("ld_p", [(T.pari[0:8, 0:7], T.par[:])], "", "pari", q="s")
-    iota(T.pi[:, 0:1], [[0, 1]], 0, 1, "pi0", flt=False)
-    iota(T.yrow[:], [[1, 144]], 0, 0, "yrow")
-    iota(T.cdat[:], [[1, 35], [35, 16]], 0, 0, "cdat")
-    iota(T.io1[:], [[1, 1088]], 1, 0, "io1")
-    iota(T.gsel[0:8, :], [[1, 8], [0, 16]], 0, -1, "gsel")
-    iota(T.jio[:], [[1, 512]], 0, 0, "jio")
-    ms(T.zer[:], 0.0, "zer")
-    pf = T.pf
-    ts(T.pi[:, 1:2], T.pi[:, 0:1], 15, AND, "pi0", "pi1")
-    ts(T.pi[:, 2:3], T.pi[:, 0:1], 112, AND, "pi0", "pi2")
-    ts(T.pi[:, 3:4], T.pi[:, 0:1], 3, AND, "pi0", "pi3")
-    ts(T.pi[:, 4:5], T.pi[:, 0:1], 2, SH, "pi0", "pi4", 3, AND)
-    ts(T.pi[:, 5:6], T.pi[:, 0:1], 8, AND, "pi0", "pi5")
-    cp(pf[:, 0:6], T.pi[:, 0:6], "pi0 pi1 pi2 pi3 pi4 pi5", "pfa")
-    ts(pf[:, 6:7], pf[:, 2:3], 15.0, A.add, "pfa", "pf6")
-    ts(pf[:, 7:8], pf[:, 1:2], 0.0, A.is_equal, "pfa", "pf7")
-    ts(pf[:, 8:9], pf[:, 1:2], 16.0, A.add, "pfa", "pf8")
-    ts(pf[:, 9:10], pf[:, 7:8], 16.0, A.mult, "pf7", "pf9")
-    ts(pf[:, 10:11], pf[:, 1:2], 35.0, A.mult, "pfa", "pf10")
-    ms(T.flG[:, 512:560], 0.0, "flG1")
-    ms(T.flT[:, 512:560], 0.0, "flT1")
-    ms(T.cum[:, 0:1], 0.0, "cum0")
-    ms(T.wb[:, 512:560], 0.0, "wb")
-    for Z, w, n in ((T.Zh, 1.0, "Zh"), (T.Z1h, pf[:, 7:8], "Z1h"), (T.Zr, pf[:, 8:9], "Zr"), (T.Zq, pf[:, 1:2], "Zq"),
-                    (T.Z16, pf[:, 9:10], "Z16"), (T.Z1f, pf[:, 7:8], "Z1f")):
-        ts(Z[:], T.yrow[:], pf[:, 6:7], A.is_equal, "yrow pf6 pf7 pf8 pf9 pfa", n, w, A.mult)
-    ts(T.f1[:, 0:128], T.yrow[:, 0:128], pf[:, 6:7], A.is_le, "yrow pf6", "f1")
-    ts(T.f2[:, 0:128], T.yrow[:, 0:128], pf[:, 2:3], A.is_ge, "yrow pfa", "f2")
-    ts(T.f3[:, 0:128], T.yrow[:, 0:128], pf[:, 0:1], A.is_ge, "yrow pfa", "f3")
-    tt(T.BOh[:], T.f1[:, 0:128], T.f2[:, 0:128], A.mult, "f1 f2", "BOh")
-    tt(T.TRI[:], T.f1[:, 0:128], T.f3[:, 0:128], A.mult, "f1 f3", "TRI")
-    ts(T.Dc[:], T.yrow[:, 0:36], pf[:, 10:11], A.add, "yrow pf10", "Dc", 1089.0, A.add)
-    ts(T.gam[:], T.yrow[:, 0:68], 16.0, A.mult, "yrow pfa", "gam", pf[:, 1:2], A.add)
-
-    def clear_l1():
-        act(T.L1[:, 0:1088], T.zer[:], F.Copy, "zer", "L1")
-    clear_l1()
-    act(T.dT[:], T.zer[:], F.Copy, "zer", "dT")
-    act(T.dG[:], T.zer[:], F.Copy, "zer", "dG")
-    for b, c0 in enumerate((8384, 10432)):
-        act(T.BW[:, c0:c0 + 768], T.zer[:, 0:768], F.Identity, "zer", "Bg%d" % b, bias=63.0)
-    for k in range(3):
-        act(T.BW[:, 1024 * k:1024 * k + 1024], T.zer[:, 0:1024], F.Copy, "zer", "Bi%d" % k)
-    for k in range(3, 8):
-        iota(T.BW[:, 1024 * k:1024 * k + 1024], [[0, 1024]], 0, 0, "Bi%d" % k)
-    for k in range(4):
-        iota(T.BW[:, 8192 + 2048 * k:8384 + 2048 * k], [[0, 192]], 64, 0, "BL")
-
-    def compact(fl, fn, no, clamp, h1=(), h2=(), h3=()):
-        n = 16 * no
-        conv(T.PX[:, 0:36], T.Zh, lambda r: T.cum[:, 35 * r:35 * r + 36], "Zh cum cum0", "PX")
-        mm(T.P0[:], [(T.BOh[:], T.cum[:, 0:512]), (T.TRI[:], fl[:, 0:512])], "BOh TRI cum cum0 " + fn, "P0")
-        mm(T.P1[:, 0:48], [(T.BOh[:], T.cum[:, 512:560]), (T.TRI[:], fl[:, 512:560])], "BOh TRI cum " + fn, "P1")
-        run(h1)
-        if clamp:
-            tt(T.se[:], T.PX[:, 0:36], T.CL[:], A.min, "PX CL", "se")
-        else:
-            ts(T.se[:], T.PX[:, 0:36], 1088.0, A.min, "PX", "se")
-        tt(T.f1[:, 0:35], T.se[:, 1:36], T.se[:, 0:35], A.is_le, "se", "f1")
-        tt(T.f1[:, 0:35], T.f1[:, 0:35], T.Dc[:, 0:35], A.mult, "f1 Dc", "f1")
-        tt(T.f1[:, 0:35], T.f1[:, 0:35], T.se[:, 0:35], A.add, "f1 se", "f1")
-        cp(T.o1[:, 0:35], T.f1[:, 0:35], "f1", "o1")
-        cp(T.L1[:].indirect(T.o1[:, 0:35]), T.cdat[:], "o1 cdat", "L1")
-        run(h2)
-        op("v", lambda: v.tensor_tensor_scan(T.cw[:, 0:n], T.L1[:, 0:n], T.L1[:, 0:n], 0.0, A.max, A.max), "L1", "cw")
-        conv(T.PX[:, 64:64 + no], T.Z1h, lambda r: T.cw[:, r:n:16], "Z1h cw", "PX")
-        conv(T.PY[:, 128:128 + no], T.Z16, lambda r: T.cw[:, no * r:no * r + no], "Z16 cw", "PY", end=False)
-        run(h3)
-        tt(T.tab[:, 0:512], T.P0[:], fl[:, 0:512], A.mult, "P0 " + fn, "tab0")
-        tt(T.tab[:, 512:560], T.P1[:, 0:48], fl[:, 512:560], A.mult, "P1 " + fn, "tab1")
-        cp(T.o2[:, 0:no], T.PX[:, 64:64 + no], "PX", "o2")
-        ts(T.cf[:, 0:no], T.PX[:, 64:64 + no], 16.0, A.mult, "PX", "cf", -16.0, A.add)
-        tt(T.M[:, 0:n], T.tab[:].indirect(T.o2[:, 0:no]), T.io1[:, 0:n], A.is_equal, "tab0 tab1 o2 io1", "M rr0 rr1")
-        conv(T.PY[:, 128:128 + no], T.Zq, lambda r: T.M[:, no * r:no * r + no], "Zq M", "PY", first=False)
-        conv(T.PX[:, 192:192 + no], T.Zr, lambda r: T.M[:, r:n:16], "Zr M", "PX")
-
-    def scan(fl, fn, a, b, init, R=""):
-        op("v", lambda: v.tensor_tensor_scan(T.cum[:, a + 1:b + 1], fl[:, a:b], fl[:, a:b], init, A.add, A.max), fn + " " + R, "cum")
-
-    def invert(src, sn, c0, gn, d, dn, ol, on, bank, h1=(), h2=(), h3=()):
-        ts(T.flG[:, 0:512], src[:], 8192.0, A.is_ge, sn, "flG0")
-        scan(T.flG, "flG0 flG1", 0, 560, 0.0)
-        ts(T.wb[:, 0:512], src[:], -8192.0, A.add, sn, "wb", 0.25, A.mult)
-        compact(T.flG, "flG0 flG1", 48, False, h1, h2, h3)
-        clear_l1()
-        tt(T.flE[:], T.wb[:].indirect(T.o2[:, 0:48]), T.M[:, 0:768], A.mult, "wb o2 M", "Eh")
-        act(T.valT[:, 0:48], T.PY[:, 128:176], F.Identity, "PY", "valT", bias=64.0)
-        dma(dn, [(d[row, 0:768], T.valT[:, 0:48])], "valT", dn)
-        conv(T.PK[:, 0:48], T.Zh, lambda r: T.flE[:, r:768:16], "Zh Eh", "PK")
-        ts(T.f1[:, 0:48], T.PX[:, 192:240], 16.0, A.is_ge, "PX", "f1")
-        ts(T.f3[:, 0:48], T.gam[:, 0:48], 768.0, A.add, "gam", "f3")
-        tt(T.f2[:, 0:48], T.PK[:, 0:48], T.f3[:, 0:48], A.subtract, "PK f3", "f2")
-        tt(T.f2[:, 0:48], T.f2[:, 0:48], T.f1[:, 0:48], A.mult, "f1 f2", "f2")
-        tt(T.f2[:, 0:48], T.f2[:, 0:48], T.f3[:, 0:48], A.add, "f2 f3", "f2")
-        cp(ol, T.f2[:, 0:48], "f2", on)
-        return (lambda: act(T.BW[:, c0:c0 + 1536].indirect(ol), d[:, 0:768], F.Silu, on + " " + dn, gn),
-                lambda: conv(T[bank][:, 0:48], T.Z1f, lambda r: T.BW[:, c0 + r:c0 + 768:16], "Z1f " + gn, bank))
-
-    def pos_b(I, In, n, dum, dn, out, on):
-        ts(T.i2[:, 0:n], I, 15, AND, In, "i2")
-        ts(T.i3[:, 0:n], I, 4, SH, In, "i3", 1023, AND)
-        ts(T.f1[:, 0:n], T.i2[:, 0:n], 512.0, A.mult, "i2", "f1")
-        ts(T.f2[:, 0:n], T.i3[:, 0:n], 512.0, A.is_ge, "i3", "f2", 7680.0, A.mult)
-        tt(T.f1[:, 0:n], T.f1[:, 0:n], T.i3[:, 0:n], A.add, "f1 i3", "f1")
-        tt(T.f2[:, 0:n], T.f2[:, 0:n], dum, A.subtract, "f2 " + dn, "f2")
-        tt(out, T.f1[:, 0:n], T.f2[:, 0:n], A.add, "f1 f2", on)
-
-    def pos_a(I, In, n, out, on):
-        ts(T.i2[:, 0:n], I, 2, SH, In, "i2", 15, AND)
-        ts(T.i3[:, 0:n], I, 3, AND, In, "i3")
-        ts(T.i4[:, 0:n], I, 6, SH, In, "i4")
-        ts(T.f1[:, 0:n], T.i2[:, 0:n], 560.0, A.mult, "i2", "f1")
-        ts(T.f2[:, 0:n], T.i3[:, 0:n], 128.0, A.mult, "i3", "f2")
-        ts(T.f3[:, 0:n], T.i4[:, 0:n], 128.0, A.is_ge, "i4", "f3", 384.0, A.mult)
-        tt(T.f1[:, 0:n], T.f1[:, 0:n], T.i4[:, 0:n], A.add, "f1 i4", "f1")
-        tt(T.f2[:, 0:n], T.f2[:, 0:n], T.dumA[:, 0:n], A.subtract, "f2 dumA", "f2")
-        tt(T.f1[:, 0:n], T.f1[:, 0:n], T.f3[:, 0:n], A.add, "f1 f3", "f1")
-        tt(out, T.f1[:, 0:n], T.f2[:, 0:n], A.add, "f1 f2", on)
-
-    def pick(out, on, pd, pn, flag, fn, dum, dn, n):
-        t = T.f4[:, 0:n]
-        tt(t, pd, flag, A.mult, pn + " " + fn, "f4")
-        tt(t, t, dum, A.add, "f4 " + dn, "f4")
-        cp(out, t, "f4", on)
+    Pq = [T.P0, T.P1, T.P2, T.P3]
+    pf, col, pc = T.pf, T.col, T.pc
+    Y0 = PL + 16
+    yv = [lambda a, b, s=1: T.xw0[:, Y0 + a:Y0 + b:s], lambda a, b, s=1: T.xw1[:, 16 + a:16 + b:s]]
+    YP = "yp0 yp1 yp2 yp3"
+    LK = slice(128, 176)
+    one = (T.cb[0:1, 512:640], T.cb[0:1, 0:512])
+    sel15 = T.ch[0:1, 704:832]
 
     def xn(b):
         return " ".join("x%d_%d" % (b, q) for q in range(4))
 
-    def send_values(b):
-        act(T.snd[:], xw[b][:, 0:2064].indirect(T.off[:, 512:560]), F.Copy, "offL vac " + xn(b), "snd")
-        exchange(T.snd, xw[b], 2064, 256, 1, "snd", "xl%d" % b)
+    def own(a, b):
+        return T.xw0[:, 16 + a:16 + b]
 
-    def own(hq):
-        return T.VA[:, 5120 + 3072 * hq:6144 + 3072 * hq]
+    def pl(B, j, a=0, b=128):
+        return B[:, 176 * j + a:176 * j + b]
 
-    def own_values(b, vec):
-        for hq in range(2):
-            src = xw[b][:, 16 + 1024 * hq:1040 + 1024 * hq]
-            if vec:
-                cp(own(hq), src, xn(b), "W%d1" % (2 + 2 * hq))
-            else:
-                act(own(hq), src, F.Copy, xn(b), "W%d1" % (2 + 2 * hq))
+    def clear(bank, n):
+        mm(T[bank][:, 0:n], [(T.Zq[0:1, 16:144], T.cb[0:1, 0:n])], "Zq cb0", bank, True, False)
 
-    put, fin = invert(T.axoi, "axoi", 8384, "Bg0", T.dT, "dT", T.oL[:], "oL", "PS")
-    put()
-    ms(T.xw0[:, 0:16], -16.0, "vac")
-    ms(T.xw1[:, 0:16], -16.0, "vac")
-    tt(pf[:, 12:13], pf[:, 2:3], pf[:, 4:5], A.add, "pfa", "pf12")
-    ts(pf[:, 13:14], pf[:, 3:4], 4.0, A.mult, "pfa", "pf13", pf[:, 2:3], A.add)
+    dma([(T.axoi[:], T.axo[:])], "", "axoi", 256)
+    dma([(T.AI[:, 0:512], T.den[:])], "", "AI", 512, q="s")
+    dma([(T.V[:, 0:2048], T.x0[:])], "", "V00 V01", 1024)
+    dma([(T.pari[0:8, 0:7], T.par[:])], "", "pari", 0, q="s")
+    iota(T.pi[:, 0:1], [[0, 1]], 0, 1, "pi0", flt=False)
+    iota(T.yrow[:], [[1, 144]], 0, 0, "yrow")
+    iota(T.wb[0:32, 0:592], [[1, 592]], 0, 0, "wb")
+    iota(T.f1[:, 0:64], [[1, 32], [0, 2]], 0, 0, "f1")
+    iota(T.dumA[:], [[176, 3], [1, 48]], 304, 0, "dumA")
+    iota(T.dumK[:], [[4, 48], [1, 3]], 8257, 0, "dumK")
+    iota(T.hiF[0:8, :], [[1, 8], [0, 16]], 0, -1, "hiF")
+    iota(T.RV[:], [[0, 2048]], -32, 0, "RV")
+    record({"g": (3.9, 0.0, lambda: g.affine_select(T.RV[:], T.RV[:], [[-1, 16], [-16, 8], [0, 16]], A.is_equal, 0.0, 0, 1))}, "RV", "RV")
+    iota(T.AX[:, 8256:AXW:4], [[0, 768]], 64, 0, "AXl")
+    ms(T.zer[:], 0.0, "zer")
+    for B, n in ((T.La, "La"), (T.dT, "dT")):
+        plus(B[:, 0:1024], T.zer[:], 64.0, "zer", n)
+        plus(B[:, 1024:1088], T.zer[:, 0:64], 64.0, "zer", n)
+    ts(T.pi[:, 1:2], T.pi[:, 0:1], 15, AND, "pi0", "pi1")
+    ts(T.pi[:, 2:3], T.pi[:, 0:1], 112, AND, "pi0", "pi2")
+    ts(T.pi[:, 3:4], T.pi[:, 0:1], 3, AND, "pi0", "pi3")
+    ts(T.pi[:, 4:5], T.pi[:, 0:1], 2, SH, "pi0", "pi4", 3, AND)
+    ts(T.pi[:, 5:6], T.pi[:, 0:1], 31, AND, "pi0", "pi5")
+    cp(pf[:, 0:6], T.pi[:, 0:6], "pi0 pi1 pi2 pi3 pi4 pi5", "pfa")
+    ts(pf[:, 6:7], pf[:, 2:3], 15.0, A.add, "pfa", "pf6")
+    ts(pf[:, 7:8], pf[:, 1:2], 0.0, A.is_equal, "pfa", "pf7")
+    ts(pf[:, 8:9], pf[:, 1:2], 15.0, A.is_equal, "pfa", "pf8")
+    ms(T.cumG[:, 0:1], 0.0, "cumG0")
+    ms(T.cumT[:, 0:1], 0.0, "cumT0")
+    ts(pf[:, 9:10], pf[:, 8:9], 17.0, A.mult, "pf8", "pf9", -1.0, A.add)
+    ts(pf[:, 10:11], pf[:, 8:9], 4032.0, A.mult, "pf8", "pf10", 64.0, A.add)
+    ts(pf[:, 11:12], pf[:, 8:9], -1.0, A.mult, "pf8", "pf11", 1.0, A.add)
+    ts(T.g1[:, 0:128], T.yrow[:, 0:128], pf[:, 6:7], A.is_le, "yrow pf6", "g1")
+    ts(T.f2[:, 0:128], T.yrow[:, 0:128], pf[:, 2:3], A.is_ge, "yrow pfa", "f2 f2b")
+    ts(T.f3[:, 0:128], T.yrow[:, 0:128], pf[:, 0:1], A.is_ge, "yrow pfa", "f3")
+    ts(T.f4[:, 0:128], T.yrow[:, 0:128], pf[:, 6:7], A.is_lt, "yrow pf6", "f4 f4b")
+    tt(T.BOh[:], T.g1[:, 0:128], T.f2[:, 0:128], A.mult, "g1 f2 f2b", "BOh")
+    tt(T.TRI[:], T.g1[:, 0:128], T.f3[:, 0:128], A.mult, "g1 f3", "TRI")
+    tt(T.TRp[:], T.f4[:, 0:128], T.f3[:, 0:128], A.mult, "f4 f4b f3", "TRp")
+    ts(T.TRe[:], T.TRI[:], 64.0, A.mult, "TRI", "TRe")
+    ts(T.gam[:, 0:68], T.yrow[:, 0:68], 16.0, A.mult, "yrow pfa", "gam", pf[:, 1:2], A.add)
+    cp(T.ch[0:32, 0:592], T.wb[0:32, 0:592], "wb", "ch")
+    ts(T.ch[0:32, 592:704], T.wb[0:32, 0:112], 592.0, A.add, "wb", "ch1")
+    ms(T.ch[0:32, 704:832], 0.0, "ch2")
+    ms(T.ch[0:32, 719:832:16], 1.0, "ch2")
+    ts(T.Dc[:], T.gam[:, 0:40], 1088.0, A.add, "gam", "Dc")
+    move(T.Lb[:, 0:768], T.zer[:, 0:768], "zer", "Lb")
+    plus(T.DEC[:, 0:1024], T.zer[:], pf[:, 11:12], "zer pf11", "DEC")
+    plus(T.DEC[:, 1024:1088], T.zer[:, 0:64], pf[:, 11:12], "zer pf11", "DEC1")
+    move(T.snd[:, 0:768], T.zer[:, 0:768], "zer", "snd")
+    move(T.D[:], T.zer[:, 0:704], "zer", "D DL")
+    move(T.dG[:, 768:1088], T.zer[:, 0:320], "zer", "dG1")
+    for a in (0, PL, W0 - 16):
+        ms(T.xw0[:, a:a + 16], 0.0, "vac")
+    ms(T.xw1[:, 0:16], 0.0, "vac1")
+    ts(pf[:, 23:24], pf[:, 7:8], 1024.0, A.mult, "pf7", "pf23")
+    ts(pf[:, 24:25], pf[:, 8:9], 513.0, A.mult, "pf8", "pf24", -512.0, A.add)
+    for Z, w, n, R in ((T.Zh, 1.0, "Zh", ""), (T.Zc, pf[:, 9:10], "Zc", "pf9"), (T.Zb, 1.0, "Zb", ""), (T.Zk, 65536.0, "Zk", ""), (T.Zr, 131072.0, "Zr", ""),
+                       (T.Zn, -65536.0, "Zn", ""), (T.Zq, pf[:, 23:24], "Zq", "pf23"), (T.Zt, pf[:, 24:25], "Zt", "pf24")):
+        ts(Z[:], T.yrow[:], pf[:, 6:7], A.is_equal, "yrow pf6 " + R, n, w, A.mult)
+    for I, w, n in ((T.Ie, 1.0 / 128, "Ie"), (T.Ib, 1.0, "Ib"), (T.I4, 4.0, "I4"), (T.In, -1.0, "In"), (T.If, 1.0, "If"), (T.Ig, -65536.0, "Ig")):
+        ts(I[:], T.yrow[:, 0:128], pf[:, 0:1], A.is_equal, "yrow pfa", n, w, A.mult)
+    ms(T.cb[0:32, 0:512], 1.0, "cb0")
+    ms(T.cb[0:32, 512:640], 3072.0, "cb1")
+    ms(T.cb[0:32, 896:976], -832.0, "cb6")
+    ms(T.cb[0:32, 640:768], 65536.0, "cb2")
+    ms(T.cb[0:32, 768:896], -16384.0, "cb2")
     for j in range(4):
         ts(pf[:, 14 + j:15 + j], pf[:, 3:4], float(j), A.is_equal, "pfa", "pm%d" % j)
         ts(pf[:, 18 + j:19 + j], pf[:, 4:5], float(j), A.is_equal, "pfa", "pn%d" % j)
-    ts(pf[:, 12:13], pf[:, 12:13], 12.0, A.add, "pf12", "pf12")
-    ts(pf[:, 13:14], pf[:, 13:14], 3.0, A.add, "pf13", "pf13")
+    ts(pf[:, 12:13], pf[:, 1:2], 704.0, A.mult, "pfa", "pf12")
+    ts(T.dumA[:], T.dumA[:], pf[:, 12:13], A.add, "dumA pf12", "dumA")
+    ts(pf[:, 13:14], pf[:, 2:3], pf[:, 4:5], A.add, "pfa", "pf13", 12.0, A.add)
+    ts(pf[:, 25:26], pf[:, 3:4], 4.0, A.mult, "pfa pf6", "pf25", pf[:, 6:7], A.add)
+    ts(pf[:, 25:26], pf[:, 25:26], -12.0, A.add, "pf25", "pf25")
     for j in range(4):
-        ts(T.Pf[:, 144 * j:144 * j + 144], T.yrow[:], pf[:, 12:13], A.is_equal, "yrow pf12 pm%d" % j, "Pf", pf[:, 14 + j:15 + j], A.mult)
-    cp(T.wa[:, 0:512], T.deni[:], "deni", "wa")
-    ts(T.tmpA[:, 0:512], T.axoi[:], 64.0, A.add, "axoi", "tmpA")
-    dma("bw2", [(T.BW[row, 0:8192], T.tmpA[:, 0:512])], "tmpA", "BW " + " ".join("Bi%d" % k for k in range(8)))
+        ts(T.Pf[:, 144 * j:144 * j + 144], T.yrow[:], pf[:, 13:14], A.is_equal, "yrow pf13 pm%d" % j, "Pf", pf[:, 14 + j:15 + j], A.mult)
+        ts(T.Qh[:, 144 * j:144 * j + 144], T.yrow[:], pf[:, 25:26], A.is_equal, "yrow pf25 pn%d" % j, "Qh", pf[:, 18 + j:19 + j], A.mult)
+    ts(pf[:, 26:27], pf[:, 1:2], 192.0, A.mult, "pfa", "pf26")
+    ts(T.dumK[:], T.dumK[:], pf[:, 26:27], A.add, "dumK pf26", "dumK")
+    tt(T.TRs[:], T.TRI[:], T.Ib[:], A.subtract, "TRI Ib", "TRs")
+    ts(T.CL[:, 0:37], T.Dc[:, 0:37], 1088.0 + 527.5, A.is_ge, "Dc", "CL", 64.0, A.mult)
+    ts(T.CL[:, 0:37], T.CL[:, 0:37], 1024.0, A.add, "CL", "CL")
+    cp(T.CL[:, 37:74], T.CL[:, 0:37], "CL", "CL")
+    ts(col[:, 20:21], pf[:, 8:9], 5.0, A.mult, "pf8 pm3", "c20", pf[:, 17:18], A.subtract)
+    ts(T.Wv[:, 0:128], T.BOh[:], col[:, 20:21], A.mult, "BOh c20", "Wv")
+    ts(T.Wv[:, 128:256], T.BOh[:], col[:, 20:21], A.mult, "BOh c20", "Wv1", -1.0, A.mult)
+    ts(col[:, 22:23], pf[:, 1:2], 68.0, A.mult, "pfa", "c22")
+    ts(T.gam[:, 68:136], T.yrow[:, 0:68], col[:, 22:23], A.add, "yrow c22", "gam2")
+    ms(T.flT[:, 512:528], 0.0, "flT1")
+    cp(T.parf[0:8, 0:7], T.pari[0:8, 0:7], "pari", "parf")
+    ts(T.hiF[0:8, :], T.hiF[0:8, :], 0.0, A.is_equal, "hiF", "hiF")
 
-    def to_planes(j):
-        mm(T.P2[:, 128 * j:128 * j + 128], [(T.Pf[:, 144 * j + 12 - 4 * b:144 * j + 140 - 4 * b], T.wa[:, b:512:4]) for b in range(4)], "Pf wa", "P2")
-    to_planes(0)
+    def heads(cum, cn, nb, lim, se, sn, o1, on, bank):
+        k = nb // 16
+        conv(T[bank][:, 0:k], T.Zh, lambda r: cum[:, r:nb:16], "Zh " + cn, bank)
+        conv(T[bank][:, k:2 * k], T.Zh, lambda r: cum[:, r + 1:nb + 1:16], "Zh " + cn, bank)
+        if lim is None:
+            ts(se[:, 0:2 * k], T[bank][:, 0:2 * k], 1088.0, A.min, bank, sn)
+        else:
+            tt(se[:, 0:2 * k], T[bank][:, 0:2 * k], lim, A.min, bank + " CL", sn)
+        tt(se[:, k:2 * k], se[:, k:2 * k], se[:, 0:k], A.is_le, sn, sn)
+        tt(se[:, k:2 * k], se[:, k:2 * k], T.Dc[:, 0:k], A.mult, sn + " Dc", sn)
+        tt(se[:, 0:k], se[:, k:2 * k], se[:, 0:k], A.max, sn, sn)
+        cp(o1[:, 0:k], se[:, 0:k], sn, on)
 
-    def first_values():
-        ts(T.off[:, 512:560], T.PS[:, 0:48], 0.25, A.mult, "PS", "offL", -0.375, A.add)
-        ts(T.AI[:, 512:560], T.PS[:, 0:48], -64.0, A.add, "PS", "AIL")
-        send_values(0)
-        own_values(0, False)
-    put, fin = invert(T.deni, "deni", 10432, "Bg1", T.dG, "dG", T.oA[:, 128:176], "oA2", "PY",
-                      [fin, lambda: to_planes(1)], [first_values], [lambda: to_planes(2)])
-    to_planes(3)
-    for Z, w, n in ((T.Zb, 1.0, "Zb"), (T.Zk, 65536.0, "Zk"), (T.Z1b, pf[:, 7:8], "Z1b")):
-        ts(Z[:], T.yrow[:], pf[:, 6:7], A.is_equal, "yrow pf6 pf7", n, w, A.mult)
-    ts(T.off[:, 0:512], T.P2[:], 0.25, A.mult, "P2", "off", 15.625, A.add)
-    cp(T.AI[:, 0:512], T.P2[:], "P2", "AI")
-    for I, w, n in ((T.Ib, 1.0, "Ib"), (T.I4, 4.0, "I4"), (T.In, -1.0, "In"), (T.If, 1.0, "If")):
-        ts(I[:], T.yrow[:, 0:128], pf[:, 0:1], A.is_equal, "yrow pfa", n, w, A.mult)
-    ms(T.cb[0:32, 0:640], 1.0, "cb0")
-    ms(T.cb[0:32, 640:768], 3072.0, "cb1")
+    def counts(fl, fn, nb, c1, wd, wn, ba, bb):
+        mm(T[ba][:], [(T.TRp[:], fl[:, 0:512]), (sel15, T.ch[0:1, 0:512])], "TRp ch ch2 " + fn, ba)
+        plus(wd[:, 0:512], T[ba][:], 64.0, ba, wn)
+        if nb > 512:
+            mm(T[bb][:, 0:nb - 512], [(T.TRp[:], fl[:, 512:nb]), (sel15, T.ch[0:1, c1:c1 + nb - 512])], "TRp ch ch1 ch2 " + fn, bb)
+            plus(wd[:, 512:nb], T[bb][:, 0:nb - 512], 64.0, bb, wn + "1")
+
+    def run_down(L, ln, cw, cn, a, b, init, R=""):
+        scan(cw[:, a:b], L[:, a:b], T.DEC[:, a:b], init, A.max, A.subtract, ln + " DEC DEC1 " + R, cn)
+
+    def link_list(src, sn, fl, fn, cum, cn, se, sen, o1, on, bank, pb):
+        ts(fl[:, 0:512], src, 8192.0, A.is_ge, sn, fn)
+        ts(T.flE[:, 0:512], src, -8192.0, A.add, sn, "flE", 0.0, A.max)
+        scan(cum[:, 1:513], fl[:, 0:512], fl[:, 0:512], 0.0, A.add, A.max, fn, cn)
+        heads(cum, cn + " " + cn + "0", 512, None, se, sen, o1, on, bank)
+        mm(T[pb][:], [(T.TRe[:], fl[:, 0:512]), (T.Ie[:], T.flE[:, 0:512])], "TRe Ie flE " + fn, pb)
+        move(T.wb[:, 0:512], T[pb][:], pb, "wb")
+        move((T.Lb[:], o1[:, 0:32]), T.wb[:, 0:512], on + " wb", "Lb")
+        scan(T.dG[:, 0:768], T.Lb[:, 0:768], T.dT[:, 0:768], 0.0, A.max, A.subtract, "Lb dT", "dG")
+        ts(T.cwb[:, 0:768], T.dG[:, 0:768], 0.0, A.max, "dG", "cwb", 32.0, A.min)
+        conv(T[bank][:, 64:112], T.Zh, lambda r: T.cwb[:, r:768:16], "Zh cwb", bank)
+
+    def place(I, In, n, out, on):
+        ts(T.i2[:, 0:n], I, 63, AND, In, "i2")
+        ts(T.i2[:, 68:68 + n], I, 6, SH, In, "i3")
+        ts(T.f4[:, 68:68 + n], T.i2[:, 0:n], 176.0, A.mult, "i2", "f4b")
+        tt(out, T.f4[:, 68:68 + n], T.i2[:, 68:68 + n], A.add, "f4b i3", on)
+
+    def pick(pos, pn, inv, vn, dum, n, out, on):
+        tt(T.dA[:, 0:n], dum, pos, A.subtract, "dumA " + pn, "dA")
+        tt(T.dA[:, 0:n], T.dA[:, 0:n], inv, A.mult, "dA " + vn, "dA")
+        tt(T.dA[:, 0:n], T.dA[:, 0:n], pos, A.add, "dA " + pn, "dA")
+        cp(out, T.dA[:, 0:n], "dA", on)
+
+    link_list(T.axoi[:], "axoi", T.flG, "flG0 flG1", T.cumG, "cumG", T.sea, "sea", T.oa, "oa", "PX", "P1")
+    counts(T.flG, "flG0", 512, 0, T.wa, "wa", "P0", "")
+    mm(T.PY[:, 0:1], [(T.BOh[:], T.cumG[:, 512:513])], "BOh cumG", "PY")
+    plus(yv[0](0, 2048), T.V[:, 0:2048], 16.0, "V00 V01", xn(0))
+    move((T.La[:], T.oa[:, 0:32]), T.wa[:, 0:512], "oa wa", "La")
+    cp(col[:, 0:1], T.PY[:, 0:1], "PY", "c0")
+    run_down(T.La, "La", T.cwa, "cwa", 0, 768, 64.0)
+    ts(T.cwa[:, 0:768], T.cwa[:, 0:768], pf[:, 10:11], A.min, "cwa pf10", "cwa")
+    conv(T.PS[:, 0:48], T.Zc, lambda r: T.cwa[:, r:768:16], "Zc cwa", "PS")
+    ts(T.oS[:, 0:48], T.PS[:, 0:48], 0.25, A.mult, "PS", "oS", -0.375, A.add)
+    conv(T.PS[:, 64:112], T.Zc, lambda r: T.cwa[:, 48 * r:48 * r + 48], "Zc cwa", "PS")
+    move(T.M[:, 0:768], (T.xw0[:, PL:Y0 + 2048], T.oS[:, 0:48]), "oS vac " + xn(0), "rr0 rr1")
+    ts(T.inv[:, 0:48], T.gam[:, 0:48], col[:, 0:1], A.is_ge, "gam c0", "inv")
+    ts(T.f3[:, 0:48], T.gam[:, 0:48], 768.0, A.add, "gam", "f3")
+    ts(T.i1[:, 0:48], T.PX[:, 64:112], 32.0, A.mult, "PX", "i1")
+    tt(T.f3[:, 0:48], T.f3[:, 0:48], T.inv[:, 0:48], A.mult, "f3 inv", "f3")
+    ts(T.i1[:, 0:48], T.i1[:, 0:48], 1023, AND, "i1", "i1")
+    tt(T.f3[:, 0:48], T.f3[:, 0:48], T.i1[:, 0:48], A.max, "f3 i1", "f3")
+    cp(T.oL[:], T.f3[:, 0:48], "f3", "oL")
+    cp((T.snd[:], T.oL[:]), T.M[:, 0:768], "oL rr0 rr1", "snd msS")
+    exchange(T.snd, 0, T.xw0, Y0 + 2048, 1, "snd", "xl0")
+    move(T.valG[:, 0:48], T.PS[:, 64:112], "PS", "valG")
+    move(T.Lb[:, 0:768], T.zer[:, 0:768], "zer", "Lb")
+    ts(T.i1[:, 0:48], T.i1[:, 0:48], 4.0, A.mult, "i1", "i1", 8192.0, A.add)
+    place(T.i1[:, 0:48], "i1", 48, T.f4[:, 0:48], "f4")
+    pick(T.f4[:, 0:48], "f4", T.inv[:, 0:48], "inv", T.dumA[:, 48:96], 48, T.oT[:, 0:48], "oT")
+    cp(T.Fb[:], T.AI[:, 0:512], "AI", "Fb")
     for j in range(4):
-        ms(T.cb[0:32, 768 + 128 * j:896 + 128 * j], 16384.0 * (4 - j), "cb%d" % (2 + j))
+        mm(T.PK[:, 128 * j:128 * j + 128], [(T.Pf[:, 144 * j + 12 - 4 * b:144 * j + 140 - 4 * b], T.Fb[:, b:512:4]) for b in range(4)], "Pf Fb", "PK")
+    for j in range(4):
+        plus(pl(T.D, j), T.PK[:, 128 * j:128 * j + 128], 64.0, "PK", "D")
+    ts(T.off[:], T.D[:], 0.25, A.mult, "D DL", "off offL", -0.375, A.add)
+    dma([(T.UA[row, :], T.D[:])], "D DL", "UA", 360)
+    link_list(T.AI[:, 0:512], "AI", T.flT, "flT0", T.cumT, "cumT", T.seb, "seb", T.ob, "ob", "PX", "PS")
+    dma([(T.dG[row, 0:768], T.valG[:, 0:48])], "valG", "dG", 30)
+    move((T.UA[:], T.oT[:, 0:48]), T.dG[:, 0:768], "oT dG", "UA")
+    mm(T.PY[:, 0:1], [(T.BOh[:], T.cumT[:, 512:513])], "BOh cumT", "PY")
+    cp(col[:, 1:2], T.PY[:, 0:1], "PY", "c1")
+    mm(T.PY[:, 0:7], [(T.hiF[0:8, :], T.parf[0:8, 0:7])], "hiF parf", "PY")
+    cp(pc[:, 0:7], T.PY[:, 0:7], "PY", "pc")
+    ts(pc[:, 8:11], pc[:, 0:3], 256.0, A.add, "pc", "pc2")
+    ts(T.inv[:, 68:116], T.gam[:, 0:48], col[:, 1:2], A.is_ge, "gam c1", "invX")
+    ts(T.i1[:, 0:48], T.PX[:, 64:112], 32.0, A.mult, "PX", "i1")
+    ts(T.i1[:, 0:48], T.i1[:, 0:48], 1023, AND, "i1", "i1")
+    ts(T.i1[:, 0:48], T.i1[:, 0:48], 4.0, A.mult, "i1", "i1", 8256.0, A.add)
+    iota(T.La[:, 0:1088], [[0, 1088]], 64, 0, "La")
+    iota(T.Lb[:, 0:1088], [[0, 1088]], 64, 0, "Lb")
+    dma([(T.D[:], T.UA[row, :])], "UA", "D DL", 360)
 
-    def late_constants():
-        put()
-        cp(T.parf[0:8, 0:7], T.pari[0:8, 0:7], "pari", "parf")
-        ts(T.gsel[0:8, :], T.gsel[0:8, :], 0.0, A.is_equal, "gsel", "gsel")
-        mm(T.PY[:, 0:7], [(T.gsel[0:8, :], T.parf[0:8, 0:7])], "gsel parf", "PY")
-        ts(T.wa[:], T.AI[:], 64.0, A.add, "AI AIL", "wa")
-        dma("ua", [(T.UA[row, 0:8960], T.wa[:])], "wa", "UA")
-        cp(T.pc[:, 0:7], T.PY[:, 0:7], "PY", "pc")
-        for b in range(4):
-            ts(T.Qh[:, 144 * b:144 * b + 144], T.yrow[:], pf[:, 13:14], A.is_equal, "yrow pf13 pn%d" % b, "Qh", pf[:, 18 + b:19 + b], A.mult)
-        cp(T.BOf[:], T.BOh[:], "BOh", "BOf")
-        ts(T.CL[:], T.Dc[:], 1089.0 + 512.5, A.is_ge, "Dc", "CL", 64.0, A.mult)
-        ts(T.CL[:], T.CL[:], 1024.0, A.add, "CL", "CL")
-        ts(T.thg[:], T.gam[:], 1024.0, A.is_ge, "gam", "thg", 8300.0, A.mult)
-        ts(T.thg[:], T.thg[:], -92.0, A.add, "thg", "thg")
-        ts(pf[:, 22:23], pf[:, 1:2], 68.0, A.mult, "pfa", "pf22", 8960.0, A.add)
-        ts(pf[:, 11:12], pf[:, 1:2], 128.0, A.mult, "pfa", "pf11", 8384.0, A.add)
-        ts(pf[:, 23:24], pf[:, 5:6], 128.0, A.mult, "pfa pf11", "pf23", pf[:, 11:12], A.add)
-        for c0, n in ((0, 68), (68, 68), (136, 40)):
-            ts(T.dumA[:, c0:c0 + n], T.yrow[:, 0:n], pf[:, 22:23], A.add, "yrow pf22", "dumA")
-        ts(T.dumV[:], T.dumA[:, 0:68], -768.0, A.add, "dumA", "dumV")
-        ts(T.dumB[:], T.yrow[:, 0:128], pf[:, 23:24], A.add, "yrow pf23", "dumB")
+    def prefetch(k, win, off, R):
+        move(T.VA[:, 1024 * k:1024 * k + 1024], (win, off), R, "W%d" % k)
 
-    lo, th, hi, K = (T.pc[:, k:k + 1] for k in range(4))
-    Pq = [T.P0, T.P1, T.P2, T.P3]
+    def sums(q, end):
+        mm(Pq[q][:], [one, (T.Ib[:], yv[0](512 * q, 512 * q + 512))], "cb0 cb1 Ib x0_%d" % q, "P%d" % q, True, False)
+        left = [4 if end else 5]
+        for j in range(4):
+            more(Pq[q][:], [(T.Ib[:], T.VA[:, 2048 * j + 512 * q:2048 * j + 512 * q + 512])], "Ib W%d" % (2 * j + q // 2), "P%d" % q, left)
+        return left
 
-    def read_plane(t):
-        dma("bt", [(T.BI[a:128:4, 0:128], T.BW[row, 512 * (4 * a + t):512 * (4 * a + t) + 512]) for a in range(4)], "BW", "Bt")
+    for k in (0, 2, 4, 6, 1, 3, 5, 7):
+        prefetch(k, T.xw0[:, PL:W0 - 16], pl(T.off, k // 2, 64 * (k % 2), 64 * (k % 2) + 64), "vac xl0 off " + xn(0))
+    for q in range(4):
+        sums(q, True)
 
-    def j_list(t):
-        ts(T.pj[:, 0:1], pf[:, 1:2], K, A.mult, "pfa pc", "pj0", T.pc[:, 4 + t:5 + t], A.add)
-        ts(T.pj[:, 1:2], T.pj[:, 0:1], 15, AND, "pj0", "pj1")
-        ts(T.pj[:, 2:3], T.pj[:, 0:1], 4, SH, "pj0", "pj2")
-        ts(T.col[:, 8:9], T.pj[:, 1:2], 512.0, A.mult, "pj1", "c8")
-        cp(T.col[:, 9:10], T.pj[:, 2:3], "pj2", "c9")
-        ts(T.deni[:], T.jio[:], K, A.mult, "jio pc c9", "deni", T.col[:, 9:10], A.add)
-        ts(T.deni[:], T.deni[:], 511, AND, "deni", "deni")
-        ts(T.joff[:], T.deni[:], T.col[:, 8:9], A.add, "deni c8", "joff")
+    def turn(out, on, ta, tan, tb, tbn, s1, o1):
+        ts(ta, (T.axoi[:], T.lpre[:]), s1, o1, "axoi lpre", tan)
+        record({"v": (1024 * CY, 0.0, lambda: v.transpose(tb, ta))}, tan, tbn)
+        move(out, (tb, T.lpost[:]), tbn + " lpost", on)
 
-    def floor16(q):
-        act(T.M[:, 512 * (q % 2):512 * (q % 2) + 512], Pq[q][:], F.Identity, "P%d" % q, "M rr%d" % (q % 2), bias=-7.5)
+    ts(pf[:, 22:23], pf[:, 1:2], 32.0, A.mult, "pfa", "pf22")
+    ts(T.lpost[:], T.yrow[:, 0:32], 32.0, A.mult, "yrow pfa", "lpost", pf[:, 5:6], A.add)
+    ts(T.lpre[:], T.f1[:, 0:64], pf[:, 22:23], A.add, "f1 pf22", "lpre")
+    turn(T.Eb[:], "Eb", T.AX[:, 64:1088], "AXa", T.AX[:, 1088:2112], "AXb", 64.0, A.add)
+    ts(T.Fb[:], T.Eb[:], 63.5, A.is_ge, "Eb", "Fb", 64.0, A.mult)
+    cp(T.j1[:, 0:1], pc[:, 3:4], "pc", "j1")
+    ts(T.f2[:, 0:16], T.yrow[:, 0:16], -1.0, A.mult, "yrow pfa", "f2", pf[:, 1:2], A.add)
+    ts(T.j1[:, 0:1], T.j1[:, 0:1], 15, AND, "j1", "j1")
+    cp(col[:, 23:24], T.j1[:, 0:1], "j1", "c23")
+    ts(T.f2[:, 0:16], T.f2[:, 0:16], col[:, 23:24], A.mult, "f2 c23", "f2", col[:, 23:24], A.mult)
+    ts(T.j1[:, 0:16], T.f2[:, 0:16], col[:, 23:24], A.mult, "f2 c23", "j1", 65536.0, A.add)
+    for b in range(4):
+        ts(T.j2[:, 16 * b:16 * b + 16], T.j1[:, 0:16], b, SH, "j1", "j2%d" % b, 1, AND)
+    for b in range(4):
+        ts(T.g2[:, 16 * b:16 * b + 16], T.j2[:, 16 * b:16 * b + 16], float(2 ** 2 ** b - 1), A.mult, "j20 j21 j2%d" % b, "g2", 1.0, A.add)
+    tt(T.g2[:, 0:32], T.g2[:, 0:32], T.g2[:, 32:64], A.mult, "g2", "g2")
+    tt(T.Ut[:], T.g2[:, 0:16], T.g2[:, 16:32], A.mult, "g2", "Ut")
+    ts(T.f3[:, 0:48], T.inv[:, 68:116], -1.0, A.mult, "invX", "f3", 1.0, A.add)
+    tt(T.f3[:, 0:48], T.f3[:, 0:48], T.i1[:, 0:48], A.mult, "f3 i1", "f3")
+    tt(T.f5[:, 0:48], T.inv[:, 68:116], T.dumK[:, 0:48], A.mult, "invX dumK", "f5")
+    tt(T.f3[:, 0:48], T.f3[:, 0:48], T.f5[:, 0:48], A.add, "f3 f5", "f3")
+    cp(T.oG[:, 0:48], T.f3[:, 0:48], "f3", "oG")
+    move((T.AX[:], T.oG[:, 0:48]), T.zer[:, 0:768], "oG zer", "AX AXl AXa AXb")
+    move(T.snd[:, 768:1536], T.AX[:, 8256:AXW:4], "AX", "msS")
+    iota(T.AX[:, 8256:AXW:4], [[0, 768]], 64, 0, "AX")
+    conv(T.PY[:, 0:48], T.Zq, lambda r: T.snd[:, 768 + r:1536:16], "Zq msS", "PY")
+    ts(T.held[:], T.PY[:, 0:48], 1.0, A.is_lt, "PY", "held")
+    dma([(T.AX[row, 64:8256], T.Eb[:]), (T.AX[row1, 64:8256], T.Fb[:])], "Eb Fb", "AX", 512)
+
+    lo, th, hi, K = pc[:, 8:9], pc[:, 9:10], pc[:, 10:11], pc[:, 3:4]
 
     def mod16(b, q):
-        tt(xw[b][:, 16 + 512 * q:528 + 512 * q], Pq[q][:], T.M[:, 512 * (q % 2):512 * (q % 2) + 512], A.subtract,
-           "P%d rr%d" % (q, q % 2), "x%d_%d" % (b, q))
-
-    def link_conv(bank):
-        conv(T[bank][:, 320:368], T.Z1f, lambda r: T.BW[:, 8192 + 2048 * (r % 4) + r // 4:8384 + 2048 * (r % 4):4], "Z1f BW", bank)
-
-    WALL = " ".join("W%d%d" % (j, h) for j in range(4) for h in range(2))
-    one = (T.cb[0:1, 640:768], T.cb[0:1, 0:512])
+        o = T.M[:, 512 * (q % 2):512 * (q % 2) + 512]
+        plus(o, Pq[q][:], -23.5, "P%d" % q, "rr%d" % (q % 2))
+        tt(yv[b](512 * q, 512 * q + 512), Pq[q][:], o, A.subtract, "P%d rr%d" % (q, q % 2), "x%d_%d" % (b, q))
 
     for t in range(RO):
         last = t == RO - 1
-        C = T.pc[:, 4 + t:5 + t]
-        win = "vac xl0 off " + xn(0)
-        for hq in range(2 if t == 0 else 0):
-            c0 = 1024 * hq
-
-            def o(j):
-                return T.xw0[:].indirect(T.off[:, 128 * j + 64 * hq:128 * j + 64 * hq + 64])
-            tt(T.V[:, c0:c0 + 1024], o(0), own(hq), A.add, win + " W%d1" % (2 + 2 * hq), "V0%d" % hq)
-            act(T.V[:, 4096 + c0:5120 + c0], o(2), F.Copy, win, "V2%d" % hq)
-            tt(T.V[:, 2048 + c0:3072 + c0], o(1), T.V[:, c0:c0 + 1024], A.add, win + " V0%d" % hq, "V1%d" % hq)
-            act(T.V[:, 6144 + c0:7168 + c0], o(3), F.Copy, win, "V3%d" % hq)
-            for k, j in enumerate((2, 1, 3)):
-                for q in (2 * hq, 2 * hq + 1):
-                    mm(Pq[q][:], [one] * (k == 0) + [(T.Ib[:], T.V[:, 2048 * j + 512 * q:2048 * j + 512 * q + 512])],
-                       "cb0 cb1 Ib V%d%d" % (j, hq), "P%d" % q, k == 0, k == 2)
+        C = pc[:, 4 + t:5 + t]
         for q in range(4):
-            if t > 0:
-                mm(Pq[q][:], [(T.Ib[:], T.VA[:, 2048 * j + 512 * q:2048 * j + 512 * q + 512]) for j in range(4)], "Ib " + WALL, "P%d" % q, False, True)
-                if q == 3:
-                    ts(T.off[:], T.tmpA[:], 0.25, A.mult, "tmpA tmpL", "off offL", -0.375, A.add)
-            floor16(q)
             mod16(1, q)
-        send_values(1)
+        if t == 0:
+            ts(T.oN[:], T.D[:, LK], 0.25, A.mult, "DL", "oN", -0.375, A.add)
+        move(T.snd[:, 0:768], (T.xw1[:, 0:2064], T.oN[:]), "oN vac1 " + xn(1), "snd")
+        exchange(T.snd, 0, T.xw1, 2064, 1, "snd", "xl1")
+        for hq in range(2):
+            copy3(own(1024 * hq, 1024 * hq + 1024), yv[1](1024 * hq, 1024 * hq + 1024), "x1_%d x1_%d" % (2 * hq, 2 * hq + 1), "yp%d yp%d" % (2 * hq, 2 * hq + 1))
         if t > 0:
-            act(T.BW[:].indirect(T.oG[:]), T.dT[:], F.Silu, "oG dT", "BW")
-            read_plane(t)
-        own_values(1, t > 0)
-        if t == 0:
-            late_constants()
-            read_plane(0)
-        else:
-            ts(T.AI[:], T.tmpA[:], -64.0, A.add, "tmpA tmpL", "AI AIL", -1.0, A.max)
-        ts(T.i1[:, 0:48], T.AI[:, 512:560], 3, AND, "AIL", "i1")
-        ts(T.loe[:], T.i1[:, 0:48], float(t), A.is_equal, "i1 pc", "loe", lo, A.mult)
-        lor, lsr = T["lor%d" % t], T["lsr%d" % t]
-        exchange(T.loe, lor, 0, 16, 1, "loe", "lor")
-        cp(T.Af[:], T.AI[:, 0:512], "AI", "Af")
-        act(T.vacm[:], T.Af[:], F.Relu, "Af", "vacm", scale=-67108864.0)
-        pos_b(T.AI[:, 512:560], "AIL", 48, T.dumB[:, 0:48], "dumB", T.pdL[:], "pdL")
-        j_list(t)
-        win = "vac xl1 off " + xn(1)
-
-        def keys(j, hq):
-            k = slice(128 * j + 64 * hq, 128 * j + 64 * hq + 64)
-            c0 = 2048 * j + 1024 * hq
-            conv(T.PK[:, k], T.Zk, lambda r: T.VA[:, c0 + r:c0 + 1024:16], "Zk If In Af vacm cb0 cb%d W%d%d" % (2 + j, j, hq), "PK",
-                 [(T.If[:], T.Af[:, k]), (T.In[:], T.vacm[:, k]), (T.cb[0:1, 0:128], T.cb[0:1, 768 + 128 * j:832 + 128 * j])])
-        for q in range(4):
-            mm(Pq[q][:], [one, (T.I4[:], T.xw1[:, 16 + 512 * q:528 + 512 * q])], "cb0 cb1 I4 x1_%d" % q, "P%d" % q, True, False)
-        if t == 0:
-            fin()
-        else:
-            link_conv("PY")
-
-        def fourth(hq):
-            act(T.V[:, 6144 + 1024 * hq:7168 + 1024 * hq], T.xw1[:].indirect(T.off[:, 384 + 64 * hq:448 + 64 * hq]), F.Copy, win, "V3%d" % hq)
-            for q in (2 * hq, 2 * hq + 1):
-                c = slice(6144 + 512 * q, 6656 + 512 * q)
-                bank = ("PS", "PX")[q % 2]
-                mm(T[bank][:], [(T.Ib[:], T.V[:, c]), (T.In[:], T.xw1[:, 16 + 512 * q:528 + 512 * q])], "Ib In V3%d x1_%d" % (hq, q), bank)
-                mm(Pq[q][:], [(T.Ib[:], T.V[:, c])], "Ib V3%d" % hq, "P%d" % q, False, False)
-
-        def fourth_keys(hq):
-            for q in (2 * hq, 2 * hq + 1):
-                bank = ("PS", "PX")[q % 2]
-                act(T.VA[:, 6144 + 512 * q:6656 + 512 * q], T[bank][:], F.Abs, bank, "W3%d" % hq)
-            keys(3, hq)
-        fourth(0)
-        for hq, j in ((0, 0), (0, 1), (0, 2), (1, 0), (1, 1), (1, 2)):
-            c0 = 1024 * hq
-            c = slice(2048 * j + c0, 2048 * j + c0 + 1024)
-            n = "%d%d" % (j, hq)
-            tt(T.V[:, c], T.xw1[:].indirect(T.off[:, 128 * j + 64 * hq:128 * j + 64 * hq + 64]), own(hq),
-               A.subtract, win + " W%d1" % (2 + 2 * hq), "V" + n)
-            for q in (2 * hq, 2 * hq + 1):
-                mm(Pq[q][:], [(T.Ib[:], T.V[:, 2048 * j + 512 * q:2048 * j + 512 * q + 512])], "Ib V" + n, "P%d" % q, False, j == 2)
-            if (hq, j) == (1, 2):
-                break
-            act(T.VA[:, c], T.V[:, c], F.Abs, "V" + n, "W" + n)
-            keys(j, hq)
-            if (hq, j) == (0, 0):
-                fourth_keys(0)
-            if (hq, j) == (0, 2):
-                fourth(1)
-            if (hq, j) == (1, 0):
-                fourth_keys(1)
-            if (hq, j) == (1, 1):
-                floor16(0)
-                floor16(1)
-        if t == 0:
-            cp(T.BI[:, 128:176], T.PY[:, 0:48], "PY", "IE")
-        else:
-            tt(T.f5[:, 0:48], T.PY[:, 320:368], T.held[:], A.mult, "PY held", "f5")
-            tt(T.BI[:, 128:176], T.f5[:, 0:48], T.IEp[:], A.add, "f5 IEp", "IE")
-        ts(T.i1[:], T.BI[:], -64.0, A.add, "Bt IE", "i1")
-        pos_a(T.i1[:], "i1", 176, T.pdA[:], "pdA")
-        ts(T.f5[:], T.BI[:], 63.5, A.is_ge, "Bt IE", "f5")
-        tt(T.pdA[:], T.pdA[:], T.f5[:], A.mult, "pdA f5", "pdA")
-        cp(T.held[:], T.f5[:, 128:176], "f5", "held")
-        for q in range(4):
-            if q >= 2:
-                floor16(q)
-            mod16(0, q)
-            mm(T.PS[:, 128:256], [(T.Zb[:, 15 - r:143 - r], T.xw0[:, 16 + 512 * q + r % 4:528 + 512 * q:4]) for r in range(4 * q, 4 * q + 4)],
-               "Zb x0_%d" % q, "PS", q == 0, q == 3)
-        act(T.VA[:, 5120:6144], T.V[:, 5120:6144], F.Abs, "V21", "W21")
-        act(T.kh[:], T.PK[:, 0:256], F.Copy, "PK", "kh")
-        keys(2, 1)
-        conv(T.PY[:, 256:384], T.Zb, lambda r: T.xw0[:, 16 + r:2064:16], "Zb " + xn(0), "PY")
-        send_values(0)
-        ts(T.f5[:, 0:128], T.PS[:, 128:256], lo, A.is_ge, "PS pc", "f5")
-        ts(T.f3[:, 0:128], T.PS[:, 128:256], lo, A.is_lt, "PS pc", "f3")
-        tt(T.Bn[:], T.BI[:, 0:128], T.f5[:, 0:128], A.mult, "Bt f5", "Bn")
-        dma("bn", [(T.BW[row, 512 * (4 * a + t):512 * (4 * a + t) + 512], T.Bn[a:128:4, :]) for a in range(4)], "Bn", "BW")
+            ts(T.off[:, 0:656], T.D[:, 0:656], 0.25, A.mult, "D DL", "off", -0.375, A.add)
+            move((T.AX[:], T.oG[:]), T.dT[:], "oG dT", "AX")
+        either(TS(T.vacm[:], T.D[:], 63.5, A.is_lt, 1e9, A.mult), ACT(T.vacm[:], T.D[:], F.Relu, scale=-134217728.0, bias=8522825728.0), "D DL", "vacm")
+        ts(T.AI[:, 0:656], T.D[:, 0:656], -64.0, A.add, "D DL", "AI")
+        ts(T.AI[:, 0:656], T.AI[:, 0:656], 8195, AND, "AI", "AI")
+        ts(T.isT[:, 0:656], T.AI[:, 0:656], float(t), A.is_equal, "AI", "isT", -8256.0, A.mult)
+        ts(T.i1[:, 0:48], T.D[:, LK], -64.0, A.add, "DL", "i1")
+        ts(T.i1[:, 0:48], T.i1[:, 0:48], 8195, AND, "i1", "i1")
+        ts(T.f5[:, 0:48], T.i1[:, 0:48], float(t), A.is_equal, "i1", "f5", -8256.0, A.mult)
+        tt(T.f5[:, 0:48], T.D[:, LK], T.f5[:, 0:48], A.add, "DL f5", "f5")
+        ts(T.oN[:], T.f5[:, 0:48], 0.25, A.mult, "f5", "oN", 2063.625, A.add)
+        ts(T.f5[:, 0:48], T.D[:, LK], 63.5, A.is_lt, "DL", "f5")
+        tt(T.f5[:, 0:48], T.f5[:, 0:48], T.dumK[:, 0:48], A.mult, "f5 dumK", "f5")
+        tt(T.f5[:, 0:48], T.f5[:, 0:48], T.D[:, LK], A.max, "f5 DL", "f5")
+        cp(T.oL[:], T.f5[:, 0:48], "f5", "oL")
+        ts(T.j1[:, 0:32], T.gam[:, 0:32], K, A.mult, "gam pc", "j1", C, A.add)
+        ts(T.j2[:, 0:32], T.j1[:, 0:32], 511, AND, "j1", "j20")
+        ts(T.j2[:, 32:64], T.j1[:, 0:32], 9, SH, "j1", "j21", 15, AND)
+        cp(T.oJ[:], T.j2[:, 0:64], "j20 j21", "oJ")
+        move(T.TG[:, 0:512], (T.Ut[:], T.oJ[:, 32:64]), "Ut oJ", "Tt")
         if last:
-            dma("yx", [(T.yx[:], T.xw0[:, 16:2064])], xn(0), "")
-        pick(T.oA[:, 0:128], "oA", T.pdA[:, 0:128], "pdA", T.f3[:, 0:128], "f3", T.dumA[:, 0:128], "dumA", 128)
+            iota(T.dG[:, 0:768], [[4, 768]], 8256 - 64, 0, "dG")
+            ts(col[:, 18:19], pf[:, 7:8], 1.0 / 64, A.mult, "pf7", "c18")
+            either(TS(T.dT[:, 0:768], T.dG[:, 0:768], col[:, 18:19], A.mult, 1.0, A.add),
+                   ACT(T.dT[:, 0:768], T.dG[:, 0:768], F.Identity, scale=col[:, 18:19], bias=1.0), "dG c18", "dT")
+        win = "vac1 xl1 off " + xn(1)
+        for q in range(4):
+            mm(Pq[q][:], [one, (T.I4[:], yv[1](512 * q, 512 * q + 512))], "cb0 cb1 I4 x1_%d" % q, "P%d" % q, True, False)
+        mms([(T.PK[:], T.cb[0:1, 640:768], T.cb[0:1, 0:512], True, False)] +
+            [(T.PK[:, 128 * j:128 * j + 128], l, r, False, False) for j in range(4)
+             for l, r in ((T.cb[0:1, 768:896], T.cb[0:1, 0:128]),) * j + ((T.If[:], pl(T.D, j)), (T.In[:], pl(T.vacm, j)))], "If In D vacm cb0 cb2", "PK")
+        clear("PY", 256)
+        left, kl, sl = [[4] for q in range(4)], [8], [6]
+        for hq in range(2):
+            for j in (3, 0, 1, 2):
+                c0, mode, vn, wn = 2048 * j + 1024 * hq, MODE[j, hq], "V%d%d" % (j, hq), "W%d" % (2 * j + hq)
+                src = (T.xw1[:], pl(T.off, j, 64 * hq, 64 * hq + 64))
+                if mode == "s":
+                    act(T.V[:, c0:c0 + 1024], src, F.Copy, win, vn)
+                else:
+                    tt(T.V[:, c0:c0 + 1024], src, own(1024 * hq, 1024 * hq + 1024), A.subtract, win + " yp%d yp%d" % (2 * hq, 2 * hq + 1), vn)
+                for k in range(2):
+                    q, c = 2 * hq + k, slice(c0 + 512 * k, c0 + 512 * k + 512)
+                    more(Pq[q][:], [(T.Ib[:], T.V[:, c])], "Ib " + vn, "P%d" % q, left[q])
+                    if mode == "s":
+                        bank = ("PS", "PX")[k]
+                        mm(T[bank][:], [(T.Ib[:], T.V[:, c]), (T.In[:], yv[1](512 * q, 512 * q + 512))], "Ib In x1_%d " % q + vn, bank)
+                        act(T.VA[:, c], T[bank][:], F.Abs, bank, wn)
+                if mode == "va":
+                    act(T.VA[:, c0:c0 + 1024], T.V[:, c0:c0 + 1024], F.Abs, vn, wn)
+                if mode == "vr":
+                    ts(T.VA[:, c0:c0 + 1024], T.V[:, c0:c0 + 1024], 0.0, A.max, vn, wn)
+                k = T.PK[:, 128 * j + 64 * hq:128 * j + 64 * hq + 64]
+                more(k, (terms(T.Zn, lambda r: T.V[:, c0 + r:c0 + 1024:16]) if mode == "vr" else []) +
+                     terms(T.Zr if mode == "vr" else T.Zk, lambda r: T.VA[:, c0 + r:c0 + 1024:16]), "Zk Zr Zn %s %s" % (vn, wn), "PK", kl)
+            for q in (2 * hq, 2 * hq + 1):
+                mod16(0, q)
+                more(T.PY[:, 128:256], [(T.Zb[:, 15 - r:143 - r], yv[0](128 * r, 128 * r + 128)) for r in range(4 * q, 4 * q + 4)], "Zb x0_%d" % q, "PY", sl)
+            more(T.PY[:, 64 * hq:64 * hq + 64], terms(T.Zb, lambda r: yv[0](1024 * hq + r, 1024 * hq + 1024, 16)), "Zb x0_%d x0_%d" % (2 * hq, 2 * hq + 1), "PY", sl)
+        ts(T.lostB[:], T.PY[:, 128:256], lo, A.is_lt, "PY pc2", "lostB")
+        ts(T.keepB[:], T.PY[:, 128:256], lo, A.is_ge, "PY pc2", "keepB", 64.0, A.mult)
+        for q in range(4):
+            mms([(Pq[q][:], T.Ib[:], yv[0](512 * q, 512 * q + 512), True, False)] +
+                [(Pq[q][:, 128 * c:128 * c + 128], T.RV[:, 128 * (4 * q + c):128 * (4 * q + c) + 128], T.lostB[:], False, c == 3) for c in range(4)],
+                "Ib RV lostB x0_%d" % q, "P%d" % q)
+            o = own(512 * q, 512 * q + 512)
+            either(TS(o, Pq[q][:], 0.0, A.max), ACT(o, Pq[q][:], F.Relu), "P%d" % q, "yp%d" % q)
+        move(T.snd[:, 0:768], (T.xw0[:, 0:Y0 + 2048], T.oN[:]), "oN vac " + YP + " " + xn(0), "snd")
+        exchange(T.snd, 0, T.xw0, Y0 + 2048, 1, "snd", "xl0")
+        move(T.f1[:], T.PK[:, 0:256], "PK", "f1")
+        tt(T.km[:], T.PK[:, 256:512], T.f1[:], A.max, "PK f1", "km")
+        ts(T.hiF[:], T.PY[:, 0:128], hi, A.is_ge, "PY pc2", "hiF")
+        ts(T.thr[:], T.PY[:, 0:128], th, A.is_lt, "PY pc2", "thr", 63.5, A.mult)
+        tt(T.km[:, 0:128], T.km[:, 0:128], T.km[:, 128:256], A.max, "km", "km")
+        tt(T.mg[:], T.km[:, 0:128], T.hiF[:], A.mult, "km hiF", "mg")
+        tt(T.i1[:, 0:128], T.mg[:], T.dumK[:, 0:128], A.max, "mg dumK", "i1")
+        ts(T.i1[:, 0:128], T.i1[:, 0:128], 16383, AND, "i1", "i1")
+        cp(T.oK[:], T.i1[:, 0:128], "i1", "oK")
         for k in range(2):
-            act(T.UA[:].indirect(T.oA[:, 64 * k:64 * k + 64]), T.zer[:, 0:1024], F.Silu, "oA zer", "UA")
-        tt(T.km[:], T.PK[:, 256:512], T.kh[:], A.max, "PK kh", "km")
-        ts(T.f5[:, 0:128], T.PY[:, 256:384], hi, A.is_ge, "PY pc", "f5")
-        tt(T.mx[:], T.km[:, 0:128], T.km[:, 128:256], A.max, "km", "mx")
-        cp(T.i1[:, 0:128], T.mx[:], "mx", "i1")
-        ts(T.mx[:], T.mx[:], 0.0, A.max, "mx", "mx")
-        pos_b(T.i1[:, 0:128], "i1", 128, T.dumB[:], "dumB", T.pdK[:], "pdK")
-        tt(T.mg[:], T.mx[:], T.f5[:, 0:128], A.mult, "mx f5", "mg")
-        ts(T.f5[:, 0:128], T.mg[:], 0.0, A.is_gt, "mg", "f5")
-        pick(T.oK[:], "oK", T.pdK[:], "pdK", T.f5[:, 0:128], "f5", T.dumB[:], "dumB", 128)
-        conv(T.PS[:, 256:304], T.Zb, lambda r: T.xw0[:, 2064 + r:XW:16], "Zb xl0", "PS")
-        cp(T.BW[:].indirect(T.oK[:, 0:64]), T.zer[:, 0:1024], "oK zer", "BW Bg0 Bg1 BL")
-        tt(T.alive[:], T.PS[:, 256:304], lor[:], A.is_ge, "PS lor", "alive")
-        ts(T.f5[:, 0:48], T.alive[:], 0.0, A.is_equal, "alive", "f5")
-        pick(T.oA[:, 128:176], "oA2", T.pdA[:, 128:176], "pdA", T.f5[:, 0:48], "f5", T.dumA[:, 128:176], "dumA", 48)
-        act(T.UA[:].indirect(T.oA[:, 128:176]), T.zer[:, 0:768], F.Silu, "oA2 zer", "UA")
-        dma("uar", [(T.tmpA[:], T.UA[row, 0:8960])], "UA", "tmpA tmpL")
-        cp(T.BW[:].indirect(T.oK[:, 64:128]), T.zer[:, 0:1024], "oK zer", "BW")
-        link_conv("PS")
-        ts(T.thr[:], T.PY[:, 256:384], th, A.is_lt, "PY pc", "thr", 63.5, A.mult)
+            move((T.AX[:], T.oK[:, 64 * k:64 * k + 64]), T.zer[:], "oK zer", "AX")
         for j in range(4):
-            tt(T.wb[:, 128 * j:128 * j + 128], T.PK[:, 128 * j:128 * j + 128], T.mg[:], A.not_equal, "PK mg", "wb")
+            tt(T.TG[:, 512 + 128 * j:640 + 128 * j], T.PK[:, 128 * j:128 * j + 128], T.mg[:], A.is_equal, "PK mg Gj", "lost%d" % j)
+            mm(T.PX[:, 128 * j:128 * j + 128], [(T.If[:], pl(T.D, j)), (T.Ib[:], pl(T.isT, j)), (T.Ig[:], T.TG[:, 512 + 128 * j:640 + 128 * j])],
+               "If Ib Ig D isT lost%d" % j, "PX")
+        ts(T.ofp[:], T.PX[:], 0.25, A.mult, "PX", "ofp", 2063.625, A.add)
+        if last:
+            plus(T.V[:, 0:2048], yv[0](0, 2048), -16.0, xn(0), "V00 V01")
+            dma([(T.yx[:], T.V[:, 0:2048])], "V00 V01", "", 512)
+        move(T.snd[:, 768:1536], T.AX[:, 8256:AXW:4], "AX", "msS")
+        exchange(T.snd, 768, T.msR, 0, -1, "msS", "msR")
+        if not last:
+            iota(T.AX[:, 8256:AXW:4], [[0, 768]], 64, 0, "AX")
+        clear("PS", 512)
+        left = [8]
+        for k in range(8):
+            prefetch(k, T.xw0[:], T.ofp[:, 64 * k:64 * k + 64], "vac xl0 ofp " + YP + " " + xn(0))
+            more(T.PS[:, 64 * k:64 * k + 64], terms(T.Zq, lambda r: T.VA[:, 1024 * k + r:1024 * k + 1024:16]), "Zq W%d" % k, "PS", left)
+        conv(T.PY[:, 0:48], T.Zq, lambda r: T.snd[:, r:768:16], "Zq snd", "PY")
+        tt(T.D[:, LK], T.PY[:, 0:48], T.D[:, LK], A.min, "PY DL", "DL")
+        conv(T.PY[:, 48:96], T.Zq, lambda r: T.xw0[:, Y0 + 2048 + r:Y0 + 2816:16], "Zq xl0", "PY")
+        ts(T.alive[:], T.PY[:, 48:96], 1.0, A.is_ge, "PY", "alive")
         tt(T.flG[:, 0:48], T.alive[:], T.held[:], A.is_gt, "alive held", "flG0")
-        op("v", lambda: v.tensor_reduce(T.col[:, 0:1], T.flG[:, 0:48], AxisListType.X, A.add), "flG0", "c0")
-        mm(T.PY[:, 0:1], [(T.BOf[:], T.col[:, 0:1])], "BOf c0", "PY")
-        ts(T.f5[:, 0:48], T.PS[:, 320:368], 63.5, A.is_lt, "PS", "f5")
-        tt(T.msg[:], T.f5[:, 0:48], T.held[:], A.mult, "f5 held", "msg")
-        exchange(T.msg, lsr, 0, 16, -1, "msg", "lsr")
+        scan(T.cumG[:, 1:49], T.flG[:, 0:48], T.flG[:, 0:48], 0.0, A.add, A.max, "flG0", "cumGa cumG")
+        mm(T.PY[:, 0:48], [(T.BOh[:], T.cumG[:, 0:48]), (T.TRI[:], T.flG[:, 0:48])], "BOh TRI cumG0 cumGa flG0", "PY")
+        mm(T.PY[:, 48:49], [(T.BOh[:], T.cumG[:, 48:49])], "BOh cumGa", "PY")
+        cp(T.g1[:, 0:49], T.PY[:, 0:49], "PY", "g1")
+        nL = T.g1[:, 48:49]
         if not last:
-            tt(T.f5[:, 0:48], T.alive[:], T.msg[:], A.is_gt, "alive msg", "f5")
-            tt(T.f5[:, 0:48], T.f5[:, 0:48], T.held[:], A.mult, "held f5", "f5")
-            tt(T.IEp[:], T.BI[:, 128:176], T.f5[:, 0:48], A.mult, "IE f5", "IEp")
-        cp(T.col[:, 1:2], T.PY[:, 0:1], "PY", "c1")
-        tt(T.tmpA[:, 0:512], T.tmpA[:, 0:512], T.wb[:, 0:512], A.mult, "tmpA wb", "tmpA")
-        for j in range(4):
-            tt(T.flE[:, 128 * j:128 * j + 128], T.tmpA[:, 128 * j:128 * j + 128], T.thr[:], A.is_lt, "tmpA thr", "Eh flP%d" % j)
+            conv(T.PY[:, 0:48], T.Zq, lambda r: T.snd[:, 768 + r:1536:16], "Zq msS", "PY")
+            tt(T.held[:], T.alive[:], T.held[:], A.mult, "alive held", "held")
+            tt(T.held[:], T.PY[:, 0:48], T.held[:], A.min, "PY held", "held")
+        if last:
+            move(T.dG[:, 0:768], T.msR[:], "msR", "dG")
+            tt((T.AX[:], T.oL[:]), T.dG[:, 0:768], T.dT[:, 0:768], A.mult, "oL dG dT", "AX")
+        else:
+            cp((T.AX[:], T.oL[:]), T.msR[:], "oL msR", "AX")
+        dma([(T.Fb[:], T.AX[row1, 64:8256])], "AX", "Fb", 256)
+        if last:
+            dma([(T.Eb[:], T.AX[row, 64:8256])], "AX", "Eb", 512)
+        conv(T.PY[:, 0:48], T.Zq, lambda r: T.msR[:, r:768:16], "Zq msR", "PY")
+        tt(T.D[:, LK], T.PY[:, 0:48], T.D[:, LK], A.min, "PY DL", "DL")
+        if not last:
+            ts(T.oN[:], T.D[:, LK], 0.25, A.mult, "DL", "oN", -0.375, A.add)
+        ts(T.isL[:], T.gam[:], nL, A.is_lt, "gam gam2 g1", "isL")
+        ts(T.flE[:, 128:144], T.D[:, 128 + 16 * t:144 + 16 * t], 63.5, A.is_lt, "DL flE", "flEL")
+        mms([(T.P1[:, b:64:4], T.Qh[:, 144 * b + 3:144 * b + 131], T.flE[:, 128:144], True, True) for b in range(4)], "Qh flEL", "P1")
+        cp(T.flT[:, 528:592], T.P1[:, 0:64], "P1", "flT2")
+        tt(T.Fb[:, t:512:4], T.Fb[:, t:512:4], T.keepB[:], A.min, "Fb keepB", "Fb")
+        tt(T.TG[:, 512:1024], (T.Fb[:], T.oJ[:, 0:32]), T.TG[:, 0:512], A.mult, "Fb oJ Tt", "Gj lost0 lost1 lost2 lost3")
+        if not last:
+            dma([(T.AX[row1, 64:8256], T.Fb[:])], "Fb", "AX", 256)
+        conv(T.PK[:, 0:32], T.Zb, lambda r: T.TG[:, 512 + r:1024:16], "Zb Gj", "PK")
+        ts(T.j1[:, 0:32], T.PK[:, 0:32], -1.0 / 64, A.mult, "PK", "j1", 65535.0, A.add)
         for b in range(4):
-            mm(T.P2[:, b:512:4], [(T.Qh[:, 144 * b + 3 - j:144 * b + 131 - j], T.flE[:, 128 * j:128 * j + 128]) for j in range(4)],
-               "Qh Eh flP0 flP1 flP2 flP3", "P2")
-        pick(T.oL[:], "oL", T.pdL[:], "pdL", lsr[:], "lsr", T.dumB[:, 0:48], "dumB", 48)
-        act(T.BW[:].indirect(T.oL[:]), T.zer[:, 0:768], F.Silu, "oL zer", "BW")
-
-        def jchunk(k, eng):
-            c = slice(1024 * k, 1024 * k + 1024)
-            n = "V%d%d" % (k // 2, k % 2)
-            src = T.BW[:, 0:8192].indirect(T.joff[:, 64 * k:64 * k + 64])
-            if eng == "s":
-                act(T.V[:, c], src, F.Sign, "BW joff", n, scale=-1.0, bias=63.5)
-            else:
-                ts(T.V[:, c], src, 63.5, A.is_lt, "BW joff", n)
-            return lambda: conv(T.P3[:, 64 * k:64 * k + 64], T.Z1b, lambda r: T.V[:, 1024 * k + r:1024 * k + 1024:16], "Z1b " + n, "P3")
-        jc = [jchunk(k, "s") for k in range(NS)]
-        if last:
-            dma("bw", [(T.wb[:, 0:512], T.BW[row, 0:8192])], "BW", "wb")
-        ts(T.f5[:, 0:48], lsr[:], -1.0, A.mult, "lsr", "f5", 1.0, A.add)
-        tt(T.tmpA[:, 512:560], T.tmpA[:, 512:560], T.f5[:, 0:48], A.mult, "tmpL f5", "tmpL")
-        ts(T.flT[:, 513:529], T.tmpA[:, 512 + 16 * t:528 + 16 * t], 63.5, A.is_lt, "tmpL", "flT1")
+            ts(T.j2[:, 32 * b:32 * b + 32], T.j1[:, 0:32], b, SH, "j1", "j2%d" % b, 0x1111, AND)
+        for k in range(4):
+            ts(T.AI[:, 128 * k:128 * k + 128], T.j2[:, 0:128], 4 * k, SH, "j20 j21 j22 j23 isT", "AI%d" % k, 1, AND)
+        cp(T.flG[:, 48:560], T.AI[:, 0:512], "AI0 AI1 AI2 AI3", "flG1 AI")
+        scan(T.cumG[:, 49:561], T.flG[:, 48:560], T.flG[:, 48:560], T.cumG[:, 48:49], A.add, A.max, "flG1 cumGa", "cumG")
+        heads(T.cumG, "cumG cumG0 cumGa", 560, None, T.seb, "seb", T.ob, "ob", "PK")
+        counts(T.flG, "flG0 flG1", 560, 512, T.wb, "wb", "P2", "P3")
+        move((T.Lb[:], T.ob[:, 0:35]), T.wb[:, 0:560], "ob wb wb1", "Lb")
+        mm(T.PK[:, 256:257], [(T.BOh[:], T.cumG[:, 560:561])], "BOh cumG", "PK")
+        cp(col[:, 5:6], T.PK[:, 256:257], "PK", "c5")
+        run_down(T.Lb, "Lb", T.cwb, "cwb", 0, 1088, 64.0)
+        ts(T.cwb[:], T.cwb[:], pf[:, 10:11], A.min, "cwb pf10", "cwb")
+        back = [(T.cb[0:1, 0:128], T.cb[0:1, 896:964])]
+        mm(T.PK[:, 64:132], back + terms(T.Zc, lambda r: T.cwb[:, r:1088:16]), "cb0 cb6 Zc cwb", "PK")
+        mm(T.PK[:, 132:200], back + terms(T.Zc, lambda r: T.cwb[:, 68 * r:68 * r + 68]), "cb0 cb6 Zc cwb", "PK")
+        for j in range(4):
+            tt(T.flE[:, 144 * j:144 * j + 128], T.PS[:, 128 * j:128 * j + 128], T.thr[:], A.is_lt, "PS thr flE", "flP%d" % j)
+        for j in range(4):
+            tt(pl(T.D, j), T.PS[:, 128 * j:128 * j + 128], pl(T.D, j), A.min, "PS D", "D")
+        FP = "flP0 flP1 flP2 flP3"
+        for b in range(4):
+            mm(T.P0[:, b:512:4], [(T.Qh[:, 144 * b + 3 - j:144 * b + 131 - j], T.flE[:, 144 * j:144 * j + 128]) for j in range(4)], "Qh " + FP, "P0")
+        cp(T.flT[:, 0:512], T.P0[:], "P0", "flT0")
+        scan(T.cumT[:, 1:513], T.flT[:, 0:512], T.flT[:, 0:512], 0.0, A.add, A.max, "flT0", "cumT")
+        mm(T.PY[:, 0:1], [(T.BOh[:], T.cumT[:, 512:513])], "BOh cumT", "PY")
+        ts(col[:, 1:2], T.PY[:, 0:1], 1024.0, A.min, "PY g1", "c1", nL, A.max)
+        ts(col[:, 0:1], T.PY[:, 0:1], 1024.0, A.min, "PY", "c0")
+        ts(col[:, 4:5], T.PY[:, 0:1], 1024.0, A.is_le, "PY", "c4")
+        ts(col[:, 3:4], col[:, 1:2], pf[:, 7:8], A.mult, "c1 pf7", "c3")
+        scan(T.cumT[:, 513:593], T.flT[:, 512:592], T.flT[:, 512:592], col[:, 3:4], A.add, A.max, "flT1 flT2 c3", "cumTa")
+        heads(T.cumT, "cumT cumT0 cumTa", 592, T.CL[:, 0:74], T.sea, "sea", T.oa, "oa", "PX")
+        counts(T.flT, "flT0 flT1 flT2", 592, 496 + 64 * t, T.wa, "wa", "P0", "P1")
+        move((T.La[:], T.oa[:, 0:37]), T.wa[:, 0:592], "oa wa wa1", "La")
+        mm(T.PY[:, 0:1], [(T.BOh[:], T.cumT[:, 592:593])], "BOh cumTa", "PY")
+        ts(col[:, 6:7], col[:, 1:2], 64.0, A.add, "c1", "c6")
+        ts(col[:, 2:3], T.PY[:, 0:1], col[:, 6:7], A.min, "PY c6", "c2")
+        ts(col[:, 8:11], col[:, 0:3], col[:, 5:6], A.min, "c0 c1 c2 c5", "c8")
+        run_down(T.La, "La", T.cwa, "cwa", 0, 1024, 64.0)
+        ts(col[:, 7:8], T.cwa[:, 1023:1024], col[:, 4:5], A.mult, "cwa c4", "c7")
+        run_down(T.La, "La", T.cwa, "cwa1", 1024, 1088, col[:, 7:8], "c7")
+        ts(T.cwa[:], T.cwa[:], pf[:, 10:11], A.min, "cwa cwa1 pf10", "cwa cwa1")
+        ts(T.j1[:], T.PK[:, 64:200], K, A.mult, "PK pc", "j1", C, A.add)
         if not last:
-            dma("ua", [(T.UA[row, 0:8960], T.tmpA[:])], "tmpA tmpL", "UA")
-        cp(T.flT[:, 0:512], T.P2[:], "P2", "flT0")
-        scan(T.flT, "flT0", 0, 512, 0.0)
-        mm(T.PY[:, 0:1], [(T.BOh[:], T.cum[:, 512:513])], "BOh cum", "PY")
-        if last:
-            ts(T.AI[:, 0:512], T.tmpA[:, 0:512], -64.0, A.add, "tmpA", "AI", -1.0, A.max)
-            cp(T.Pf[:], T.Qh[:], "Qh", "Pf")
-            cp(T.Af[:], T.AI[:, 0:512], "AI", "Af")
-        else:
-            ts(T.off[:, 0:512], T.tmpA[:, 0:512], 0.25, A.mult, "tmpA", "off", -0.375, A.add)
-        ts(T.col[:, 2:3], T.PY[:, 0:1], 1024.0, A.min, "PY c1", "c2", T.col[:, 1:2], A.max)
-        ts(T.col[:, 3:4], T.PY[:, 0:1], 1024.0, A.min, "PY", "c3")
-        ts(T.col[:, 4:5], T.col[:, 2:3], pf[:, 7:8], A.mult, "c2 pf7", "c4")
-        ts(T.col[:, 5:6], T.col[:, 2:3], 64.0, A.add, "c2", "c5")
-        cp(T.cum[:, 513:514], T.col[:, 4:5], "c4", "cum")
-        scan(T.flT, "flT1", 513, 560, T.col[:, 4:5], "c4")
-        nat = [lambda b=b: mm(T.P2[:, b:512:4], [(T.Pf[:, 144 * b + 3 - j:144 * b + 131 - j], T.Af[:, 128 * j:128 * j + 128]) for j in range(4)],
-                              "Pf Af", "P2") for b in range(4) if last]
-        compact(T.flT, "flT0 flT1", 68, True, nat[0:3], jc[0:1], jc[1:2] + nat[3:])
-        run(jc[2:NS - 1])
-        cp(T.nn[:, 68:136], T.PY[:, 128:196], "PY", "nn1")
-        tt(T.nn[:, 0:68], T.PX[:, 192:260], T.cf[:], A.add, "PX cf", "nn0")
-        ts(T.vT[:], T.PX[:, 192:260], 16.0, A.is_ge, "PX", "vT")
-        ts(T.f1[:, 0:136], T.nn[:], 3.0, A.mult, "nn0 nn1", "f1", float(8192 + 1024 * t - 64 * 513), A.add)
-        ts(T.f2[:, 0:136], T.nn[:], 8208.0, A.is_ge, "nn0 nn1", "f2")
-        tt(T.f3[:, 0:68], T.nn[:, 0:68], T.thg[:], A.is_ge, "nn0 thg", "f3")
-        tt(T.f1[:, 0:136], T.f1[:, 0:136], T.f2[:, 0:136], A.mult, "f1 f2", "f1")
-        ts(T.f4[:, 0:68], T.gam[:], T.col[:, 5:6], A.is_lt, "gam c5", "f4")
-        tt(T.vT[:], T.vT[:], T.f3[:, 0:68], A.mult, "vT f3", "vT")
-        tt(T.valT[:], T.f1[:, 0:136], T.nn[:], A.add, "f1 nn0 nn1", "valT")
-        tt(T.vT[:], T.vT[:], T.f4[:, 0:68], A.mult, "vT f4", "vT")
-        if not last:
-            ts(T.valT[:, 68:136], T.valT[:, 68:136], 64.0, A.add, "valT", "valT")
-        dma("dT", [(T.dT[row, :], T.valT[:, 68:136])], "valT", "dT")
-        cp(T.i1[:, 0:68], T.valT[:, 0:68], "valT", "i1")
-        if last:
-            pos_b(T.i1[:, 0:68], "i1", 68, T.dumA[:, 0:68], "dumA", T.pdT[:], "pdT")
-            ts(T.f3[:, 0:68], T.valT[:, 0:68], 8192.0, A.is_lt, "valT", "f3")
-            tt(T.pdT[:], T.pdT[:], T.f3[:, 0:68], A.mult, "pdT f3", "pdT")
-        else:
-            pos_a(T.i1[:, 0:68], "i1", 68, T.pdT[:], "pdT")
-            ts(T.i2[:, 0:68], T.i1[:, 0:68], 2, SH, "i1", "i2")
-            ts(T.f1[:, 0:68], T.i3[:, 0:68], 2048.0, A.mult, "i3", "f1")
-            tt(T.f2[:, 0:68], T.i2[:, 0:68], T.dumV[:], A.subtract, "i2 dumV", "f2")
-            ts(T.f3[:, 0:68], T.valT[:, 0:68], 8192.0, A.is_lt, "valT", "f3")
-            tt(T.f1[:, 0:68], T.f1[:, 0:68], T.f2[:, 0:68], A.add, "f1 f2", "f1")
-            tt(T.pdV[:], T.f1[:, 0:68], T.f3[:, 0:68], A.mult, "f1 f3", "pdV")
-        jc += [jchunk(k, "v") for k in range(NS, 8)]
-        run(jc[NS - 1:])
-        clear_l1()
-        if not last:
-            for k in range(8):
-                act(T.VA[:, 1024 * k:1024 * k + 1024], T.xw0[:].indirect(T.off[:, 64 * k:64 * k + 64]), F.Copy,
-                    "vac xl0 off " + xn(0), "W%d%d" % (k // 2, k % 2))
-        ts(T.flG[:, 48:560], T.P3[:], 0.0, A.max, "P3", "flG1")
-        scan(T.flG, "flG0 flG1", 0, 560, 0.0)
-
-        def to_natural():
-            act(T.wa[:, 0:512], T.P2[:], F.Copy, "P2", "wa")
-            dma("ua", [(T.UA[row, 0:8192], T.wa[:, 0:512])], "wa", "UA")
-
-        def plain_entries():
-            ts(T.deni[:], T.wb[:, 0:512], -64.0, A.add, "wb", "deni", -1.0, A.max)
-            cp(T.wb[:, 0:512], T.deni[:], "deni", "wb")
-            dma("bw2", [(T.BW[row, 0:8192], T.wb[:, 0:512])], "wb", "BW")
-        compact(T.flG, "flG0 flG1", 68, False, [to_natural] if last else (), (), [plain_entries] if last else ())
-        if not last:
+            dma([(T.UA[row, :], T.D[:])], "D DL", "UA", 360)
+            iota(T.Lb[:, 0:1088], [[0, 1088]], 64, 0, "Lb")
+            iota(T.La[:, 0:1088], [[0, 1088]], 64, 0, "La")
+            for k, TR in enumerate((T.TRI, T.TRs)):
+                mm(T.PY[:, 128 + 128 * k:256 + 128 * k], [(T.BOh[:], T.cumT[:, 0:512:4])] +
+                   [(TR[:], T.flE[:, 144 * j:144 * j + 128]) for j in range(4)], "BOh TRI TRs cumT cumT0 " + FP, "PY")
+            ts(T.f1[:], T.PY[:, 128:384], 1024.0, A.min, "PY", "f1")
+            tt(T.f3[:, 0:128], T.f1[:, 0:128], T.f1[:, 128:256], A.is_gt, "f1", "f3")
+            tt(T.f3[:, 0:128], T.f3[:, 0:128], T.f1[:, 0:128], A.mult, "f1 f3", "f3")
+            ts(T.oE[:], T.f3[:, 0:128], 15.0, A.add, "f3", "oE")
+            for k, bank in enumerate(("PS", "PY")):
+                a = 512 * k + (k == 0)
+                o, p = T.TG[:, a:512 * k + 512], T[bank][:, a - 512 * k:512]
+                mm(p, [(T.Wv[:, 0:128], T.cwa[:, a:512 * k + 512]), (T.Wv[:, 128:256], T.cwa[:, a - 1:512 * k + 511])], "Wv Wv1 cwa", bank)
+                either(TS(o, p, 0.0, A.is_equal), ACT(o, p, F.Relu, scale=-1.0, bias=1.0), bank, ("Tt", "Gj")[k])
+            left = [sums(q, False) for q in range(4)]
+            ts(T.pre[:], T.gam[:, 0:64], col[:, 5:6], A.is_ge, "gam c5", "pre", float(W0 - 32 - PL), A.mult)
+            ts(T.f2[:, 0:64], T.PK[:, 64:128], 2816.0, A.add, "PK", "f2")
+            ts(T.j2[:, 0:64], T.j1[:, 0:64], 2, SH, "j1", "j20 j21", 2047, AND)
+            tt(T.f2[:, 0:64], T.f2[:, 0:64], T.isL[:, 0:64], A.mult, "f2 isL", "f2")
+            tt(T.f2[:, 0:64], T.f2[:, 0:64], T.pre[:], A.max, "f2 pre", "f2")
+            tt(T.f2[:, 0:64], T.f2[:, 0:64], T.j2[:, 0:64], A.max, "f2 j20 j21", "f2")
+            ts(T.oS[:], T.f2[:, 0:64], 16.0, A.add, "f2", "oS")
+            move(T.M[:], (T.xw0[:, PL:W0], T.oS[:]), "oS vac xl0 " + xn(0), "rr0 rr1")
+            scan(T.xw0[:, 16:1040], T.TG[:], T.M[:], 0.0, A.mult, A.add, "Tt Gj rr0 rr1", "yp0 yp1")
+            for k in range(2):
+                move(T.V[:, 1024 * k:1024 * k + 1024], (T.xw0[:, 0:1040], T.oE[:, 64 * k:64 * k + 64]), "yp0 yp1 vac oE", "V0%d" % k)
             for q in range(4):
-                mm(Pq[q][:], [one, (T.Ib[:], T.xw0[:, 16 + 512 * q:528 + 512 * q])], "cb0 cb1 Ib x0_%d" % q, "P%d" % q, True, False)
-            ts(T.f5[:, 0:48], T.tab[:, 0:48], T.col[:, 3:4], A.is_le, "tab0 c3", "f5")
-            tt(T.held[:], T.f5[:, 0:48], T.flG[:, 0:48], A.mult, "f5 flG0", "held")
-        cp(T.nn[:, 68:136], T.PY[:, 128:196], "PY", "nn1")
-        tt(T.nn[:, 0:68], T.PX[:, 192:260], T.cf[:], A.add, "PX cf", "nn0")
-        ts(T.f1[:, 0:136], T.nn[:], -768.0, A.add, "nn0 nn1 pc", "f1", K, A.mult)
-        ts(T.f2[:, 0:136], T.nn[:], 768.0, A.is_lt, "nn0 nn1", "f2")
-        ts(T.i1[:, 0:136], T.f1[:, 0:136], C, A.add, "f1 pc", "i1")
-        ts(T.f3[:, 0:136], T.nn[:], 4.0, A.mult, "nn0 nn1", "f3", 8192.0, A.add)
-        ts(T.i1[:, 0:136], T.i1[:, 0:136], 8191, AND, "i1", "i1")
-        ts(T.vG[:], T.PX[:, 192:260], 16.0, A.is_ge, "PX", "vG")
-        tt(T.f3[:, 0:136], T.f3[:, 0:136], T.i1[:, 0:136], A.subtract, "f3 i1", "f3")
-        tt(T.f3[:, 0:136], T.f3[:, 0:136], T.f2[:, 0:136], A.mult, "f3 f2", "f3")
-        tt(T.valG[:], T.f3[:, 0:136], T.i1[:, 0:136], A.add, "f3 i1", "valG")
+                more(Pq[q][:], [(T.Ib[:], T.V[:, 512 * q:512 * q + 512])], "Ib V0%d" % (q // 2), "P%d" % q, left[q])
+        conv(T.PX[:, 128:196], T.Zt if last else T.Zc, lambda r: T.cwa[:, r:1088:16], "Zc Zt cwa", "PX")
+        conv(T.PX[:, 196:264], T.Zc, lambda r: T.cwa[:, 68 * r:68 * r + 68], "Zc cwa", "PX")
+        ts(T.g2[:, 0:68], T.PK[:, 132:200], 4.0, A.mult, "PK", "g2", 11264.0, A.add)
+        ts(T.j1[:], T.j1[:], 8191, AND, "j1", "j1")
+        tt(T.g2[:, 0:68], T.g2[:, 0:68], T.isL[:, 68:136], A.mult, "g2 isL", "g2")
+        tt(T.valG[:], T.g2[:, 0:68], T.j1[:, 68:136], A.max, "g2 j1", "valG")
         if not last:
-            ts(T.valG[:, 68:136], T.valG[:, 68:136], 64.0, A.add, "valG", "valG")
-        dma("dG", [(T.dG[row, :], T.valG[:, 68:136])], "valG", "dG")
-        tt(T.vG[:], T.vG[:], T.vT[:], A.mult, "vG vT", "vG")
-        cp(T.i1[:, 0:68], T.valG[:, 0:68], "valG", "i1")
-        pick(T.oT[:], "oT", T.pdT[:], "pdT", T.vG[:], "vG", T.dumA[:, 0:68], "dumA", 68)
+            plus(T.valG[:], T.valG[:], 64.0, "valG", "valG")
+        dma([(T.dG[row, :], T.valG[:])], "valG", "dG dG1", 40)
+        plus(T.valT[:], T.PX[:, 196:264], -64.0 if last else 0.0, "PX", "valT")
+        dma([(T.dT[row, :], T.valT[:])], "valT", "dT", 40)
+        inv, invX = T.inv[:, 0:68], T.inv[:, 68:136]
+        ts(inv, T.gam[:, 0:68], col[:, 8:9], A.is_ge, "gam c8", "inv")
+        ts(T.f2[:, 68:136], T.gam[:, 0:68], col[:, 9:10], A.is_lt, "gam c8", "f2b")
+        ts(T.f5[:, 0:68], T.gam[:, 0:68], col[:, 10:11], A.is_ge, "gam c8", "f5")
+        tt(invX, inv, T.f2[:, 68:136], A.mult, "inv f2b", "invX")
+        tt(invX, invX, T.f5[:, 0:68], A.max, "invX f5", "invX")
         if not last:
-            act(T.UA[:].indirect(T.oT[:]), T.dG[:], F.Silu, "oT dG", "UA")
-            dma("uar", [(T.tmpA[:], T.UA[row, 0:8960])], "UA", "tmpA tmpL")
-            ts(T.oS[:], T.valG[:, 0:68], 0.25, A.mult, "valG", "oS", 15.625, A.add)
-            pick(T.oV[:], "oV", T.pdV[:], "pdV", T.vG[:], "vG", T.dumV[:], "dumV", 68)
-            cp(T.M[:], T.xw0[:].indirect(T.oS[:]), "oS vac xl0 " + xn(0), "M rr0 rr1")
-            cp(T.VA[:].indirect(T.oV[:]), T.M[:], "oV M rr0 rr1", WALL + " W41")
-            clear_l1()
-        pos_b(T.i1[:, 0:68], "i1", 68, T.dumB[:, 0:68], "dumB", T.pdT[:], "pdT")
-        pick(T.oG[:], "oG", T.pdT[:], "pdT", T.vG[:], "vG", T.dumB[:, 0:68], "dumB", 68)
-        if last:
-            cp(T.BW[:].indirect(T.oG[:]), T.dT[:], "oG dT", "BW")
-            dma("ya", [(T.ya[:], T.BW[row, 0:8192])], "BW", "")
-            cp(T.UA[:].indirect(T.oT[:]), T.dG[:], "oT dG", "UA")
-            dma("yd", [(T.yd[:], T.UA[row, 0:8192])], "UA", "", q="s")
+            ts(T.i1[:, 0:68], T.PX[:, 128:196], -64.0, A.add, "PX", "i1")
+            place(T.i1[:, 0:68], "i1", 68, T.posT[:], "posT")
+            pick(T.posT[:], "posT", invX, "invX", T.dumA[:, 0:68], 68, T.oT[:], "oT")
+            move((T.UA[:], T.oT[:]), T.dG[:], "oT dG dG1", "UA")
+            dma([(T.D[:], T.UA[row, :])], "UA", "D DL", 360)
+            tt(invX, invX, T.isL[:, 0:68], A.max, "invX isL", "invX")
+            tt(T.dX[:], invX, T.dumK[:, 0:68], A.mult, "invX dumK", "dX")
+            ts(T.f2[:, 68:136], T.j1[:, 0:68], 64.0, A.add, "j1", "f2b")
+            tt(T.f2[:, 68:136], T.f2[:, 68:136], T.dX[:], A.max, "f2b dX", "f2b")
+            cp(T.oG[:], T.f2[:, 68:136], "f2b", "oG")
+            ts(T.f4[:, 0:48], T.g1[:, 0:48], col[:, 0:1], A.is_le, "g1 c0", "f4")
+            tt(T.f4[:, 0:48], T.f4[:, 0:48], T.flG[:, 0:48], A.mult, "f4 flG0", "f4")
+            tt(T.held[:], T.held[:], T.f4[:, 0:48], A.add, "held f4", "held")
+        else:
+            ts(T.dA[:], T.gam[:, 0:68], 8448.0, A.add, "gam", "dA")
+            ts(T.posT[:], T.PX[:, 128:196], 512.0 * 960 - 64, A.add, "PX", "posT")
+            tt(T.dX[:], T.dA[:], inv, A.mult, "dA inv", "dX")
+            tt(T.posT[:], T.posT[:], T.dX[:], A.max, "posT dX", "posT")
+            cp(T.oT[:], T.posT[:], "posT", "oT")
+            ts(T.AI[:], T.D[:], -64.0, A.add, "D DL", "AI AI0 AI1 AI2 AI3", -1.0, A.max)
+            cp(T.Pf[:], T.Qh[:], "Qh", "Pf")
+            cp(T.D[:], T.AI[:], "AI", "D DL")
+            for b in range(4):
+                mm(T.PS[:, b:512:4], [(T.Pf[:, 144 * b + 3 - j:144 * b + 131 - j], pl(T.D, j)) for j in range(4)], "Pf D", "PS")
+            move(T.D[:, 0:512], T.PS[:], "PS", "D DL")
+            iota(T.km[:, 0:64], [[16, 32], [0, 2]], 0, 0, "km")
+            iota(T.km[:, 64:96], [[1, 16], [512, 2]], 0, 0, "km")
+            ts(pf[:, 22:23], pf[:, 1:2], 31.0, A.mult, "pfa", "pf22", pf[:, 5:6], A.add)
+            ts(T.lpre[:], T.km[:, 0:64], pf[:, 1:2], A.add, "km pfa", "lpre")
+            ts(T.lpost[:], T.km[:, 64:96], pf[:, 22:23], A.add, "km pf22", "lpost")
+            tt(T.Eb[:], T.Eb[:], T.Fb[:], A.mult, "Eb Fb", "Eb")
+            ts(T.axoi[:], T.Eb[:], 1.0 / 64, A.mult, "Eb", "axoi", -64.0, A.add)
+            turn(T.Eb[:], "Eb", T.UA[:, 8192:9216], "UA", T.UA[:, 9216:10240], "UAb", -1.0, A.max)
+            dma([(T.UA[row, 0:8192], T.D[:, 0:512])], "D", "UAn", 256)
+            dma([(T.AX[row, 0:8192], T.Eb[:])], "Eb", "AX", 256)
+            tt(invX, invX, T.isL[:, 0:68], A.max, "invX isL", "invX")
+            ts(T.i2[:, 0:68], T.j1[:, 0:68], 15, AND, "j1", "i2")
+            ts(T.i2[:, 68:136], T.j1[:, 0:68], 4, SH, "j1", "i3")
+            tt(T.dX[:], invX, T.dA[:], A.mult, "invX dA", "dX")
+            ts(T.f2[:, 0:68], T.i2[:, 0:68], 512.0, A.mult, "i2", "f2")
+            tt(T.f2[:, 0:68], T.f2[:, 0:68], T.i2[:, 68:136], A.add, "f2 i3", "f2")
+            tt(T.f2[:, 0:68], T.f2[:, 0:68], T.dX[:], A.max, "f2 dX", "f2")
+            cp(T.oG[:], T.f2[:, 0:68], "f2", "oG")
+            cp((T.AX[:], T.oG[:]), T.dT[:], "oG dT", "AX")
+            dma([(T.ya[:], T.AX[row, 0:8192])], "AX", "", 256)
+            cp((T.UA[:], T.oT[:]), T.dG[:], "oT dG dG1", "UA UAb UAn")
+            dma([(T.yd[:], T.UA[row, 0:8192])], "UA", "", 256, q="s")
+
+    if "order" not in PLAN:
+        PLAN["order"] = schedule(ops)
+    toks, cnt, seen = {}, {}, {q: {} for q in Q}
+
+    def wait(q, need):
+        for s, n in need:
+            if seen[q].get(s, 0) < n and not q == "t" == s[1]:
+                Q[q].wait_ge(T.sem[s], n)
+                seen[q][s] = n
+    for i, q in PLAN["order"]:
+        wait(q, sorted((tok for p in ops[i][0] for tok in toks[p]), key=lambda x: -x[1]))
+        got = calls[i][q]()
+        if not isinstance(got, list):
+            s = "q" + q
+            got.then_inc(T.sem[s], 1)
+            got = [(s, cnt.get(s, 0) + 1)]
+        toks[i] = got
+        cnt.update(got)
     wait("g", list(cnt.items()))

@@ -6,9 +6,8 @@ N, RO = 4, 3
 W0, W1 = 4912, 2832
 PL = 2064
 UAW, AXW, L1W = 11264, 11328, 1680
-MODE = {(0, 0): "vr", (1, 0): "va", (2, 0): "va", (3, 0): "s", (0, 1): "va", (1, 1): "va", (2, 1): "va", (3, 1): "s"}
-PASSES = 3000
-HEAT = 0.3
+SP = 3
+PASSES, STARTS, HEAT = 2500, 3, 0.1
 f32, bf, f16, i32, u16 = "float32", "bfloat16", "float16", "int32", "uint16"
 
 
@@ -19,12 +18,12 @@ def sb(n, t):
 SCRATCH = {
     "xw0": sb(W0, bf), "xw1": sb(W1, bf), "V": sb(8192, bf), "VA": sb(8192, bf), "snd": sb(1536, bf),
     "UA": sb(UAW, f32), "AX": sb(AXW, f32), "La": sb(L1W, f32), "Lb": sb(L1W, f32), "zer": sb(1024, f32),
-    "dT": sb(1088, f32), "dG": sb(1088, f32), "cwa": sb(1088, f16), "cwb": sb(1088, f16), "DEC": sb(1088, bf),
+    "dT": sb(1088, f32), "dG": sb(1088, f32), "cwa": sb(1088, f16), "cwb": sb(1088, f16), "DEC": sb(1160, bf),
     "wa": sb(592, f32), "wb": sb(592, f32), "D": sb(704, f32), "AI": sb(704, i32), "isT": sb(704, bf), "vacm": sb(704, bf),
     "off": sb(704, u16), "ofp": sb(512, u16), "M": sb(1024, bf), "msR": sb(768, bf), "TG": sb(1024, bf),
     "Fb": sb(512, f32), "Eb": sb(512, f32), "RV": sb(2048, bf),
     "axoi": sb(512, i32), "pari": sb(8, i32), "parf": sb(8, f32), "pc": sb(16, f32),
-    "flT": sb(592, f16), "flG": sb(560, f16), "flE": sb(576, f16), "cumT": sb(608, f16), "cumG": sb(576, f16),
+    "flT": sb(592, bf), "flG": sb(560, bf), "flE": sb(576, bf), "cumT": sb(608, f16), "cumG": sb(576, f16),
     "km": sb(256, f32), "held": sb(48, f32), "alive": sb(48, f32),
     "i1": sb(136, i32), "i2": sb(136, i32), "j1": sb(136, i32), "j2": sb(136, i32),
     "f1": sb(256, f32), "f2": sb(136, f32), "f3": sb(136, f32), "f4": sb(136, f32), "f5": sb(136, f32), "g1": sb(136, f32), "g2": sb(136, f32),
@@ -34,11 +33,11 @@ SCRATCH = {
     "sea": sb(80, f32), "seb": sb(80, f32), "posT": sb(68, f32), "valT": sb(68, f32), "valG": sb(68, f32),
     "inv": sb(136, f32), "dA": sb(68, f32), "dX": sb(68, f32), "isL": sb(136, f32), "pre": sb(64, f32),
     "col": sb(24, f32), "pi": sb(8, i32), "pf": sb(28, f32), "yrow": sb(144, f32),
-    "Zb": sb(144, bf), "Zk": sb(144, bf), "Zr": sb(144, bf), "Zn": sb(144, bf), "Zq": sb(144, bf),
+    "Zb": sb(144, bf), "Zk": sb(144, bf), "Zp": sb(288, bf), "Zq": sb(144, bf),
     "Zh": sb(144, f16), "Zc": sb(144, f16), "Zt": sb(144, f16),
     "Ib": sb(128, bf), "I4": sb(128, bf), "In": sb(128, bf), "Ig": sb(128, bf), "If": sb(128, f32),
-    "BOh": sb(128, f16), "TRI": sb(128, f16), "TRp": sb(128, f16), "TRs": sb(128, f16), "TRe": sb(128, f16), "Ie": sb(128, f16),
-    "Wv": sb(256, f16), "Pf": sb(576, f32), "Qh": sb(576, f16), "cb": sb(976, bf), "ch": sb(832, f16), "Ut": sb(16, bf),
+    "BOh": sb(128, f16), "TRI": sb(128, bf), "TRp": sb(128, bf), "TRs": sb(128, bf), "TRe": sb(128, bf), "Ie": sb(128, f16),
+    "Wv": sb(256, f16), "Pf": sb(576, f32), "Qh": sb(576, bf), "cb": sb(976, bf), "ch": sb(832, f16), "Ut": sb(16, bf),
     "Dc": sb(40, f32), "CL": sb(80, f32), "gam": sb(136, f32), "dumA": sb(144, f32), "dumK": sb(144, f32),
 }
 for _k in ("P0", "P1", "P2", "P3", "PK", "PS", "PX", "PY"):
@@ -98,20 +97,59 @@ def schedule(ops):
             if new:
                 ready.sort()
         return max(fin), fin, where
-    rng = np.random.default_rng(1)
-    prio, pen = level, [0.5] * n
-    best = now = one(prio, pen, pred, succ, None)
-    for k in range(PASSES):
-        base = one(now[1], pen, succ, pred, now[2])[1] if k % 4 == 0 else prio
-        t0 = rng.random() * now[0]
-        near = (np.abs(np.array(now[1]) - t0) < 8.0) * (rng.random(n) < 0.3)
-        p2 = (np.array(base) + near * rng.normal(0.0, (0.4, 1.2)[k % 2], n)).tolist()
-        e2 = np.where(near * (rng.random(n) < 0.4), rng.random(n) * 3.0 - 0.5, pen).tolist()
-        got = one(p2, e2, pred, succ, None)
-        if got[0] <= now[0] + HEAT * (1.0 - k / PASSES):
-            now, prio, pen = got, p2, e2
-            if got[0] < best[0]:
-                best = got
+
+    def tight(s):
+        fin, where = s[1], s[2]
+        st = [fin[i] - sum(ops[i][1][where[i]]) for i in range(n)]
+        before, last = [-1] * n, {}
+        for i in sorted(range(n), key=lambda i: st[i]):
+            before[i] = last.get(where[i], -1)
+            last[where[i]] = i
+        out, i = [], fin.index(s[0])
+        while i >= 0:
+            a, p = before[i], max(pred[i], key=lambda p: fin[p], default=-1)
+            if a >= 0 and a not in pred[i] and (p < 0 or st[a] + ops[a][1][where[a]][0] > fin[p] + 0.02):
+                out.append((a, i))
+                i = a
+            else:
+                if len(ops[i][1]) > 1:
+                    out.append((i, i))
+                i = p
+        return out
+    prio0, pen0 = level, [1.0] * n
+    best = now = one(prio0, pen0, pred, succ, None)
+    for k in range(12):
+        p2 = one(now[1], pen0, succ, pred, now[2])[1]
+        now = one(p2, pen0, pred, succ, None)
+        if now[0] < best[0]:
+            best, prio0 = now, p2
+    first = best
+    for seed in range(1, STARTS + 1):
+        rng = np.random.default_rng(seed)
+        now, prio, pen = first, prio0, pen0
+        path = tight(now)
+        for k in range(PASSES):
+            p2, e2 = list(prio), list(pen)
+            for z in range(1 + (k % 3 == 0)):
+                a, b = path[int(rng.random() * len(path))]
+                u = rng.random()
+                c = [x for x in (a, b) if len(ops[x][1]) > 1]
+                if c and (a == b or u < 0.4):
+                    x = c[int(rng.random() * len(c))]
+                    e2[x] = -0.9 if now[2][x] != "v" else 9.0
+                elif u < 0.75:
+                    p2[a] = min(p2[a], p2[b]) - 3.0 * rng.random() ** 2
+                else:
+                    todo, up = [b], max(p2[a], p2[b]) + rng.random() - p2[b]
+                    for x in todo:
+                        p2[x] += up
+                        todo += [y for y in pred[x] if y not in todo and now[1][y] > now[1][b] - 6.0]
+            got = one(p2, e2, pred, succ, None)
+            if got[0] <= now[0] + HEAT * (1.0 - k / PASSES) * rng.random():
+                now, prio, pen = got, p2, e2
+                path = tight(now)
+                if got[0] < best[0]:
+                    best = got
     best = (best[0], [(best[1][i] - sum(ops[i][1][best[2][i]]), i, best[2][i]) for i in range(n)])
     return [(i, q) for st, i, q in sorted(best[1])]
 
@@ -177,7 +215,15 @@ def rank_program(g, core, T, topo):
         return {"s": (cost("s", out, a), 0.0, lambda: g.scalar.activation(ap(out), ap(a), f, **kw))}
 
     def ts(out, a, s1, o0, R, W, s2=None, o1=None):
-        record(TS(out, a, s1, o0, s2, o1), R, W)
+        alts = TS(out, a, s1, o0, s2, o1)
+        if not isinstance(a, tuple) and all("float32" in str(x.dtype) or "bfloat16" in str(x.dtype) for x in (out, a)):
+            if o0 == A.mult and o1 == A.add:
+                alts.update(ACT(out, a, F.Identity, scale=s1, bias=s2))
+            if o0 == A.add and o1 is None:
+                alts.update(ACT(out, a, F.Identity, bias=s1))
+            if o0 == A.mult and o1 is None:
+                alts.update(ACT(out, a, F.Identity, scale=s1))
+        record(alts, R, W)
 
     def tt(out, a, b, o, R, W):
         record({"v": (cost("v", out, a, b, True), 0.0, lambda: v.tensor_tensor(ap(out), ap(a), b, o))}, R, W)
@@ -198,6 +244,11 @@ def rank_program(g, core, T, topo):
         n = out.shape[1]
         record({**CP(out, a), **ACT(out, a, F.Copy), "g": (0.17 + 2 * n * CY, 0.0, lambda: g.affine_select(out, a, [[0, n]], A.is_ge, 0.0, 0, 0))}, R, W)
 
+    def zero(out, W):
+        n = out.shape[1]
+        record({**CP(out, T.zer[:, 0:n]), **ACT(out, T.zer[:, 0:n], F.Copy),
+                "g": (0.13 + 2 * n * CY, 0.0, lambda: g.iota(out, [[0, n]], 0, 0, allow_small_or_imprecise_dtypes=True))}, "zer", W)
+
     def plus(out, a, c, R, W):
         either(TS(out, a, c, A.add), ACT(out, a, F.Identity, bias=c), R, W)
 
@@ -206,6 +257,9 @@ def rank_program(g, core, T, topo):
 
     def scan(out, a, b, init, o0, o1, R, W):
         record({"v": (cost("v", out, a, b), 0.0, lambda: v.tensor_tensor_scan(out, a, b, init, o0, o1))}, R, W)
+
+    def turned(out, a, R, W):
+        record({"v": (cost("v", out, a), 0.0, lambda: v.transpose(out, a))}, R, W)
 
     def iota(out, pat, base, cm, W, flt=True):
         kw = {"allow_small_or_imprecise_dtypes": True} if flt else {}
@@ -301,6 +355,10 @@ def rank_program(g, core, T, topo):
     def clear(bank, n):
         mm(T[bank][:, 0:n], [(T.Zq[0:1, 16:144], T.cb[0:1, 0:n])], "Zq cb0", bank, True, False)
 
+    def refill(L, n):
+        plus(L[:, 0:1024], T.zer[:], pf[:, 10:11], "zer pf10", n)
+        plus(L[:, 1024:1088], T.zer[:, 0:64], pf[:, 10:11], "zer pf10", n)
+
     dma([(T.axoi[:], T.axo[:])], "", "axoi", 256)
     dma([(T.AI[:, 0:512], T.den[:])], "", "AI", 512, q="s")
     dma([(T.V[:, 0:2048], T.x0[:])], "", "V00 V01", 1024)
@@ -316,9 +374,7 @@ def rank_program(g, core, T, topo):
     record({"g": (3.9, 0.0, lambda: g.affine_select(T.RV[:], T.RV[:], [[-1, 16], [-16, 8], [0, 16]], A.is_equal, 0.0, 0, 1))}, "RV", "RV")
     iota(T.AX[:, 8256:AXW:4], [[0, 768]], 64, 0, "AXl")
     ms(T.zer[:], 0.0, "zer")
-    for B, n in ((T.La, "La"), (T.dT, "dT")):
-        plus(B[:, 0:1024], T.zer[:], 64.0, "zer", n)
-        plus(B[:, 1024:1088], T.zer[:, 0:64], 64.0, "zer", n)
+    iota(T.dT[:], [[0, 1088]], 64, 0, "dT")
     ts(T.pi[:, 1:2], T.pi[:, 0:1], 15, AND, "pi0", "pi1")
     ts(T.pi[:, 2:3], T.pi[:, 0:1], 112, AND, "pi0", "pi2")
     ts(T.pi[:, 3:4], T.pi[:, 0:1], 3, AND, "pi0", "pi3")
@@ -330,9 +386,10 @@ def rank_program(g, core, T, topo):
     ts(pf[:, 8:9], pf[:, 1:2], 15.0, A.is_equal, "pfa", "pf8")
     ms(T.cumG[:, 0:1], 0.0, "cumG0")
     ms(T.cumT[:, 0:1], 0.0, "cumT0")
-    ts(pf[:, 9:10], pf[:, 8:9], 17.0, A.mult, "pf8", "pf9", -1.0, A.add)
-    ts(pf[:, 10:11], pf[:, 8:9], 4032.0, A.mult, "pf8", "pf10", 64.0, A.add)
-    ts(pf[:, 11:12], pf[:, 8:9], -1.0, A.mult, "pf8", "pf11", 1.0, A.add)
+    ts(pf[:, 9:10], pf[:, 8:9], 16.0 + 1.0 / 32, A.mult, "pf8", "pf9", -1.0 / 32, A.add)
+    ts(pf[:, 10:11], pf[:, 8:9], 965.0 - 32783.5, A.mult, "pf8", "pf10", 32783.5, A.add)
+    ts(pf[:, 11:12], pf[:, 8:9], -1.0, A.add, "pf8", "pf11")
+    refill(T.La, "La")
     ts(T.g1[:, 0:128], T.yrow[:, 0:128], pf[:, 6:7], A.is_le, "yrow pf6", "g1")
     ts(T.f2[:, 0:128], T.yrow[:, 0:128], pf[:, 2:3], A.is_ge, "yrow pfa", "f2 f2b")
     ts(T.f3[:, 0:128], T.yrow[:, 0:128], pf[:, 0:1], A.is_ge, "yrow pfa", "f3")
@@ -347,22 +404,25 @@ def rank_program(g, core, T, topo):
     ms(T.ch[0:32, 704:832], 0.0, "ch2")
     ms(T.ch[0:32, 719:832:16], 1.0, "ch2")
     ts(T.Dc[:], T.gam[:, 0:40], 1088.0, A.add, "gam", "Dc")
-    move(T.Lb[:, 0:768], T.zer[:, 0:768], "zer", "Lb")
+    zero(T.Lb[:, 0:768], "Lb")
     plus(T.DEC[:, 0:1024], T.zer[:], pf[:, 11:12], "zer pf11", "DEC")
-    plus(T.DEC[:, 1024:1088], T.zer[:, 0:64], pf[:, 11:12], "zer pf11", "DEC1")
-    move(T.snd[:, 0:768], T.zer[:, 0:768], "zer", "snd")
-    move(T.D[:], T.zer[:, 0:704], "zer", "D DL")
-    move(T.dG[:, 768:1088], T.zer[:, 0:320], "zer", "dG1")
+    plus(T.DEC[:, 1024:1160], T.zer[:, 0:136], pf[:, 11:12], "zer pf11", "DEC1 DEC2")
+    zero(T.snd[:, 0:768], "snd")
+    zero(T.D[:], "D DL")
+    zero(T.dG[:, 768:1088], "dG1")
     for a in (0, PL, W0 - 16):
         ms(T.xw0[:, a:a + 16], 0.0, "vac")
     ms(T.xw1[:, 0:16], 0.0, "vac1")
     ts(pf[:, 23:24], pf[:, 7:8], 1024.0, A.mult, "pf7", "pf23")
-    ts(pf[:, 24:25], pf[:, 8:9], 513.0, A.mult, "pf8", "pf24", -512.0, A.add)
-    for Z, w, n, R in ((T.Zh, 1.0, "Zh", ""), (T.Zc, pf[:, 9:10], "Zc", "pf9"), (T.Zb, 1.0, "Zb", ""), (T.Zk, 65536.0, "Zk", ""), (T.Zr, 131072.0, "Zr", ""),
-                       (T.Zn, -65536.0, "Zn", ""), (T.Zq, pf[:, 23:24], "Zq", "pf23"), (T.Zt, pf[:, 24:25], "Zt", "pf24")):
+    ts(pf[:, 24:25], pf[:, 8:9], 17.0, A.mult, "pf8", "pf24", -16.0, A.add)
+    for Z, w, n, R in ((T.Zh, 1.0, "Zh", ""), (T.Zc, pf[:, 9:10], "Zc", "pf9"), (T.Zb, 1.0, "Zb", ""), (T.Zt, pf[:, 24:25], "Zt", "pf24")):
         ts(Z[:], T.yrow[:], pf[:, 6:7], A.is_equal, "yrow pf6 " + R, n, w, A.mult)
-    for I, w, n in ((T.Ie, 1.0 / 128, "Ie"), (T.Ib, 1.0, "Ib"), (T.I4, 4.0, "I4"), (T.In, -1.0, "In"), (T.If, 1.0, "If"), (T.Ig, -65536.0, "Ig")):
+    ts(T.Zk[:], T.Zb[:], 65536.0, A.mult, "Zb", "Zk")
+    ts(T.Zq[:], T.Zb[:], pf[:, 23:24], A.mult, "Zb pf23", "Zq")
+    for I, w, n in ((T.Ie, 1.0 / 128, "Ie"), (T.Ib, 1.0, "Ib")):
         ts(I[:], T.yrow[:, 0:128], pf[:, 0:1], A.is_equal, "yrow pfa", n, w, A.mult)
+    for I, w, n in ((T.In, -1.0, "In"), (T.If, 1.0, "If"), (T.Ig, -65536.0, "Ig"), (T.I4, 4.0, "I4")):
+        ts(I[:], T.Ib[:], w, A.mult, "Ib", n)
     ms(T.cb[0:32, 0:512], 1.0, "cb0")
     ms(T.cb[0:32, 512:640], 3072.0, "cb1")
     ms(T.cb[0:32, 896:976], -832.0, "cb6")
@@ -376,16 +436,19 @@ def rank_program(g, core, T, topo):
     ts(pf[:, 13:14], pf[:, 2:3], pf[:, 4:5], A.add, "pfa", "pf13", 12.0, A.add)
     ts(pf[:, 25:26], pf[:, 3:4], 4.0, A.mult, "pfa pf6", "pf25", pf[:, 6:7], A.add)
     ts(pf[:, 25:26], pf[:, 25:26], -12.0, A.add, "pf25", "pf25")
+    ts(T.Zp[:, 0:144], T.yrow[:], pf[:, 13:14], A.is_equal, "yrow pf13", "Zp0")
+    ts(T.Zp[:, 144:288], T.yrow[:], pf[:, 25:26], A.is_equal, "yrow pf25", "Zp1")
     for j in range(4):
-        ts(T.Pf[:, 144 * j:144 * j + 144], T.yrow[:], pf[:, 13:14], A.is_equal, "yrow pf13 pm%d" % j, "Pf", pf[:, 14 + j:15 + j], A.mult)
-        ts(T.Qh[:, 144 * j:144 * j + 144], T.yrow[:], pf[:, 25:26], A.is_equal, "yrow pf25 pn%d" % j, "Qh", pf[:, 18 + j:19 + j], A.mult)
+        ts(T.Pf[:, 144 * j:144 * j + 144], T.Zp[:, 0:144], pf[:, 14 + j:15 + j], A.mult, "Zp0 pm%d" % j, "Pf")
+        ts(T.Qh[:, 144 * j:144 * j + 144], T.Zp[:, 144:288], pf[:, 18 + j:19 + j], A.mult, "Zp1 pn%d" % j, "Qh")
     ts(pf[:, 26:27], pf[:, 1:2], 192.0, A.mult, "pfa", "pf26")
     ts(T.dumK[:], T.dumK[:], pf[:, 26:27], A.add, "dumK pf26", "dumK")
     tt(T.TRs[:], T.TRI[:], T.Ib[:], A.subtract, "TRI Ib", "TRs")
     ts(T.CL[:, 0:37], T.Dc[:, 0:37], 1088.0 + 527.5, A.is_ge, "Dc", "CL", 64.0, A.mult)
     ts(T.CL[:, 0:37], T.CL[:, 0:37], 1024.0, A.add, "CL", "CL")
-    cp(T.CL[:, 37:74], T.CL[:, 0:37], "CL", "CL")
-    ts(col[:, 20:21], pf[:, 8:9], 5.0, A.mult, "pf8 pm3", "c20", pf[:, 17:18], A.subtract)
+    move(T.CL[:, 37:74], T.CL[:, 0:37], "CL", "CL")
+    ts(col[:, 19:20], pf[:, 17:18], 1.0 / 32, A.mult, "pm3", "c19")
+    ts(col[:, 20:21], pf[:, 8:9], 4.0 + 1.0 / 32, A.mult, "pf8 c19", "c20", col[:, 19:20], A.subtract)
     ts(T.Wv[:, 0:128], T.BOh[:], col[:, 20:21], A.mult, "BOh c20", "Wv")
     ts(T.Wv[:, 128:256], T.BOh[:], col[:, 20:21], A.mult, "BOh c20", "Wv1", -1.0, A.mult)
     ts(col[:, 22:23], pf[:, 1:2], 68.0, A.mult, "pfa", "c22")
@@ -409,20 +472,20 @@ def rank_program(g, core, T, topo):
 
     def counts(fl, fn, nb, c1, wd, wn, ba, bb):
         mm(T[ba][:], [(T.TRp[:], fl[:, 0:512]), (sel15, T.ch[0:1, 0:512])], "TRp ch ch2 " + fn, ba)
-        plus(wd[:, 0:512], T[ba][:], 64.0, ba, wn)
+        plus(wd[:, 0:512], T[ba][:], pf[:, 10:11], ba + " pf10", wn)
         if nb > 512:
             mm(T[bb][:, 0:nb - 512], [(T.TRp[:], fl[:, 512:nb]), (sel15, T.ch[0:1, c1:c1 + nb - 512])], "TRp ch ch1 ch2 " + fn, bb)
-            plus(wd[:, 512:nb], T[bb][:, 0:nb - 512], 64.0, bb, wn + "1")
+            plus(wd[:, 512:nb], T[bb][:, 0:nb - 512], pf[:, 10:11], bb + " pf10", wn + "1")
 
-    def run_down(L, ln, cw, cn, a, b, init, R=""):
-        scan(cw[:, a:b], L[:, a:b], T.DEC[:, a:b], init, A.max, A.subtract, ln + " DEC DEC1 " + R, cn)
+    def run_down(L, ln, cw, cn, n, d0=0, R=""):
+        scan(cw[:, 0:n], T.DEC[:, d0:d0 + n], L[:, 0:n], 0.0, A.add, A.max, ln + " DEC DEC1 " + R, cn)
 
     def link_list(src, sn, fl, fn, cum, cn, se, sen, o1, on, bank, pb):
         ts(fl[:, 0:512], src, 8192.0, A.is_ge, sn, fn)
-        ts(T.flE[:, 0:512], src, -8192.0, A.add, sn, "flE", 0.0, A.max)
+        ts(T.cwb[:, 0:512], src, -8192.0, A.add, sn, "cwb", 0.0, A.max)
         scan(cum[:, 1:513], fl[:, 0:512], fl[:, 0:512], 0.0, A.add, A.max, fn, cn)
         heads(cum, cn + " " + cn + "0", 512, None, se, sen, o1, on, bank)
-        mm(T[pb][:], [(T.TRe[:], fl[:, 0:512]), (T.Ie[:], T.flE[:, 0:512])], "TRe Ie flE " + fn, pb)
+        mm(T[pb][:], [(T.TRe[:], fl[:, 0:512]), (T.Ie[:], T.cwb[:, 0:512])], "TRe Ie cwb " + fn, pb)
         move(T.wb[:, 0:512], T[pb][:], pb, "wb")
         move((T.Lb[:], o1[:, 0:32]), T.wb[:, 0:512], on + " wb", "Lb")
         scan(T.dG[:, 0:768], T.Lb[:, 0:768], T.dT[:, 0:768], 0.0, A.max, A.subtract, "Lb dT", "dG")
@@ -446,11 +509,10 @@ def rank_program(g, core, T, topo):
     mm(T.PY[:, 0:1], [(T.BOh[:], T.cumG[:, 512:513])], "BOh cumG", "PY")
     plus(yv[0](0, 2048), T.V[:, 0:2048], 16.0, "V00 V01", xn(0))
     move((T.La[:], T.oa[:, 0:32]), T.wa[:, 0:512], "oa wa", "La")
-    cp(col[:, 0:1], T.PY[:, 0:1], "PY", "c0")
-    run_down(T.La, "La", T.cwa, "cwa", 0, 768, 64.0)
-    ts(T.cwa[:, 0:768], T.cwa[:, 0:768], pf[:, 10:11], A.min, "cwa pf10", "cwa")
+    move(col[:, 0:1], T.PY[:, 0:1], "PY", "c0")
+    run_down(T.La, "La", T.cwa, "cwa", 768)
     conv(T.PS[:, 0:48], T.Zc, lambda r: T.cwa[:, r:768:16], "Zc cwa", "PS")
-    ts(T.oS[:, 0:48], T.PS[:, 0:48], 0.25, A.mult, "PS", "oS", -0.375, A.add)
+    ts(T.oS[:, 0:48], T.PS[:, 0:48], 0.25, A.mult, "PS", "oS", -0.625, A.add)
     conv(T.PS[:, 64:112], T.Zc, lambda r: T.cwa[:, 48 * r:48 * r + 48], "Zc cwa", "PS")
     move(T.M[:, 0:768], (T.xw0[:, PL:Y0 + 2048], T.oS[:, 0:48]), "oS vac " + xn(0), "rr0 rr1")
     ts(T.inv[:, 0:48], T.gam[:, 0:48], col[:, 0:1], A.is_ge, "gam c0", "inv")
@@ -460,10 +522,10 @@ def rank_program(g, core, T, topo):
     ts(T.i1[:, 0:48], T.i1[:, 0:48], 1023, AND, "i1", "i1")
     tt(T.f3[:, 0:48], T.f3[:, 0:48], T.i1[:, 0:48], A.max, "f3 i1", "f3")
     cp(T.oL[:], T.f3[:, 0:48], "f3", "oL")
-    cp((T.snd[:], T.oL[:]), T.M[:, 0:768], "oL rr0 rr1", "snd msS")
-    exchange(T.snd, 0, T.xw0, Y0 + 2048, 1, "snd", "xl0")
-    move(T.valG[:, 0:48], T.PS[:, 64:112], "PS", "valG")
-    move(T.Lb[:, 0:768], T.zer[:, 0:768], "zer", "Lb")
+    cp((T.snd[:], T.oL[:]), T.M[:, 0:768], "oL rr0 rr1", "snd snd1 msS")
+    exchange(T.snd, 0, T.xw0, Y0 + 2048, 1, "snd snd1", "xl0")
+    plus(T.valG[:, 0:48], T.PS[:, 64:112], -1.0, "PS", "valG")
+    zero(T.Lb[:, 0:768], "Lb")
     ts(T.i1[:, 0:48], T.i1[:, 0:48], 4.0, A.mult, "i1", "i1", 8192.0, A.add)
     place(T.i1[:, 0:48], "i1", 48, T.f4[:, 0:48], "f4")
     pick(T.f4[:, 0:48], "f4", T.inv[:, 0:48], "inv", T.dumA[:, 48:96], 48, T.oT[:, 0:48], "oT")
@@ -478,16 +540,19 @@ def rank_program(g, core, T, topo):
     dma([(T.dG[row, 0:768], T.valG[:, 0:48])], "valG", "dG", 30)
     move((T.UA[:], T.oT[:, 0:48]), T.dG[:, 0:768], "oT dG", "UA")
     mm(T.PY[:, 0:1], [(T.BOh[:], T.cumT[:, 512:513])], "BOh cumT", "PY")
-    cp(col[:, 1:2], T.PY[:, 0:1], "PY", "c1")
+    move(col[:, 1:2], T.PY[:, 0:1], "PY", "c1")
     mm(T.PY[:, 0:7], [(T.hiF[0:8, :], T.parf[0:8, 0:7])], "hiF parf", "PY")
-    cp(pc[:, 0:7], T.PY[:, 0:7], "PY", "pc")
+    move(pc[:, 0:7], T.PY[:, 0:7], "PY", "pc")
     ts(pc[:, 8:11], pc[:, 0:3], 256.0, A.add, "pc", "pc2")
+    ts(pc[:, 11:12], pc[:, 0:1], -64.0, A.mult, "pc", "pc3", -255.0 * 64, A.add)
+    ts(pc[:, 12:13], pc[:, 2:3], -2.0 ** 25, A.mult, "pc", "pc3", -255.0 * 2 ** 25, A.add)
+    ts(pc[:, 13:16], pc[:, 4:7], pc[:, 3:4], A.subtract, "pc", "pc4")
     ts(T.inv[:, 68:116], T.gam[:, 0:48], col[:, 1:2], A.is_ge, "gam c1", "invX")
     ts(T.i1[:, 0:48], T.PX[:, 64:112], 32.0, A.mult, "PX", "i1")
     ts(T.i1[:, 0:48], T.i1[:, 0:48], 1023, AND, "i1", "i1")
     ts(T.i1[:, 0:48], T.i1[:, 0:48], 4.0, A.mult, "i1", "i1", 8256.0, A.add)
-    iota(T.La[:, 0:1088], [[0, 1088]], 64, 0, "La")
-    iota(T.Lb[:, 0:1088], [[0, 1088]], 64, 0, "Lb")
+    refill(T.La, "La")
+    refill(T.Lb, "Lb")
     dma([(T.D[:], T.UA[row, :])], "UA", "D DL", 360)
 
     def prefetch(k, win, off, R):
@@ -505,15 +570,16 @@ def rank_program(g, core, T, topo):
     for q in range(4):
         sums(q, True)
 
-    def turn(out, on, ta, tan, tb, tbn, s1, o1):
-        ts(ta, (T.axoi[:], T.lpre[:]), s1, o1, "axoi lpre", tan)
-        record({"v": (1024 * CY, 0.0, lambda: v.transpose(tb, ta))}, tan, tbn)
+    def turn(out, on, ta, tan, tb, tbn):
+        move(ta, (out, T.lpre[:]), on + " lpre", tan)
+        turned(tb, ta, tan, tbn)
         move(out, (tb, T.lpost[:]), tbn + " lpost", on)
 
     ts(pf[:, 22:23], pf[:, 1:2], 32.0, A.mult, "pfa", "pf22")
     ts(T.lpost[:], T.yrow[:, 0:32], 32.0, A.mult, "yrow pfa", "lpost", pf[:, 5:6], A.add)
     ts(T.lpre[:], T.f1[:, 0:64], pf[:, 22:23], A.add, "f1 pf22", "lpre")
-    turn(T.Eb[:], "Eb", T.AX[:, 64:1088], "AXa", T.AX[:, 1088:2112], "AXb", 64.0, A.add)
+    ts(T.Eb[:], T.axoi[:], 64.0, A.add, "axoi", "Eb")
+    turn(T.Eb[:], "Eb", T.AX[:, 64:1088], "AXa", T.AX[:, 1088:2112], "AXb")
     ts(T.Fb[:], T.Eb[:], 63.5, A.is_ge, "Eb", "Fb", 64.0, A.mult)
     cp(T.j1[:, 0:1], pc[:, 3:4], "pc", "j1")
     ts(T.f2[:, 0:16], T.yrow[:, 0:16], -1.0, A.mult, "yrow pfa", "f2", pf[:, 1:2], A.add)
@@ -542,19 +608,24 @@ def rank_program(g, core, T, topo):
     lo, th, hi, K = pc[:, 8:9], pc[:, 9:10], pc[:, 10:11], pc[:, 3:4]
 
     def mod16(b, q):
-        o = T.M[:, 512 * (q % 2):512 * (q % 2) + 512]
-        plus(o, Pq[q][:], -23.5, "P%d" % q, "rr%d" % (q % 2))
-        tt(yv[b](512 * q, 512 * q + 512), Pq[q][:], o, A.subtract, "P%d rr%d" % (q, q % 2), "x%d_%d" % (b, q))
+        o, n = T.M[:, 512 * (q % 2):512 * (q % 2) + 512], "rr%d" % (q % 2)
+        if b:
+            o, n = T.V[:, 4096 + 1024 * q:4608 + 1024 * q], "V%d%d" % (2 + q // 2, q % 2)
+        plus(o, Pq[q][:], -23.5, "P%d" % q, n)
+        tt(yv[b](512 * q, 512 * q + 512), Pq[q][:], o, A.subtract, "P%d %s" % (q, n), "x%d_%d" % (b, q))
+
+    def send(win, R, dst, d0, W):
+        for k in range(2):
+            move(T.snd[:, 384 * k:384 * k + 384], (win, T.oN[:, 24 * k:24 * k + 24]), "oN " + R, ("snd", "snd1")[k])
+        exchange(T.snd, 0, dst, d0, 1, "snd snd1", W)
 
     for t in range(RO):
         last = t == RO - 1
-        C = pc[:, 4 + t:5 + t]
         for q in range(4):
             mod16(1, q)
         if t == 0:
             ts(T.oN[:], T.D[:, LK], 0.25, A.mult, "DL", "oN", -0.375, A.add)
-        move(T.snd[:, 0:768], (T.xw1[:, 0:2064], T.oN[:]), "oN vac1 " + xn(1), "snd")
-        exchange(T.snd, 0, T.xw1, 2064, 1, "snd", "xl1")
+        send(T.xw1[:, 0:2064], "vac1 " + xn(1), T.xw1, 2064, "xl1")
         for hq in range(2):
             copy3(own(1024 * hq, 1024 * hq + 1024), yv[1](1024 * hq, 1024 * hq + 1024), "x1_%d x1_%d" % (2 * hq, 2 * hq + 1), "yp%d yp%d" % (2 * hq, 2 * hq + 1))
         if t > 0:
@@ -573,66 +644,74 @@ def rank_program(g, core, T, topo):
         tt(T.f5[:, 0:48], T.f5[:, 0:48], T.dumK[:, 0:48], A.mult, "f5 dumK", "f5")
         tt(T.f5[:, 0:48], T.f5[:, 0:48], T.D[:, LK], A.max, "f5 DL", "f5")
         cp(T.oL[:], T.f5[:, 0:48], "f5", "oL")
-        ts(T.j1[:, 0:32], T.gam[:, 0:32], K, A.mult, "gam pc", "j1", C, A.add)
+        ts(T.j1[:, 0:32], T.gam[:, 0:32], K, A.mult, "gam pc", "j1", pc[:, 4 + t:5 + t], A.add)
         ts(T.j2[:, 0:32], T.j1[:, 0:32], 511, AND, "j1", "j20")
         ts(T.j2[:, 32:64], T.j1[:, 0:32], 9, SH, "j1", "j21", 15, AND)
         cp(T.oJ[:], T.j2[:, 0:64], "j20 j21", "oJ")
         move(T.TG[:, 0:512], (T.Ut[:], T.oJ[:, 32:64]), "Ut oJ", "Tt")
         if last:
+            dma([(T.Eb[:], T.AX[row, 64:8256])], "AX", "Eb", 256)
+            iota(T.wa[:, 0:64], [[16, 32], [0, 2]], 0, 0, "wa")
+            iota(T.wa[:, 64:96], [[1, 16], [512, 2]], 0, 0, "wa")
+            ts(pf[:, 22:23], pf[:, 1:2], 31.0, A.mult, "pfa", "pf22", pf[:, 5:6], A.add)
+            ts(T.lpre[:], T.wa[:, 0:64], pf[:, 1:2], A.add, "wa pfa", "lpre")
+            ts(T.lpost[:], T.wa[:, 64:96], pf[:, 22:23], A.add, "wa pf22", "lpost")
+            ts(T.axoi[:], T.Eb[:], -64.0, A.add, "Eb", "axoi")
+            ts(T.Eb[:], T.axoi[:], -1.0, A.max, "axoi", "Eb")
+            turn(T.Eb[:], "Eb", T.UA[:, 8192:9216], "UA", T.UA[:, 9216:10240], "UAb")
+        if t == RO - 2:
             iota(T.dG[:, 0:768], [[4, 768]], 8256 - 64, 0, "dG")
             ts(col[:, 18:19], pf[:, 7:8], 1.0 / 64, A.mult, "pf7", "c18")
-            either(TS(T.dT[:, 0:768], T.dG[:, 0:768], col[:, 18:19], A.mult, 1.0, A.add),
-                   ACT(T.dT[:, 0:768], T.dG[:, 0:768], F.Identity, scale=col[:, 18:19], bias=1.0), "dG c18", "dT")
+            ts(T.dT[:, 0:768], T.dG[:, 0:768], col[:, 18:19], A.mult, "dG c18", "dT", 1.0, A.add)
         win = "vac1 xl1 off " + xn(1)
         for q in range(4):
             mm(Pq[q][:], [one, (T.I4[:], yv[1](512 * q, 512 * q + 512))], "cb0 cb1 I4 x1_%d" % q, "P%d" % q, True, False)
         mms([(T.PK[:], T.cb[0:1, 640:768], T.cb[0:1, 0:512], True, False)] +
-            [(T.PK[:, 128 * j:128 * j + 128], l, r, False, False) for j in range(4)
-             for l, r in ((T.cb[0:1, 768:896], T.cb[0:1, 0:128]),) * j + ((T.If[:], pl(T.D, j)), (T.In[:], pl(T.vacm, j)))], "If In D vacm cb0 cb2", "PK")
+            [(T.PK[:, 128 * j:512], T.cb[0:1, 768:896], T.cb[0:1, 128 * j:512], False, False) for j in range(1, 4)], "cb0 cb2", "PK")
+        kl = [16]
+        for j in range(4):
+            more(T.PK[:, 128 * j:128 * j + 128], [(T.If[:], pl(T.D, j))], "If D", "PK", kl)
+            more(T.PK[:, 128 * j:128 * j + 128], [(T.In[:], pl(T.vacm, j))], "In vacm", "PK", kl)
         clear("PY", 256)
-        left, kl, sl = [[4] for q in range(4)], [8], [6]
+        left, sl = [[4] for q in range(4)], [6]
         for hq in range(2):
             for j in (3, 0, 1, 2):
-                c0, mode, vn, wn = 2048 * j + 1024 * hq, MODE[j, hq], "V%d%d" % (j, hq), "W%d" % (2 * j + hq)
+                c0, vn, wn = 2048 * j + 1024 * hq, "V%d%d" % (j, hq), "W%d" % (2 * j + hq)
                 src = (T.xw1[:], pl(T.off, j, 64 * hq, 64 * hq + 64))
-                if mode == "s":
+                if j == SP:
                     act(T.V[:, c0:c0 + 1024], src, F.Copy, win, vn)
                 else:
                     tt(T.V[:, c0:c0 + 1024], src, own(1024 * hq, 1024 * hq + 1024), A.subtract, win + " yp%d yp%d" % (2 * hq, 2 * hq + 1), vn)
+                    act(T.VA[:, c0:c0 + 1024], T.V[:, c0:c0 + 1024], F.Abs, vn, wn)
                 for k in range(2):
                     q, c = 2 * hq + k, slice(c0 + 512 * k, c0 + 512 * k + 512)
                     more(Pq[q][:], [(T.Ib[:], T.V[:, c])], "Ib " + vn, "P%d" % q, left[q])
-                    if mode == "s":
+                    if j == SP:
                         bank = ("PS", "PX")[k]
-                        mm(T[bank][:], [(T.Ib[:], T.V[:, c]), (T.In[:], yv[1](512 * q, 512 * q + 512))], "Ib In x1_%d " % q + vn, bank)
+                        mm(T[bank][:], [(T.In[:], yv[1](512 * q, 512 * q + 512))], "In x1_%d" % q, bank, True, False)
+                        mm(T[bank][:], [(T.Ib[:], T.V[:, c])], "Ib " + vn, bank, False, True)
                         act(T.VA[:, c], T[bank][:], F.Abs, bank, wn)
-                if mode == "va":
-                    act(T.VA[:, c0:c0 + 1024], T.V[:, c0:c0 + 1024], F.Abs, vn, wn)
-                if mode == "vr":
-                    ts(T.VA[:, c0:c0 + 1024], T.V[:, c0:c0 + 1024], 0.0, A.max, vn, wn)
-                k = T.PK[:, 128 * j + 64 * hq:128 * j + 64 * hq + 64]
-                more(k, (terms(T.Zn, lambda r: T.V[:, c0 + r:c0 + 1024:16]) if mode == "vr" else []) +
-                     terms(T.Zr if mode == "vr" else T.Zk, lambda r: T.VA[:, c0 + r:c0 + 1024:16]), "Zk Zr Zn %s %s" % (vn, wn), "PK", kl)
+                more(T.PK[:, 128 * j + 64 * hq:128 * j + 64 * hq + 64], terms(T.Zk, lambda r: T.VA[:, c0 + r:c0 + 1024:16]), "Zk " + wn, "PK", kl)
             for q in (2 * hq, 2 * hq + 1):
                 mod16(0, q)
                 more(T.PY[:, 128:256], [(T.Zb[:, 15 - r:143 - r], yv[0](128 * r, 128 * r + 128)) for r in range(4 * q, 4 * q + 4)], "Zb x0_%d" % q, "PY", sl)
             more(T.PY[:, 64 * hq:64 * hq + 64], terms(T.Zb, lambda r: yv[0](1024 * hq + r, 1024 * hq + 1024, 16)), "Zb x0_%d x0_%d" % (2 * hq, 2 * hq + 1), "PY", sl)
-        ts(T.lostB[:], T.PY[:, 128:256], lo, A.is_lt, "PY pc2", "lostB")
-        ts(T.keepB[:], T.PY[:, 128:256], lo, A.is_ge, "PY pc2", "keepB", 64.0, A.mult)
+        SB, SL = T.PY[:, 128:256], T.PY[:, 0:128]
+        either(TS(T.lostB[:], SB, lo, A.is_lt), ACT(T.lostB[:], SB, F.Relu, scale=-1.0, bias=lo), "PY pc2", "lostB")
+        either(TS(T.keepB[:], SB, lo, A.is_ge, 64.0, A.mult), ACT(T.keepB[:], SB, F.Relu, scale=64.0, bias=pc[:, 11:12]), "PY pc2 pc3", "keepB")
         for q in range(4):
             mms([(Pq[q][:], T.Ib[:], yv[0](512 * q, 512 * q + 512), True, False)] +
                 [(Pq[q][:, 128 * c:128 * c + 128], T.RV[:, 128 * (4 * q + c):128 * (4 * q + c) + 128], T.lostB[:], False, c == 3) for c in range(4)],
                 "Ib RV lostB x0_%d" % q, "P%d" % q)
             o = own(512 * q, 512 * q + 512)
             either(TS(o, Pq[q][:], 0.0, A.max), ACT(o, Pq[q][:], F.Relu), "P%d" % q, "yp%d" % q)
-        move(T.snd[:, 0:768], (T.xw0[:, 0:Y0 + 2048], T.oN[:]), "oN vac " + YP + " " + xn(0), "snd")
-        exchange(T.snd, 0, T.xw0, Y0 + 2048, 1, "snd", "xl0")
+        send(T.xw0[:, 0:Y0 + 2048], "vac " + YP + " " + xn(0), T.xw0, Y0 + 2048, "xl0")
         move(T.f1[:], T.PK[:, 0:256], "PK", "f1")
         tt(T.km[:], T.PK[:, 256:512], T.f1[:], A.max, "PK f1", "km")
-        ts(T.hiF[:], T.PY[:, 0:128], hi, A.is_ge, "PY pc2", "hiF")
-        ts(T.thr[:], T.PY[:, 0:128], th, A.is_lt, "PY pc2", "thr", 63.5, A.mult)
+        either(TS(T.hiF[:], SL, hi, A.is_ge, 2.0 ** 25, A.mult), ACT(T.hiF[:], SL, F.Relu, scale=2.0 ** 25, bias=pc[:, 12:13]), "PY pc2 pc3", "hiF")
+        either(TS(T.thr[:], SL, th, A.is_lt), ACT(T.thr[:], SL, F.Relu, scale=-1.0, bias=th), "PY pc2", "thr")
         tt(T.km[:, 0:128], T.km[:, 0:128], T.km[:, 128:256], A.max, "km", "km")
-        tt(T.mg[:], T.km[:, 0:128], T.hiF[:], A.mult, "km hiF", "mg")
+        tt(T.mg[:], T.km[:, 0:128], T.hiF[:], A.min, "km hiF", "mg")
         tt(T.i1[:, 0:128], T.mg[:], T.dumK[:, 0:128], A.max, "mg dumK", "i1")
         ts(T.i1[:, 0:128], T.i1[:, 0:128], 16383, AND, "i1", "i1")
         cp(T.oK[:], T.i1[:, 0:128], "i1", "oK")
@@ -655,7 +734,7 @@ def rank_program(g, core, T, topo):
         for k in range(8):
             prefetch(k, T.xw0[:], T.ofp[:, 64 * k:64 * k + 64], "vac xl0 ofp " + YP + " " + xn(0))
             more(T.PS[:, 64 * k:64 * k + 64], terms(T.Zq, lambda r: T.VA[:, 1024 * k + r:1024 * k + 1024:16]), "Zq W%d" % k, "PS", left)
-        conv(T.PY[:, 0:48], T.Zq, lambda r: T.snd[:, r:768:16], "Zq snd", "PY")
+        conv(T.PY[:, 0:48], T.Zq, lambda r: T.snd[:, r:768:16], "Zq snd snd1", "PY")
         tt(T.D[:, LK], T.PY[:, 0:48], T.D[:, LK], A.min, "PY DL", "DL")
         conv(T.PY[:, 48:96], T.Zq, lambda r: T.xw0[:, Y0 + 2048 + r:Y0 + 2816:16], "Zq xl0", "PY")
         ts(T.alive[:], T.PY[:, 48:96], 1.0, A.is_ge, "PY", "alive")
@@ -663,20 +742,19 @@ def rank_program(g, core, T, topo):
         scan(T.cumG[:, 1:49], T.flG[:, 0:48], T.flG[:, 0:48], 0.0, A.add, A.max, "flG0", "cumGa cumG")
         mm(T.PY[:, 0:48], [(T.BOh[:], T.cumG[:, 0:48]), (T.TRI[:], T.flG[:, 0:48])], "BOh TRI cumG0 cumGa flG0", "PY")
         mm(T.PY[:, 48:49], [(T.BOh[:], T.cumG[:, 48:49])], "BOh cumGa", "PY")
-        cp(T.g1[:, 0:49], T.PY[:, 0:49], "PY", "g1")
+        move(T.g1[:, 0:49], T.PY[:, 0:49], "PY", "g1")
         nL = T.g1[:, 48:49]
         if not last:
             conv(T.PY[:, 0:48], T.Zq, lambda r: T.snd[:, 768 + r:1536:16], "Zq msS", "PY")
             tt(T.held[:], T.alive[:], T.held[:], A.mult, "alive held", "held")
             tt(T.held[:], T.PY[:, 0:48], T.held[:], A.min, "PY held", "held")
-        if last:
+        if t == RO - 2:
             move(T.dG[:, 0:768], T.msR[:], "msR", "dG")
             tt((T.AX[:], T.oL[:]), T.dG[:, 0:768], T.dT[:, 0:768], A.mult, "oL dG dT", "AX")
+            iota(T.dT[:, 0:768], [[0, 768]], 64, 0, "dT")
         else:
             cp((T.AX[:], T.oL[:]), T.msR[:], "oL msR", "AX")
         dma([(T.Fb[:], T.AX[row1, 64:8256])], "AX", "Fb", 256)
-        if last:
-            dma([(T.Eb[:], T.AX[row, 64:8256])], "AX", "Eb", 512)
         conv(T.PY[:, 0:48], T.Zq, lambda r: T.msR[:, r:768:16], "Zq msR", "PY")
         tt(T.D[:, LK], T.PY[:, 0:48], T.D[:, LK], A.min, "PY DL", "DL")
         if not last:
@@ -684,7 +762,7 @@ def rank_program(g, core, T, topo):
         ts(T.isL[:], T.gam[:], nL, A.is_lt, "gam gam2 g1", "isL")
         ts(T.flE[:, 128:144], T.D[:, 128 + 16 * t:144 + 16 * t], 63.5, A.is_lt, "DL flE", "flEL")
         mms([(T.P1[:, b:64:4], T.Qh[:, 144 * b + 3:144 * b + 131], T.flE[:, 128:144], True, True) for b in range(4)], "Qh flEL", "P1")
-        cp(T.flT[:, 528:592], T.P1[:, 0:64], "P1", "flT2")
+        move(T.flT[:, 528:592], T.P1[:, 0:64], "P1", "flT2")
         tt(T.Fb[:, t:512:4], T.Fb[:, t:512:4], T.keepB[:], A.min, "Fb keepB", "Fb")
         tt(T.TG[:, 512:1024], (T.Fb[:], T.oJ[:, 0:32]), T.TG[:, 0:512], A.mult, "Fb oJ Tt", "Gj lost0 lost1 lost2 lost3")
         if not last:
@@ -701,12 +779,10 @@ def rank_program(g, core, T, topo):
         counts(T.flG, "flG0 flG1", 560, 512, T.wb, "wb", "P2", "P3")
         move((T.Lb[:], T.ob[:, 0:35]), T.wb[:, 0:560], "ob wb wb1", "Lb")
         mm(T.PK[:, 256:257], [(T.BOh[:], T.cumG[:, 560:561])], "BOh cumG", "PK")
-        cp(col[:, 5:6], T.PK[:, 256:257], "PK", "c5")
-        run_down(T.Lb, "Lb", T.cwb, "cwb", 0, 1088, 64.0)
-        ts(T.cwb[:], T.cwb[:], pf[:, 10:11], A.min, "cwb pf10", "cwb")
+        move(col[:, 5:6], T.PK[:, 256:257], "PK", "c5")
+        run_down(T.Lb, "Lb", T.cwb, "cwb", 1088)
         back = [(T.cb[0:1, 0:128], T.cb[0:1, 896:964])]
         mm(T.PK[:, 64:132], back + terms(T.Zc, lambda r: T.cwb[:, r:1088:16]), "cb0 cb6 Zc cwb", "PK")
-        mm(T.PK[:, 132:200], back + terms(T.Zc, lambda r: T.cwb[:, 68 * r:68 * r + 68]), "cb0 cb6 Zc cwb", "PK")
         for j in range(4):
             tt(T.flE[:, 144 * j:144 * j + 128], T.PS[:, 128 * j:128 * j + 128], T.thr[:], A.is_lt, "PS thr flE", "flP%d" % j)
         for j in range(4):
@@ -714,12 +790,12 @@ def rank_program(g, core, T, topo):
         FP = "flP0 flP1 flP2 flP3"
         for b in range(4):
             mm(T.P0[:, b:512:4], [(T.Qh[:, 144 * b + 3 - j:144 * b + 131 - j], T.flE[:, 144 * j:144 * j + 128]) for j in range(4)], "Qh " + FP, "P0")
-        cp(T.flT[:, 0:512], T.P0[:], "P0", "flT0")
+        move(T.flT[:, 0:512], T.P0[:], "P0", "flT0")
         scan(T.cumT[:, 1:513], T.flT[:, 0:512], T.flT[:, 0:512], 0.0, A.add, A.max, "flT0", "cumT")
         mm(T.PY[:, 0:1], [(T.BOh[:], T.cumT[:, 512:513])], "BOh cumT", "PY")
         ts(col[:, 1:2], T.PY[:, 0:1], 1024.0, A.min, "PY g1", "c1", nL, A.max)
         ts(col[:, 0:1], T.PY[:, 0:1], 1024.0, A.min, "PY", "c0")
-        ts(col[:, 4:5], T.PY[:, 0:1], 1024.0, A.is_le, "PY", "c4")
+        ts(col[:, 4:5], T.PY[:, 0:1], 1024.0, A.is_gt, "PY", "c4", 64.0, A.mult)
         ts(col[:, 3:4], col[:, 1:2], pf[:, 7:8], A.mult, "c1 pf7", "c3")
         scan(T.cumT[:, 513:593], T.flT[:, 512:592], T.flT[:, 512:592], col[:, 3:4], A.add, A.max, "flT1 flT2 c3", "cumTa")
         heads(T.cumT, "cumT cumT0 cumTa", 592, T.CL[:, 0:74], T.sea, "sea", T.oa, "oa", "PX")
@@ -729,15 +805,17 @@ def rank_program(g, core, T, topo):
         ts(col[:, 6:7], col[:, 1:2], 64.0, A.add, "c1", "c6")
         ts(col[:, 2:3], T.PY[:, 0:1], col[:, 6:7], A.min, "PY c6", "c2")
         ts(col[:, 8:11], col[:, 0:3], col[:, 5:6], A.min, "c0 c1 c2 c5", "c8")
-        run_down(T.La, "La", T.cwa, "cwa", 0, 1024, 64.0)
-        ts(col[:, 7:8], T.cwa[:, 1023:1024], col[:, 4:5], A.mult, "cwa c4", "c7")
-        run_down(T.La, "La", T.cwa, "cwa1", 1024, 1088, col[:, 7:8], "c7")
-        ts(T.cwa[:], T.cwa[:], pf[:, 10:11], A.min, "cwa cwa1 pf10", "cwa cwa1")
-        ts(T.j1[:], T.PK[:, 64:200], K, A.mult, "PK pc", "j1", C, A.add)
+        ts(T.DEC[:, 1096:1097], col[:, 4:5], 1.0, A.add, "c4 pf11", "DEC2", pf[:, 11:12], A.mult)
+        run_down(T.La, "La", T.cwa, "cwa", 1088, 72, "DEC2")
+        CK = pc[:, 13 + t:14 + t]
+        ts(T.j1[:, 0:68], T.PK[:, 64:132], K, A.mult, "PK pc pc4", "j1", CK, A.add)
+        ts(T.f2[:, 0:64], T.PK[:, 64:128], 2815.0, A.add, "PK", "f2")
+        mm(T.PK[:, 132:200], back + terms(T.Zc, lambda r: T.cwb[:, 68 * r:68 * r + 68]), "cb0 cb6 Zc cwb", "PK")
+        ts(T.j1[:, 68:136], T.PK[:, 132:200], K, A.mult, "PK pc pc4", "j1b", CK, A.add)
         if not last:
             dma([(T.UA[row, :], T.D[:])], "D DL", "UA", 360)
-            iota(T.Lb[:, 0:1088], [[0, 1088]], 64, 0, "Lb")
-            iota(T.La[:, 0:1088], [[0, 1088]], 64, 0, "La")
+            refill(T.Lb, "Lb")
+            refill(T.La, "La")
             for k, TR in enumerate((T.TRI, T.TRs)):
                 mm(T.PY[:, 128 + 128 * k:256 + 128 * k], [(T.BOh[:], T.cumT[:, 0:512:4])] +
                    [(TR[:], T.flE[:, 144 * j:144 * j + 128]) for j in range(4)], "BOh TRI TRs cumT cumT0 " + FP, "PY")
@@ -752,28 +830,29 @@ def rank_program(g, core, T, topo):
                 either(TS(o, p, 0.0, A.is_equal), ACT(o, p, F.Relu, scale=-1.0, bias=1.0), bank, ("Tt", "Gj")[k])
             left = [sums(q, False) for q in range(4)]
             ts(T.pre[:], T.gam[:, 0:64], col[:, 5:6], A.is_ge, "gam c5", "pre", float(W0 - 32 - PL), A.mult)
-            ts(T.f2[:, 0:64], T.PK[:, 64:128], 2816.0, A.add, "PK", "f2")
             ts(T.j2[:, 0:64], T.j1[:, 0:64], 2, SH, "j1", "j20 j21", 2047, AND)
             tt(T.f2[:, 0:64], T.f2[:, 0:64], T.isL[:, 0:64], A.mult, "f2 isL", "f2")
             tt(T.f2[:, 0:64], T.f2[:, 0:64], T.pre[:], A.max, "f2 pre", "f2")
             tt(T.f2[:, 0:64], T.f2[:, 0:64], T.j2[:, 0:64], A.max, "f2 j20 j21", "f2")
             ts(T.oS[:], T.f2[:, 0:64], 16.0, A.add, "f2", "oS")
-            move(T.M[:], (T.xw0[:, PL:W0], T.oS[:]), "oS vac xl0 " + xn(0), "rr0 rr1")
-            scan(T.xw0[:, 16:1040], T.TG[:], T.M[:], 0.0, A.mult, A.add, "Tt Gj rr0 rr1", "yp0 yp1")
             for k in range(2):
-                move(T.V[:, 1024 * k:1024 * k + 1024], (T.xw0[:, 0:1040], T.oE[:, 64 * k:64 * k + 64]), "yp0 yp1 vac oE", "V0%d" % k)
+                move(T.M[:, 512 * k:512 * k + 512], (T.xw0[:, PL:W0], T.oS[:, 32 * k:32 * k + 32]), "oS vac xl0 " + xn(0), "rr%d" % k)
+            scan(T.xw0[:, 16:1040], T.TG[:], T.M[:], 0.0, A.mult, A.add, "Tt Gj rr0 rr1", "yp0 yp1")
             for q in range(4):
-                more(Pq[q][:], [(T.Ib[:], T.V[:, 512 * q:512 * q + 512])], "Ib V0%d" % (q // 2), "P%d" % q, left[q])
+                c, vn = T.V[:, 1024 * q:1024 * q + 512], "V%d%d" % (q // 2, q % 2)
+                move(c, (T.xw0[:, 0:1040], T.oE[:, 32 * q:32 * q + 32]), "yp0 yp1 vac oE", vn)
+                more(Pq[q][:], [(T.Ib[:], c)], "Ib " + vn, "P%d" % q, left[q])
         conv(T.PX[:, 128:196], T.Zt if last else T.Zc, lambda r: T.cwa[:, r:1088:16], "Zc Zt cwa", "PX")
         conv(T.PX[:, 196:264], T.Zc, lambda r: T.cwa[:, 68 * r:68 * r + 68], "Zc cwa", "PX")
-        ts(T.g2[:, 0:68], T.PK[:, 132:200], 4.0, A.mult, "PK", "g2", 11264.0, A.add)
-        ts(T.j1[:], T.j1[:], 8191, AND, "j1", "j1")
+        ts(T.g2[:, 0:68], T.PK[:, 132:200], 4.0, A.mult, "PK", "g2", 11260.0, A.add)
+        ts(T.j1[:, 68:136], T.j1[:, 68:136], 8191, AND, "j1b", "j1b")
+        ts(T.j1[:, 0:68], T.j1[:, 0:68], 8191, AND, "j1", "j1")
         tt(T.g2[:, 0:68], T.g2[:, 0:68], T.isL[:, 68:136], A.mult, "g2 isL", "g2")
-        tt(T.valG[:], T.g2[:, 0:68], T.j1[:, 68:136], A.max, "g2 j1", "valG")
+        tt(T.valG[:], T.g2[:, 0:68], T.j1[:, 68:136], A.max, "g2 j1b", "valG")
         if not last:
             plus(T.valG[:], T.valG[:], 64.0, "valG", "valG")
         dma([(T.dG[row, :], T.valG[:])], "valG", "dG dG1", 40)
-        plus(T.valT[:], T.PX[:, 196:264], -64.0 if last else 0.0, "PX", "valT")
+        plus(T.valT[:], T.PX[:, 196:264], -65.0 if last else -1.0, "PX", "valT")
         dma([(T.dT[row, :], T.valT[:])], "valT", "dT", 40)
         inv, invX = T.inv[:, 0:68], T.inv[:, 68:136]
         ts(inv, T.gam[:, 0:68], col[:, 8:9], A.is_ge, "gam c8", "inv")
@@ -782,7 +861,7 @@ def rank_program(g, core, T, topo):
         tt(invX, inv, T.f2[:, 68:136], A.mult, "inv f2b", "invX")
         tt(invX, invX, T.f5[:, 0:68], A.max, "invX f5", "invX")
         if not last:
-            ts(T.i1[:, 0:68], T.PX[:, 128:196], -64.0, A.add, "PX", "i1")
+            ts(T.i1[:, 0:68], T.PX[:, 128:196], -65.0, A.add, "PX", "i1")
             place(T.i1[:, 0:68], "i1", 68, T.posT[:], "posT")
             pick(T.posT[:], "posT", invX, "invX", T.dumA[:, 0:68], 68, T.oT[:], "oT")
             move((T.UA[:], T.oT[:]), T.dG[:], "oT dG dG1", "UA")
@@ -797,24 +876,21 @@ def rank_program(g, core, T, topo):
             tt(T.held[:], T.held[:], T.f4[:, 0:48], A.add, "held f4", "held")
         else:
             ts(T.dA[:], T.gam[:, 0:68], 8448.0, A.add, "gam", "dA")
-            ts(T.posT[:], T.PX[:, 128:196], 512.0 * 960 - 64, A.add, "PX", "posT")
+            ts(T.posT[:], T.PX[:, 128:196], 16.0 * 15 * 32800 - 965, A.add, "PX", "posT")
             tt(T.dX[:], T.dA[:], inv, A.mult, "dA inv", "dX")
             tt(T.posT[:], T.posT[:], T.dX[:], A.max, "posT dX", "posT")
             cp(T.oT[:], T.posT[:], "posT", "oT")
             ts(T.AI[:], T.D[:], -64.0, A.add, "D DL", "AI AI0 AI1 AI2 AI3", -1.0, A.max)
-            cp(T.Pf[:], T.Qh[:], "Qh", "Pf")
+            move(T.Pf[:], T.Qh[:], "Qh", "Pf")
             cp(T.D[:], T.AI[:], "AI", "D DL")
             for b in range(4):
                 mm(T.PS[:, b:512:4], [(T.Pf[:, 144 * b + 3 - j:144 * b + 131 - j], pl(T.D, j)) for j in range(4)], "Pf D", "PS")
             move(T.D[:, 0:512], T.PS[:], "PS", "D DL")
-            iota(T.km[:, 0:64], [[16, 32], [0, 2]], 0, 0, "km")
-            iota(T.km[:, 64:96], [[1, 16], [512, 2]], 0, 0, "km")
-            ts(pf[:, 22:23], pf[:, 1:2], 31.0, A.mult, "pfa", "pf22", pf[:, 5:6], A.add)
-            ts(T.lpre[:], T.km[:, 0:64], pf[:, 1:2], A.add, "km pfa", "lpre")
-            ts(T.lpost[:], T.km[:, 64:96], pf[:, 22:23], A.add, "km pf22", "lpost")
-            tt(T.Eb[:], T.Eb[:], T.Fb[:], A.mult, "Eb Fb", "Eb")
-            ts(T.axoi[:], T.Eb[:], 1.0 / 64, A.mult, "Eb", "axoi", -64.0, A.add)
-            turn(T.Eb[:], "Eb", T.UA[:, 8192:9216], "UA", T.UA[:, 9216:10240], "UAb", -1.0, A.max)
+            ta, tb = T.V[:, 4096:5120], T.V[:, 6144:7168]
+            move(ta, (T.Fb[:], T.lpre[:]), "Fb lpre", "V20")
+            turned(tb, ta, "V20", "V30")
+            either(TS(T.Fb[:], (tb, T.lpost[:]), 256.0, A.mult, -1.0, A.add), ACT(T.Fb[:], (tb, T.lpost[:]), F.Identity, scale=256.0, bias=-1.0), "V30 lpost", "Fb")
+            tt(T.Eb[:], T.Eb[:], T.Fb[:], A.min, "Eb Fb", "Eb")
             dma([(T.UA[row, 0:8192], T.D[:, 0:512])], "D", "UAn", 256)
             dma([(T.AX[row, 0:8192], T.Eb[:])], "Eb", "AX", 256)
             tt(invX, invX, T.isL[:, 0:68], A.max, "invX isL", "invX")
@@ -827,7 +903,7 @@ def rank_program(g, core, T, topo):
             cp(T.oG[:], T.f2[:, 0:68], "f2", "oG")
             cp((T.AX[:], T.oG[:]), T.dT[:], "oG dT", "AX")
             dma([(T.ya[:], T.AX[row, 0:8192])], "AX", "", 256)
-            cp((T.UA[:], T.oT[:]), T.dG[:], "oT dG dG1", "UA UAb UAn")
+            cp((T.UA[:], T.oT[:, 0:64]), T.dG[:, 0:1024], "oT dG dG1", "UA UAb UAn")
             dma([(T.yd[:], T.UA[row, 0:8192])], "UA", "", 256, q="s")
 
     if "order" not in PLAN:

@@ -5,9 +5,9 @@ from concourse.mybir import AluOpType as A, ActivationFunctionType as F
 N, RO = 4, 3
 W0, W1 = 4912, 2832
 PL = 2064
-UAW, AXW, L1W = 11264, 11328, 1680
+UAW, AXW, L1W = 11264, 11392, 1680
 SP = 3
-PASSES, STARTS, HEAT = 2500, 3, 0.1
+PASSES, STARTS, HEAT = 6000, 1, 0.001
 f32, bf, f16, i32, u16 = "float32", "bfloat16", "float16", "int32", "uint16"
 
 
@@ -23,11 +23,11 @@ SCRATCH = {
     "off": sb(704, u16), "ofp": sb(512, u16), "M": sb(1024, bf), "msR": sb(768, bf), "TG": sb(1024, bf),
     "Fb": sb(512, f32), "Eb": sb(512, f32), "RV": sb(2048, bf),
     "axoi": sb(512, i32), "pari": sb(8, i32), "parf": sb(8, f32), "pc": sb(16, f32),
-    "flT": sb(592, bf), "flG": sb(560, bf), "flE": sb(576, bf), "cumT": sb(608, f16), "cumG": sb(576, f16),
+    "flT": sb(592, bf), "flG": sb(560, bf), "flE": sb(528, bf), "cumT": sb(608, f16), "cumG": sb(576, f16),
     "km": sb(256, f32), "held": sb(48, f32), "alive": sb(48, f32),
     "i1": sb(136, i32), "i2": sb(136, i32), "j1": sb(136, i32), "j2": sb(136, i32),
     "f1": sb(256, f32), "f2": sb(136, f32), "f3": sb(136, f32), "f4": sb(136, f32), "f5": sb(136, f32), "g1": sb(136, f32), "g2": sb(136, f32),
-    "mg": sb(128, f32), "thr": sb(128, f32), "hiF": sb(128, f32), "lostB": sb(128, bf), "keepB": sb(128, f32),
+    "mg": sb(128, f32), "thr": sb(128, bf), "hiF": sb(128, f32), "lostB": sb(128, bf), "keepB": sb(128, f32),
     "oK": sb(128, u16), "oL": sb(48, u16), "oN": sb(48, u16), "oa": sb(40, u16), "ob": sb(40, u16), "oT": sb(68, u16), "oG": sb(68, u16),
     "oS": sb(64, u16), "oE": sb(128, u16), "oJ": sb(64, u16), "lpre": sb(64, u16), "lpost": sb(32, u16),
     "sea": sb(80, f32), "seb": sb(80, f32), "posT": sb(68, f32), "valT": sb(68, f32), "valG": sb(68, f32),
@@ -35,7 +35,7 @@ SCRATCH = {
     "col": sb(24, f32), "pi": sb(8, i32), "pf": sb(28, f32), "yrow": sb(144, f32),
     "Zb": sb(144, bf), "Zk": sb(144, bf), "Zp": sb(288, bf), "Zq": sb(144, bf),
     "Zh": sb(144, f16), "Zc": sb(144, f16), "Zt": sb(144, f16),
-    "Ib": sb(128, bf), "I4": sb(128, bf), "In": sb(128, bf), "Ig": sb(128, bf), "If": sb(128, f32),
+    "Ib": sb(128, bf), "I4": sb(128, bf), "I8": sb(128, bf), "In": sb(128, bf), "Ig": sb(128, bf), "If": sb(128, f32),
     "BOh": sb(128, f16), "TRI": sb(128, bf), "TRp": sb(128, bf), "TRs": sb(128, bf), "TRe": sb(128, bf), "Ie": sb(128, f16),
     "Wv": sb(256, f16), "Pf": sb(576, f32), "Qh": sb(576, bf), "cb": sb(976, bf), "ch": sb(832, f16), "Ut": sb(16, bf),
     "Dc": sb(40, f32), "CL": sb(80, f32), "gam": sb(136, f32), "dumA": sb(144, f32), "dumK": sb(144, f32),
@@ -43,12 +43,16 @@ SCRATCH = {
 for _k in ("P0", "P1", "P2", "P3", "PK", "PS", "PX", "PY"):
     SCRATCH[_k] = ("psum", [128, 512], f32)
 SEMAPHORES = ["qv", "qs", "qt", "qg"] + ["d%d" % k for k in range(40)] + ["ar%d" % k for k in range(10)] + ["lo%d" % k for k in range(10)]
-CY, GA, SC, PE, WAKE, NEAR = 0.9e-3, 1.56, 3.8, 0.5e-3, 0.12, 0.05
+CY, GA, SC, PE, WK, DM = (np.array(x) for x in ((.97e-3, .83e-3, 1.1e-3, 1.15e-3, .95e-3), (1.65, 1.45, 1.75, 1.9, 1.4), (4.1, 3.5, 5.3, 2.7, 4.8),
+                                                (.5e-3, .417e-3, .55e-3, .58e-3, .48e-3), (.14, .2, .11, .11, .1), (1., .9, 1.1, 1., 1.)))
+WAKE = float(WK[0])
 PLAN = {}
 
 
 def schedule(ops):
     n = len(ops)
+    each = [[{q: (float((b + 0 * WK)[k]), float((l + 0 * WK)[k])) for q, (b, l) in o[1].items()} for o in ops] for k in range(len(WK))]
+    ops = [(o[0], e) for o, e in zip(ops, each[0])]
     pred, succ = [o[0] for o in ops], [[] for _ in ops]
     for i in range(n):
         for p in pred[i]:
@@ -67,9 +71,9 @@ def schedule(ops):
             for q, (b, l) in ops[i][1].items():
                 if fixed and q != fixed[i]:
                     continue
-                est, near = 0.0, 0.0 if q == "t" else NEAR
+                est = 0.0
                 for p in pre[i]:
-                    e = fin[p] + (near if where[p] == q else WAKE)
+                    e = fin[p] if q == "t" == where[p] else fin[p] + WAKE
                     if e > est:
                         est = e
                 if fixed:
@@ -98,24 +102,31 @@ def schedule(ops):
                 ready.sort()
         return max(fin), fin, where
 
-    def tight(s):
-        fin, where = s[1], s[2]
-        st = [fin[i] - sum(ops[i][1][where[i]]) for i in range(n)]
-        before, last = [-1] * n, {}
-        for i in sorted(range(n), key=lambda i: st[i]):
-            before[i] = last.get(where[i], -1)
-            last[where[i]] = i
-        out, i = [], fin.index(s[0])
-        while i >= 0:
-            a, p = before[i], max(pred[i], key=lambda p: fin[p], default=-1)
-            if a >= 0 and a not in pred[i] and (p < 0 or st[a] + ops[a][1][where[a]][0] > fin[p] + 0.02):
-                out.append((a, i))
-                i = a
-            else:
-                if len(ops[i][1]) > 1:
+    def judge(s):
+        where, total, out = s[2], 0.0, []
+        order = sorted(range(n), key=lambda i: (s[1][i] - sum(ops[i][1][where[i]]), i))
+        for k in range(1, len(WK)):
+            fin, why, free, prev, wake, cost = [0.0] * n, [-1] * n, dict.fromkeys("vstgy", 0.0), dict.fromkeys("vstgy", -1), float(WK[k]), each[k]
+            for i in order:
+                q = where[i]
+                st, w = free[q], prev[q]
+                for p in pred[i]:
+                    e = fin[p] if q == "t" == where[p] else fin[p] + wake
+                    if e >= st:
+                        st, w = e, p
+                b, l = cost[i][q]
+                free[q], prev[q], fin[i], why[i] = st + b, i, st + b + l, w
+            end = max(fin)
+            total += end / unit.setdefault(k, end)
+            i = fin.index(end)
+            while why[i] >= 0:
+                if why[i] not in pred[i]:
+                    out.append((why[i], i))
+                elif len(cost[i]) > 1:
                     out.append((i, i))
-                i = p
-        return out
+                i = why[i]
+        return total, order, out
+    unit = {}
     prio0, pen0 = level, [1.0] * n
     best = now = one(prio0, pen0, pred, succ, None)
     for k in range(12):
@@ -123,13 +134,13 @@ def schedule(ops):
         now = one(p2, pen0, pred, succ, None)
         if now[0] < best[0]:
             best, prio0 = now, p2
-    first = best
+    first, top = best, judge(best)
+    best = (top, best)
     for seed in range(1, STARTS + 1):
         rng = np.random.default_rng(seed)
-        now, prio, pen = first, prio0, pen0
-        path = tight(now)
+        now, prio, pen, val = first, prio0, pen0, top
         for k in range(PASSES):
-            p2, e2 = list(prio), list(pen)
+            p2, e2, path = list(prio), list(pen), val[2]
             for z in range(1 + (k % 3 == 0)):
                 a, b = path[int(rng.random() * len(path))]
                 u = rng.random()
@@ -145,13 +156,12 @@ def schedule(ops):
                         p2[x] += up
                         todo += [y for y in pred[x] if y not in todo and now[1][y] > now[1][b] - 6.0]
             got = one(p2, e2, pred, succ, None)
-            if got[0] <= now[0] + HEAT * (1.0 - k / PASSES) * rng.random():
-                now, prio, pen = got, p2, e2
-                path = tight(now)
-                if got[0] < best[0]:
-                    best = got
-    best = (best[0], [(best[1][i] - sum(ops[i][1][best[2][i]]), i, best[2][i]) for i in range(n)])
-    return [(i, q) for st, i, q in sorted(best[1])]
+            new = judge(got)
+            if new[0] <= val[0] + HEAT * (1.0 - k / PASSES) * rng.random():
+                now, prio, pen, val = got, p2, e2, new
+                if new[0] < best[0][0]:
+                    best = (new, got)
+    return [(i, best[1][2][i]) for i in best[0][1]]
 
 
 def rank_program(g, core, T, topo):
@@ -238,7 +248,7 @@ def rank_program(g, core, T, topo):
         record({**x, **y}, R, W)
 
     def move(out, a, R, W):
-        either(CP(out, a), ACT(out, a, F.Silu if isinstance(out, tuple) else F.Copy), R, W)
+        either(CP(out, a), ACT(out, a, F.Silu if isinstance(out, tuple) else F.Copy), R + " silu" * isinstance(out, tuple), W)
 
     def copy3(out, a, R, W):
         n = out.shape[1]
@@ -291,21 +301,24 @@ def rank_program(g, core, T, topo):
             for o, i in pairs:
                 Q[q].dma_start(o, i).then_inc(T.sem[s], 16)
             return [(s, 16 * len(pairs))]
-        record({q: (0.05 * len(pairs), 2.0 + kb / 200.0, call)}, R, W)
+        record({q: (0.05 * len(pairs), (2.0 + kb / 200.0) * DM, call)}, R, W)
 
     def engines_of(src):
         peers = [c for c in T.cores if c != src]
         far = [c for c in peers if topo.chip(c) != topo.chip(src)]
         near = [c for c in peers if topo.chip(c) == topo.chip(src)]
         out, used = {}, set()
-        for grp in (far, near):
-            for k, c in enumerate(grp):
-                free = [e for e in topo.engines(src, c) if e not in used]
-                n = len(free) // (len(grp) - k)
-                while n & (n - 1):
-                    n -= 1
-                out[c] = free[:n]
-                used.update(free[:n])
+        for k, c in enumerate(far):
+            free = [e for e in topo.engines(src, c) if e not in used]
+            n = len(free) // (len(far) - k)
+            while n & (n - 1):
+                n -= 1
+            out[c] = free[:n]
+            used.update(free[:n])
+        for c in near:
+            free = [e for e in topo.engines(src, c) if e not in used]
+            out[c] = free[::len(free) // n][:n]
+            used.update(out[c])
         return out
 
     def exchange(src, s0, dst, d0, sign, R, W):
@@ -324,7 +337,7 @@ def rank_program(g, core, T, topo):
                 arr += len(engines_of(c)[core])
             g.remote_dma_fused(tr, local_sem=T.sem["lo%d" % k])
             return [("lo%d" % k, tot), ("ar%d" % k, arr)]
-        record({"g": (0.6 + 3.0 * (k == 0), 4.5, call)}, R, W)
+        record({"g": (0.6 + 3.0 * (k == 0), 4.5 * DM, call)}, R, W)
 
     def terms(Z, rhs):
         return [(Z[:, 15 - r:143 - r], rhs(r)) for r in range(16)]
@@ -340,6 +353,7 @@ def rank_program(g, core, T, topo):
     yv = [lambda a, b, s=1: T.xw0[:, Y0 + a:Y0 + b:s], lambda a, b, s=1: T.xw1[:, 16 + a:16 + b:s]]
     YP = "yp0 yp1 yp2 yp3"
     LK = slice(128, 176)
+    AXL = T.AX[:, 8256:11328:4]
     one = (T.cb[0:1, 512:640], T.cb[0:1, 0:512])
     sel15 = T.ch[0:1, 704:832]
 
@@ -361,7 +375,7 @@ def rank_program(g, core, T, topo):
 
     dma([(T.axoi[:], T.axo[:])], "", "axoi", 256)
     dma([(T.AI[:, 0:512], T.den[:])], "", "AI", 512, q="s")
-    dma([(T.V[:, 0:2048], T.x0[:])], "", "V00 V01", 1024)
+    dma([(yv[0](0, 2048), T.x0[:])], "", xn(0), 1024)
     dma([(T.pari[0:8, 0:7], T.par[:])], "", "pari", 0, q="s")
     iota(T.pi[:, 0:1], [[0, 1]], 0, 1, "pi0", flt=False)
     iota(T.yrow[:], [[1, 144]], 0, 0, "yrow")
@@ -371,8 +385,8 @@ def rank_program(g, core, T, topo):
     iota(T.dumK[:], [[4, 48], [1, 3]], 8257, 0, "dumK")
     iota(T.hiF[0:8, :], [[1, 8], [0, 16]], 0, -1, "hiF")
     iota(T.RV[:], [[0, 2048]], -32, 0, "RV")
-    record({"g": (3.9, 0.0, lambda: g.affine_select(T.RV[:], T.RV[:], [[-1, 16], [-16, 8], [0, 16]], A.is_equal, 0.0, 0, 1))}, "RV", "RV")
-    iota(T.AX[:, 8256:AXW:4], [[0, 768]], 64, 0, "AXl")
+    record({"g": (0.17 + 4096 * CY, 0.0, lambda: g.affine_select(T.RV[:], T.RV[:], [[-1, 16], [-16, 8], [0, 16]], A.is_equal, 0.0, 0, 1))}, "RV", "RV")
+    iota(AXL, [[0, 768]], 64, 0, "AXl")
     ms(T.zer[:], 0.0, "zer")
     iota(T.dT[:], [[0, 1088]], 64, 0, "dT")
     ts(T.pi[:, 1:2], T.pi[:, 0:1], 15, AND, "pi0", "pi1")
@@ -404,7 +418,7 @@ def rank_program(g, core, T, topo):
     ms(T.ch[0:32, 704:832], 0.0, "ch2")
     ms(T.ch[0:32, 719:832:16], 1.0, "ch2")
     ts(T.Dc[:], T.gam[:, 0:40], 1088.0, A.add, "gam", "Dc")
-    zero(T.Lb[:, 0:768], "Lb")
+    record({"s": (1.4 + 768 * CY, 0.0, lambda: g.scalar.activation(T.Lb[:, 0:768], T.zer[:, 0:768], F.Silu))}, "zer", "Lb silu")
     plus(T.DEC[:, 0:1024], T.zer[:], pf[:, 11:12], "zer pf11", "DEC")
     plus(T.DEC[:, 1024:1160], T.zer[:, 0:136], pf[:, 11:12], "zer pf11", "DEC1 DEC2")
     zero(T.snd[:, 0:768], "snd")
@@ -421,7 +435,7 @@ def rank_program(g, core, T, topo):
     ts(T.Zq[:], T.Zb[:], pf[:, 23:24], A.mult, "Zb pf23", "Zq")
     for I, w, n in ((T.Ie, 1.0 / 128, "Ie"), (T.Ib, 1.0, "Ib")):
         ts(I[:], T.yrow[:, 0:128], pf[:, 0:1], A.is_equal, "yrow pfa", n, w, A.mult)
-    for I, w, n in ((T.In, -1.0, "In"), (T.If, 1.0, "If"), (T.Ig, -65536.0, "Ig"), (T.I4, 4.0, "I4")):
+    for I, w, n in ((T.In, -1.0, "In"), (T.If, 1.0, "If"), (T.Ig, -65536.0, "Ig"), (T.I4, 4.0, "I4"), (T.I8, 0.125, "I8")):
         ts(I[:], T.Ib[:], w, A.mult, "Ib", n)
     ms(T.cb[0:32, 0:512], 1.0, "cb0")
     ms(T.cb[0:32, 512:640], 3072.0, "cb1")
@@ -492,22 +506,9 @@ def rank_program(g, core, T, topo):
         ts(T.cwb[:, 0:768], T.dG[:, 0:768], 0.0, A.max, "dG", "cwb", 32.0, A.min)
         conv(T[bank][:, 64:112], T.Zh, lambda r: T.cwb[:, r:768:16], "Zh cwb", bank)
 
-    def place(I, In, n, out, on):
-        ts(T.i2[:, 0:n], I, 63, AND, In, "i2")
-        ts(T.i2[:, 68:68 + n], I, 6, SH, In, "i3")
-        ts(T.f4[:, 68:68 + n], T.i2[:, 0:n], 176.0, A.mult, "i2", "f4b")
-        tt(out, T.f4[:, 68:68 + n], T.i2[:, 68:68 + n], A.add, "f4b i3", on)
-
-    def pick(pos, pn, inv, vn, dum, n, out, on):
-        tt(T.dA[:, 0:n], dum, pos, A.subtract, "dumA " + pn, "dA")
-        tt(T.dA[:, 0:n], T.dA[:, 0:n], inv, A.mult, "dA " + vn, "dA")
-        tt(T.dA[:, 0:n], T.dA[:, 0:n], pos, A.add, "dA " + pn, "dA")
-        cp(out, T.dA[:, 0:n], "dA", on)
-
     link_list(T.axoi[:], "axoi", T.flG, "flG0 flG1", T.cumG, "cumG", T.sea, "sea", T.oa, "oa", "PX", "P1")
     counts(T.flG, "flG0", 512, 0, T.wa, "wa", "P0", "")
     mm(T.PY[:, 0:1], [(T.BOh[:], T.cumG[:, 512:513])], "BOh cumG", "PY")
-    plus(yv[0](0, 2048), T.V[:, 0:2048], 16.0, "V00 V01", xn(0))
     move((T.La[:], T.oa[:, 0:32]), T.wa[:, 0:512], "oa wa", "La")
     move(col[:, 0:1], T.PY[:, 0:1], "PY", "c0")
     run_down(T.La, "La", T.cwa, "cwa", 768)
@@ -526,9 +527,14 @@ def rank_program(g, core, T, topo):
     exchange(T.snd, 0, T.xw0, Y0 + 2048, 1, "snd snd1", "xl0")
     plus(T.valG[:, 0:48], T.PS[:, 64:112], -1.0, "PS", "valG")
     zero(T.Lb[:, 0:768], "Lb")
-    ts(T.i1[:, 0:48], T.i1[:, 0:48], 4.0, A.mult, "i1", "i1", 8192.0, A.add)
-    place(T.i1[:, 0:48], "i1", 48, T.f4[:, 0:48], "f4")
-    pick(T.f4[:, 0:48], "f4", T.inv[:, 0:48], "inv", T.dumA[:, 48:96], 48, T.oT[:, 0:48], "oT")
+    ts(T.i2[:, 0:48], T.i1[:, 0:48], 15, AND, "i1", "i2")
+    ts(T.i2[:, 68:116], T.i1[:, 0:48], 4, SH, "i1", "i3")
+    ts(T.f4[:, 68:116], T.i2[:, 0:48], 704.0, A.mult, "i2", "f4b", 128.0, A.add)
+    tt(T.f4[:, 0:48], T.f4[:, 68:116], T.i2[:, 68:116], A.add, "f4b i3", "f4")
+    tt(T.dA[:, 0:48], T.dumA[:, 48:96], T.f4[:, 0:48], A.subtract, "dumA f4", "dA")
+    tt(T.dA[:, 0:48], T.dA[:, 0:48], T.inv[:, 0:48], A.mult, "dA inv", "dA")
+    tt(T.dA[:, 0:48], T.dA[:, 0:48], T.f4[:, 0:48], A.add, "dA f4", "dA")
+    cp(T.oT[:, 0:48], T.dA[:, 0:48], "dA", "oT")
     cp(T.Fb[:], T.AI[:, 0:512], "AI", "Fb")
     for j in range(4):
         mm(T.PK[:, 128 * j:128 * j + 128], [(T.Pf[:, 144 * j + 12 - 4 * b:144 * j + 140 - 4 * b], T.Fb[:, b:512:4]) for b in range(4)], "Pf Fb", "PK")
@@ -546,6 +552,7 @@ def rank_program(g, core, T, topo):
     ts(pc[:, 8:11], pc[:, 0:3], 256.0, A.add, "pc", "pc2")
     ts(pc[:, 11:12], pc[:, 0:1], -64.0, A.mult, "pc", "pc3", -255.0 * 64, A.add)
     ts(pc[:, 12:13], pc[:, 2:3], -2.0 ** 25, A.mult, "pc", "pc3", -255.0 * 2 ** 25, A.add)
+    ts(pc[:, 7:8], pc[:, 1:2], -1.0, A.mult, "pc", "pc5", -255.0, A.add)
     ts(pc[:, 13:16], pc[:, 4:7], pc[:, 3:4], A.subtract, "pc", "pc4")
     ts(T.inv[:, 68:116], T.gam[:, 0:48], col[:, 1:2], A.is_ge, "gam c1", "invX")
     ts(T.i1[:, 0:48], T.PX[:, 64:112], 32.0, A.mult, "PX", "i1")
@@ -599,8 +606,8 @@ def rank_program(g, core, T, topo):
     tt(T.f3[:, 0:48], T.f3[:, 0:48], T.f5[:, 0:48], A.add, "f3 f5", "f3")
     cp(T.oG[:, 0:48], T.f3[:, 0:48], "f3", "oG")
     move((T.AX[:], T.oG[:, 0:48]), T.zer[:, 0:768], "oG zer", "AX AXl AXa AXb")
-    move(T.snd[:, 768:1536], T.AX[:, 8256:AXW:4], "AX", "msS")
-    iota(T.AX[:, 8256:AXW:4], [[0, 768]], 64, 0, "AX")
+    move(T.snd[:, 768:1536], AXL, "AX", "msS")
+    iota(AXL, [[0, 768]], 64, 0, "AX")
     conv(T.PY[:, 0:48], T.Zq, lambda r: T.snd[:, 768 + r:1536:16], "Zq msS", "PY")
     ts(T.held[:], T.PY[:, 0:48], 1.0, A.is_lt, "PY", "held")
     dma([(T.AX[row, 64:8256], T.Eb[:]), (T.AX[row1, 64:8256], T.Fb[:])], "Eb Fb", "AX", 512)
@@ -640,10 +647,10 @@ def rank_program(g, core, T, topo):
         ts(T.f5[:, 0:48], T.i1[:, 0:48], float(t), A.is_equal, "i1", "f5", -8256.0, A.mult)
         tt(T.f5[:, 0:48], T.D[:, LK], T.f5[:, 0:48], A.add, "DL f5", "f5")
         ts(T.oN[:], T.f5[:, 0:48], 0.25, A.mult, "f5", "oN", 2063.625, A.add)
-        ts(T.f5[:, 0:48], T.D[:, LK], 63.5, A.is_lt, "DL", "f5")
-        tt(T.f5[:, 0:48], T.f5[:, 0:48], T.dumK[:, 0:48], A.mult, "f5 dumK", "f5")
-        tt(T.f5[:, 0:48], T.f5[:, 0:48], T.D[:, LK], A.max, "f5 DL", "f5")
-        cp(T.oL[:], T.f5[:, 0:48], "f5", "oL")
+        ts(T.f4[:, 0:48], T.D[:, LK], 63.5, A.is_lt, "DL", "f4")
+        tt(T.f4[:, 0:48], T.f4[:, 0:48], T.dumK[:, 0:48], A.mult, "f4 dumK", "f4")
+        tt(T.f4[:, 0:48], T.f4[:, 0:48], T.D[:, LK], A.max, "f4 DL", "f4")
+        cp(T.oL[:], T.f4[:, 0:48], "f4", "oL")
         ts(T.j1[:, 0:32], T.gam[:, 0:32], K, A.mult, "gam pc", "j1", pc[:, 4 + t:5 + t], A.add)
         ts(T.j2[:, 0:32], T.j1[:, 0:32], 511, AND, "j1", "j20")
         ts(T.j2[:, 32:64], T.j1[:, 0:32], 9, SH, "j1", "j21", 15, AND)
@@ -706,10 +713,10 @@ def rank_program(g, core, T, topo):
             o = own(512 * q, 512 * q + 512)
             either(TS(o, Pq[q][:], 0.0, A.max), ACT(o, Pq[q][:], F.Relu), "P%d" % q, "yp%d" % q)
         send(T.xw0[:, 0:Y0 + 2048], "vac " + YP + " " + xn(0), T.xw0, Y0 + 2048, "xl0")
-        move(T.f1[:], T.PK[:, 0:256], "PK", "f1")
-        tt(T.km[:], T.PK[:, 256:512], T.f1[:], A.max, "PK f1", "km")
+        move(T.f1[:], T.PK[:, 0:256], "PK", "f1 f1b")
+        tt(T.km[:], T.PK[:, 256:512], T.f1[:], A.max, "PK f1 f1b", "km")
         either(TS(T.hiF[:], SL, hi, A.is_ge, 2.0 ** 25, A.mult), ACT(T.hiF[:], SL, F.Relu, scale=2.0 ** 25, bias=pc[:, 12:13]), "PY pc2 pc3", "hiF")
-        either(TS(T.thr[:], SL, th, A.is_lt), ACT(T.thr[:], SL, F.Relu, scale=-1.0, bias=th), "PY pc2", "thr")
+        either(TS(T.thr[:], SL, th, A.is_ge), ACT(T.thr[:], SL, F.Relu, bias=pc[:, 7:8]), "PY pc2 pc5", "thr")
         tt(T.km[:, 0:128], T.km[:, 0:128], T.km[:, 128:256], A.max, "km", "km")
         tt(T.mg[:], T.km[:, 0:128], T.hiF[:], A.min, "km hiF", "mg")
         tt(T.i1[:, 0:128], T.mg[:], T.dumK[:, 0:128], A.max, "mg dumK", "i1")
@@ -725,12 +732,13 @@ def rank_program(g, core, T, topo):
         if last:
             plus(T.V[:, 0:2048], yv[0](0, 2048), -16.0, xn(0), "V00 V01")
             dma([(T.yx[:], T.V[:, 0:2048])], "V00 V01", "", 512)
-        move(T.snd[:, 768:1536], T.AX[:, 8256:AXW:4], "AX", "msS")
+        move(T.snd[:, 768:1536], AXL, "AX", "msS")
         exchange(T.snd, 768, T.msR, 0, -1, "msS", "msR")
         if not last:
-            iota(T.AX[:, 8256:AXW:4], [[0, 768]], 64, 0, "AX")
+            iota(AXL, [[0, 768]], 64, 0, "AX")
         clear("PS", 512)
-        left = [8]
+        left = [9]
+        mms([(T.PS[:, 128 * j:128 * j + 128], T.I8[:], T.thr[:], False, False) for j in range(4)], "I8 thr", "PS", left)
         for k in range(8):
             prefetch(k, T.xw0[:], T.ofp[:, 64 * k:64 * k + 64], "vac xl0 ofp " + YP + " " + xn(0))
             more(T.PS[:, 64 * k:64 * k + 64], terms(T.Zq, lambda r: T.VA[:, 1024 * k + r:1024 * k + 1024:16]), "Zq W%d" % k, "PS", left)
@@ -760,8 +768,8 @@ def rank_program(g, core, T, topo):
         if not last:
             ts(T.oN[:], T.D[:, LK], 0.25, A.mult, "DL", "oN", -0.375, A.add)
         ts(T.isL[:], T.gam[:], nL, A.is_lt, "gam gam2 g1", "isL")
-        ts(T.flE[:, 128:144], T.D[:, 128 + 16 * t:144 + 16 * t], 63.5, A.is_lt, "DL flE", "flEL")
-        mms([(T.P1[:, b:64:4], T.Qh[:, 144 * b + 3:144 * b + 131], T.flE[:, 128:144], True, True) for b in range(4)], "Qh flEL", "P1")
+        ts(T.flE[:, 512:528], T.D[:, 128 + 16 * t:144 + 16 * t], 63.5, A.is_lt, "DL", "flEL")
+        mms([(T.P1[:, b:64:4], T.Qh[:, 144 * b + 3:144 * b + 131], T.flE[:, 512:528], True, True) for b in range(4)], "Qh flEL", "P1")
         move(T.flT[:, 528:592], T.P1[:, 0:64], "P1", "flT2")
         tt(T.Fb[:, t:512:4], T.Fb[:, t:512:4], T.keepB[:], A.min, "Fb keepB", "Fb")
         tt(T.TG[:, 512:1024], (T.Fb[:], T.oJ[:, 0:32]), T.TG[:, 0:512], A.mult, "Fb oJ Tt", "Gj lost0 lost1 lost2 lost3")
@@ -783,13 +791,11 @@ def rank_program(g, core, T, topo):
         run_down(T.Lb, "Lb", T.cwb, "cwb", 1088)
         back = [(T.cb[0:1, 0:128], T.cb[0:1, 896:964])]
         mm(T.PK[:, 64:132], back + terms(T.Zc, lambda r: T.cwb[:, r:1088:16]), "cb0 cb6 Zc cwb", "PK")
-        for j in range(4):
-            tt(T.flE[:, 144 * j:144 * j + 128], T.PS[:, 128 * j:128 * j + 128], T.thr[:], A.is_lt, "PS thr flE", "flP%d" % j)
+        either(TS(T.flE[:, 0:512], T.PS[:], 0.0, A.is_equal), ACT(T.flE[:, 0:512], T.PS[:], F.Relu, scale=-8.0, bias=1.0), "PS", "flP")
         for j in range(4):
             tt(pl(T.D, j), T.PS[:, 128 * j:128 * j + 128], pl(T.D, j), A.min, "PS D", "D")
-        FP = "flP0 flP1 flP2 flP3"
         for b in range(4):
-            mm(T.P0[:, b:512:4], [(T.Qh[:, 144 * b + 3 - j:144 * b + 131 - j], T.flE[:, 144 * j:144 * j + 128]) for j in range(4)], "Qh " + FP, "P0")
+            mm(T.P0[:, b:512:4], [(T.Qh[:, 144 * b + 3 - j:144 * b + 131 - j], T.flE[:, 128 * j:128 * j + 128]) for j in range(4)], "Qh flP", "P0")
         move(T.flT[:, 0:512], T.P0[:], "P0", "flT0")
         scan(T.cumT[:, 1:513], T.flT[:, 0:512], T.flT[:, 0:512], 0.0, A.add, A.max, "flT0", "cumT")
         mm(T.PY[:, 0:1], [(T.BOh[:], T.cumT[:, 512:513])], "BOh cumT", "PY")
@@ -818,11 +824,14 @@ def rank_program(g, core, T, topo):
             refill(T.La, "La")
             for k, TR in enumerate((T.TRI, T.TRs)):
                 mm(T.PY[:, 128 + 128 * k:256 + 128 * k], [(T.BOh[:], T.cumT[:, 0:512:4])] +
-                   [(TR[:], T.flE[:, 144 * j:144 * j + 128]) for j in range(4)], "BOh TRI TRs cumT cumT0 " + FP, "PY")
-            ts(T.f1[:], T.PY[:, 128:384], 1024.0, A.min, "PY", "f1")
-            tt(T.f3[:, 0:128], T.f1[:, 0:128], T.f1[:, 128:256], A.is_gt, "f1", "f3")
-            tt(T.f3[:, 0:128], T.f3[:, 0:128], T.f1[:, 0:128], A.mult, "f1 f3", "f3")
-            ts(T.oE[:], T.f3[:, 0:128], 15.0, A.add, "f3", "oE")
+                   [(TR[:], T.flE[:, 128 * j:128 * j + 128]) for j in range(4)], "BOh TRI TRs cumT cumT0 flP", "PY")
+            act(T.f1[:, 0:128], T.PY[:, 256:384], F.Relu, "PY", "f1", scale=-1.0, bias=1024.0)
+            act(T.f1[:, 128:256], T.PY[:, 128:256], F.Relu, "PY", "f1b", scale=-1.0, bias=1024.0)
+            tt(T.f3[:, 0:128], T.f1[:, 0:128], T.f1[:, 128:256], A.subtract, "f1 f1b", "f3")
+            ts(T.f1[:, 128:256], T.f1[:, 128:256], -1.0, A.mult, "f1b f3", "f1b", 1039.0, A.add)
+            ts(T.f3[:, 0:128], T.f3[:, 0:128], 2048.0, A.mult, "f3", "f3")
+            tt(T.f3[:, 0:128], T.f3[:, 0:128], T.f1[:, 128:256], A.min, "f1b f3", "f3")
+            cp(T.oE[:], T.f3[:, 0:128], "f3", "oE")
             for k, bank in enumerate(("PS", "PY")):
                 a = 512 * k + (k == 0)
                 o, p = T.TG[:, a:512 * k + 512], T[bank][:, a - 512 * k:512]
@@ -832,8 +841,8 @@ def rank_program(g, core, T, topo):
             ts(T.pre[:], T.gam[:, 0:64], col[:, 5:6], A.is_ge, "gam c5", "pre", float(W0 - 32 - PL), A.mult)
             ts(T.j2[:, 0:64], T.j1[:, 0:64], 2, SH, "j1", "j20 j21", 2047, AND)
             tt(T.f2[:, 0:64], T.f2[:, 0:64], T.isL[:, 0:64], A.mult, "f2 isL", "f2")
+            tt(T.pre[:], T.pre[:], T.j2[:, 0:64], A.max, "pre j20 j21", "pre")
             tt(T.f2[:, 0:64], T.f2[:, 0:64], T.pre[:], A.max, "f2 pre", "f2")
-            tt(T.f2[:, 0:64], T.f2[:, 0:64], T.j2[:, 0:64], A.max, "f2 j20 j21", "f2")
             ts(T.oS[:], T.f2[:, 0:64], 16.0, A.add, "f2", "oS")
             for k in range(2):
                 move(T.M[:, 512 * k:512 * k + 512], (T.xw0[:, PL:W0], T.oS[:, 32 * k:32 * k + 32]), "oS vac xl0 " + xn(0), "rr%d" % k)
@@ -861,16 +870,21 @@ def rank_program(g, core, T, topo):
         tt(invX, inv, T.f2[:, 68:136], A.mult, "inv f2b", "invX")
         tt(invX, invX, T.f5[:, 0:68], A.max, "invX f5", "invX")
         if not last:
-            ts(T.i1[:, 0:68], T.PX[:, 128:196], -65.0, A.add, "PX", "i1")
-            place(T.i1[:, 0:68], "i1", 68, T.posT[:], "posT")
-            pick(T.posT[:], "posT", invX, "invX", T.dumA[:, 0:68], 68, T.oT[:], "oT")
+            ts(T.i1[:, 0:68], T.PX[:, 128:196], 1.0 / 64, A.mult, "PX", "i1", -96.5 / 64, A.add)
+            ts(T.posT[:], T.PX[:, 128:196], 176.0, A.mult, "PX", "posT", -65.0 * 176, A.add)
+            ts(T.f4[:, 68:136], T.i1[:, 0:68], -11263.0, A.mult, "i1", "f4b")
+            tt(T.dA[:], invX, T.dumA[:, 0:68], A.mult, "invX dumA", "dA")
+            ts(T.f5[:, 68:136], invX, -20000.0, A.mult, "invX", "f5b", 20000.0, A.add)
+            tt(T.posT[:], T.posT[:], T.f4[:, 68:136], A.add, "posT f4b", "posT")
+            tt(T.posT[:], T.posT[:], T.f5[:, 68:136], A.min, "posT f5b", "posT")
+            tt(T.posT[:], T.posT[:], T.dA[:], A.max, "posT dA", "posT")
+            cp(T.oT[:], T.posT[:], "posT", "oT")
             move((T.UA[:], T.oT[:]), T.dG[:], "oT dG dG1", "UA")
             dma([(T.D[:], T.UA[row, :])], "UA", "D DL", 360)
             tt(invX, invX, T.isL[:, 0:68], A.max, "invX isL", "invX")
-            tt(T.dX[:], invX, T.dumK[:, 0:68], A.mult, "invX dumK", "dX")
-            ts(T.f2[:, 68:136], T.j1[:, 0:68], 64.0, A.add, "j1", "f2b")
-            tt(T.f2[:, 68:136], T.f2[:, 68:136], T.dX[:], A.max, "f2b dX", "f2b")
-            cp(T.oG[:], T.f2[:, 68:136], "f2b", "oG")
+            tt(T.dX[:], invX, T.dumK[:, 72:140], A.mult, "invX dumK", "dX")
+            tt(T.f2[:, 68:136], T.j1[:, 0:68], T.dX[:], A.max, "j1 dX", "f2b")
+            ts(T.oG[:], T.f2[:, 68:136], 64.0, A.add, "f2b", "oG")
             ts(T.f4[:, 0:48], T.g1[:, 0:48], col[:, 0:1], A.is_le, "g1 c0", "f4")
             tt(T.f4[:, 0:48], T.f4[:, 0:48], T.flG[:, 0:48], A.mult, "f4 flG0", "f4")
             tt(T.held[:], T.held[:], T.f4[:, 0:48], A.add, "held f4", "held")
@@ -908,20 +922,24 @@ def rank_program(g, core, T, topo):
 
     if "order" not in PLAN:
         PLAN["order"] = schedule(ops)
-    toks, cnt, seen = {}, {}, {q: {} for q in Q}
+    toks, at, cnt, known, seen = {}, {}, {}, {}, {q: {} for q in Q}
 
     def wait(q, need):
         for s, n in need:
             if seen[q].get(s, 0) < n and not q == "t" == s[1]:
                 Q[q].wait_ge(T.sem[s], n)
                 seen[q][s] = n
+                for a, b in known.get((s, n), {}).items():
+                    seen[q][a] = max(seen[q].get(a, 0), b)
     for i, q in PLAN["order"]:
-        wait(q, sorted((tok for p in ops[i][0] for tok in toks[p]), key=lambda x: -x[1]))
+        wait(q, [tok for p in sorted(ops[i][0], key=lambda p: -at[p]) for tok in toks[p]])
+        at[i] = len(at)
         got = calls[i][q]()
         if not isinstance(got, list):
             s = "q" + q
             got.then_inc(T.sem[s], 1)
             got = [(s, cnt.get(s, 0) + 1)]
         toks[i] = got
+        known[got[0]] = dict(seen[q])
         cnt.update(got)
     wait("g", list(cnt.items()))

import numpy as np
from concourse.bass import DstId, RemoteDMATransfer
from concourse.mybir import AluOpType as A, ActivationFunctionType as F

N, RO = 4, 3
W0, W1 = 4912, 2832
PL = 2064
UAW, AXW, L1W = 11264, 11392, 1680
SP = 3
PASSES, STARTS, HEAT = 6000, 1, 0.001
f32, bf, f16, i32, u16 = "float32", "bfloat16", "float16", "int32", "uint16"


def sb(n, t):
    return ("sbuf", [128, n], t)


SCRATCH = {
    "xw0": sb(W0, bf), "xw1": sb(W1, bf), "V": sb(8192, bf), "VA": sb(8192, bf), "snd": sb(1536, bf),
    "UA": sb(UAW, f32), "AX": sb(AXW, f32), "La": sb(L1W, f32), "Lb": sb(L1W, f32), "zer": sb(1024, f32),
    "dT": sb(1088, f32), "dG": sb(1088, f32), "cwa": sb(1088, f16), "cwb": sb(1088, f16), "DEC": sb(1160, bf),
    "wa": sb(592, f32), "wb": sb(592, f32), "D": sb(704, f32), "AI": sb(704, i32), "isT": sb(704, bf), "vacm": sb(704, bf),
    "off": sb(704, u16), "ofp": sb(512, u16), "M": sb(1024, bf), "msR": sb(768, bf), "TG": sb(1024, bf),
    "Fb": sb(512, f32), "Eb": sb(512, f32), "RV": sb(2048, bf),
    "axoi": sb(512, i32), "pari": sb(8, i32), "parf": sb(8, f32), "pc": sb(16, f32),
    "flT": sb(592, bf), "flG": sb(560, bf), "flE": sb(528, bf), "cumT": sb(608, f16), "cumG": sb(576, f16),
    "km": sb(256, f32), "held": sb(48, f32), "alive": sb(48, f32),
    "i1": sb(136, i32), "i2": sb(136, i32), "j1": sb(136, i32), "j2": sb(136, i32),
    "f1": sb(256, f32), "f2": sb(136, f32), "f3": sb(136, f32), "f4": sb(136, f32), "f5": sb(136, f32), "g1": sb(136, f32), "g2": sb(136, f32),
    "mg": sb(128, f32), "thr": sb(128, bf), "hiF": sb(128, f32), "lostB": sb(128, bf), "keepB": sb(128, f32),
    "oK": sb(128, u16), "oL": sb(48, u16), "oN": sb(48, u16), "oa": sb(40, u16), "ob": sb(40, u16), "oT": sb(68, u16), "oG": sb(68, u16),
    "oS": sb(64, u16), "oE": sb(128, u16), "oJ": sb(64, u16), "lpre": sb(64, u16), "lpost": sb(32, u16),
    "sea": sb(80, f32), "seb": sb(80, f32), "posT": sb(68, f32), "valT": sb(68, f32), "valG": sb(68, f32),
    "inv": sb(136, f32), "dA": sb(68, f32), "dX": sb(68, f32), "isL": sb(136, f32), "pre": sb(64, f32),
    "col": sb(24, f32), "pi": sb(8, i32), "pf": sb(28, f32), "yrow": sb(144, f32),
    "Zb": sb(144, bf), "Zk": sb(144, bf), "Zp": sb(288, bf), "Zq": sb(144, bf),
    "Zh": sb(144, f16), "Zc": sb(144, f16), "Zt": sb(144, f16),
    "Ib": sb(128, bf), "I4": sb(128, bf), "I8": sb(128, bf), "In": sb(128, bf), "Ig": sb(128, bf), "If": sb(128, f32),
    "BOh": sb(128, f16), "TRI": sb(128, bf), "TRp": sb(128, bf), "TRs": sb(128, bf), "TRe": sb(128, bf), "Ie": sb(128, f16),
    "Wv": sb(256, f16), "Pf": sb(576, f32), "Qh": sb(576, bf), "cb": sb(976, bf), "ch": sb(832, f16), "Ut": sb(16, bf),
    "Dc": sb(40, f32), "CL": sb(80, f32), "gam": sb(136, f32), "dumA": sb(144, f32), "dumK": sb(144, f32),
}
for _k in ("P0", "P1", "P2", "P3", "PK", "PS", "PX", "PY"):
    SCRATCH[_k] = ("psum", [128, 512], f32)
SEMAPHORES = ["qv", "qs", "qt", "qg"] + ["d%d" % k for k in range(40)] + ["ar%d" % k for k in range(10)] + ["lo%d" % k for k in range(10)]
CY, GA, SC, PE, WK, DM = (np.array(x) for x in ((.97e-3, .83e-3, 1.1e-3, 1.15e-3, .95e-3), (1.65, 1.45, 1.75, 1.9, 1.4), (4.1, 3.5, 5.3, 2.7, 4.8),
                                                (.5e-3, .417e-3, .55e-3, .58e-3, .48e-3), (.14, .2, .11, .11, .1), (1., .9, 1.1, 1., 1.)))
WAKE = float(WK[0])
PLAN = {}


def schedule(ops):
    n = len(ops)
    each = [[{q: (float((b + 0 * WK)[k]), float((l + 0 * WK)[k])) for q, (b, l) in o[1].items()} for o in ops] for k in range(len(WK))]
    ops = [(o[0], e) for o, e in zip(ops, each[0])]
    pred, succ = [o[0] for o in ops], [[] for _ in ops]
    for i in range(n):
        for p in pred[i]:
            succ[p].append(i)
    level = [0.0] * n
    for i in range(n - 1, -1, -1):
        level[i] = min(b + l for b, l in ops[i][1].values()) + max([level[s] + WAKE for s in succ[i]], default=0.0)

    def one(prio, pen, pre, suc, fixed):
        left = [len(p) for p in pre]
        fin, where, gaps = [0.0] * n, [""] * n, {q: [[0.0, 1e9]] for q in "vstgy"}
        ready = sorted((prio[i], i) for i in range(n) if not left[i])
        while ready:
            i = ready.pop()[1]
            top = None
            for q, (b, l) in ops[i][1].items():
                if fixed and q != fixed[i]:
                    continue
                est = 0.0
                for p in pre[i]:
                    e = fin[p] if q == "t" == where[p] else fin[p] + WAKE
                    if e > est:
                        est = e
                if fixed:
                    est += l
                gq = gaps[q]
                k = len(gq) - 1
                while k > 0 and gq[k - 1][1] >= est + b:
                    k -= 1
                while gq[k][1] < max(gq[k][0], est) + b:
                    k += 1
                st = max(gq[k][0], est)
                key = st + b * (1 + pen[i] * (q == "v"))
                if top is None or key < top[0]:
                    top = (key, q, k, st, b, 0.0 if fixed else l)
            key, q, k, st, b, l = top
            a, z = gaps[q][k]
            gaps[q][k:k + 1] = [x for x in ([a, st], [st + b, z]) if x[1] - x[0] > 0.03]
            fin[i], where[i] = st + b + l, q
            new = False
            for s in suc[i]:
                left[s] -= 1
                if not left[s]:
                    ready.append((prio[s], s))
                    new = True
            if new:
                ready.sort()
        return max(fin), fin, where

    def judge(s):
        where, total, out = s[2], 0.0, []
        order = sorted(range(n), key=lambda i: (s[1][i] - sum(ops[i][1][where[i]]), i))
        for k in range(1, len(WK)):
            fin, why, free, prev, wake, cost = [0.0] * n, [-1] * n, dict.fromkeys("vstgy", 0.0), dict.fromkeys("vstgy", -1), float(WK[k]), each[k]
            for i in order:
                q = where[i]
                st, w = free[q], prev[q]
                for p in pred[i]:
                    e = fin[p] if q == "t" == where[p] else fin[p] + wake
                    if e >= st:
                        st, w = e, p
                b, l = cost[i][q]
                free[q], prev[q], fin[i], why[i] = st + b, i, st + b + l, w
            end = max(fin)
            total += end / unit.setdefault(k, end)
            i = fin.index(end)
            while why[i] >= 0:
                if why[i] not in pred[i]:
                    out.append((why[i], i))
                elif len(cost[i]) > 1:
                    out.append((i, i))
                i = why[i]
        return total, order, out
    unit = {}
    prio0, pen0 = level, [1.0] * n
    best = now = one(prio0, pen0, pred, succ, None)
    for k in range(12):
        p2 = one(now[1], pen0, succ, pred, now[2])[1]
        now = one(p2, pen0, pred, succ, None)
        if now[0] < best[0]:
            best, prio0 = now, p2
    first, top = best, judge(best)
    best = (top, best)
    for seed in range(1, STARTS + 1):
        rng = np.random.default_rng(seed)
        now, prio, pen, val = first, prio0, pen0, top
        for k in range(PASSES):
            p2, e2, path = list(prio), list(pen), val[2]
            for z in range(1 + (k % 3 == 0)):
                a, b = path[int(rng.random() * len(path))]
                u = rng.random()
                c = [x for x in (a, b) if len(ops[x][1]) > 1]
                if c and (a == b or u < 0.4):
                    x = c[int(rng.random() * len(c))]
                    e2[x] = -0.9 if now[2][x] != "v" else 9.0
                elif u < 0.75:
                    p2[a] = min(p2[a], p2[b]) - 3.0 * rng.random() ** 2
                else:
                    todo, up = [b], max(p2[a], p2[b]) + rng.random() - p2[b]
                    for x in todo:
                        p2[x] += up
                        todo += [y for y in pred[x] if y not in todo and now[1][y] > now[1][b] - 6.0]
            got = one(p2, e2, pred, succ, None)
            new = judge(got)
            if new[0] <= val[0] + HEAT * (1.0 - k / PASSES) * rng.random():
                now, prio, pen, val = got, p2, e2, new
                if new[0] < best[0][0]:
                    best = (new, got)
    return [(i, best[1][2][i]) for i in best[0][1]]


def rank_program(g, core, T, topo):
    rank = T.rank_of(core)
    if rank is None:
        return
    Q = {"v": g.vector, "s": g.scalar, "t": g.tensor, "g": g, "y": g.sync}
    ops, calls = [], []
    wr, rd = {}, {}

    def record(alts, R, W, any_order=""):
        R, W = R.split(), W.split()
        W = W + [r for r in R if r[0] == "P" and r != "Pf"]
        i, pre = len(ops), set()
        for r in R:
            if r in wr:
                pre.add(wr[r])
        for w in W:
            if w in wr:
                pre.add(wr[w])
            pre.update(rd.get(w, []))
        if any_order:
            pre.add(wr[any_order])
            R = R + [any_order]
        for r in R:
            rd.setdefault(r, []).append(i)
        for w in W:
            wr[w] = i
            rd[w] = []
        ops.append((sorted(pre), {q: a[:2] for q, a in alts.items()}))
        calls.append({q: a[2] for q, a in alts.items()})

    def ap(x):
        return x[0].indirect(x[1]) if isinstance(x, tuple) else x

    def cost(q, out, a, other=None, two=False):
        if isinstance(out, tuple):
            return 0.06 + 16 * out[1].shape[1] * SC * CY
        if isinstance(a, tuple):
            return 0.06 + 16 * a[1].shape[1] * GA * CY
        n = out.shape[1]
        if q == "s":
            return 0.07 + n * CY
        if two:
            n *= 1 if "P" in (a.name[0], other.name[0]) else 2
        elif all("16" in str(x.dtype) for x in (out, a, other) if x is not None):
            n *= 0.5
        return max(n, 64) * CY

    v = g.vector

    def TS(out, a, s1, o0, s2=None, o1=None):
        if o1 is None:
            return {"v": (cost("v", out, a), 0.0, lambda: v.tensor_scalar(ap(out), ap(a), s1, None, o0))}
        return {"v": (cost("v", out, a), 0.0, lambda: v.tensor_scalar(ap(out), ap(a), s1, s2, o0, o1))}

    def CP(out, a):
        return {"v": (cost("v", out, a), 0.0, lambda: v.tensor_copy(ap(out), ap(a)))}

    def ACT(out, a, f, **kw):
        return {"s": (cost("s", out, a), 0.0, lambda: g.scalar.activation(ap(out), ap(a), f, **kw))}

    def ts(out, a, s1, o0, R, W, s2=None, o1=None):
        alts = TS(out, a, s1, o0, s2, o1)
        if not isinstance(a, tuple) and all("float32" in str(x.dtype) or "bfloat16" in str(x.dtype) for x in (out, a)):
            if o0 == A.mult and o1 == A.add:
                alts.update(ACT(out, a, F.Identity, scale=s1, bias=s2))
            if o0 == A.add and o1 is None:
                alts.update(ACT(out, a, F.Identity, bias=s1))
            if o0 == A.mult and o1 is None:
                alts.update(ACT(out, a, F.Identity, scale=s1))
        record(alts, R, W)

    def tt(out, a, b, o, R, W):
        record({"v": (cost("v", out, a, b, True), 0.0, lambda: v.tensor_tensor(ap(out), ap(a), b, o))}, R, W)

    def cp(out, a, R, W):
        record(CP(out, a), R, W)

    def act(out, a, f, R, W, **kw):
        record(ACT(out, a, f, **kw), R, W)

    def either(x, y, R, W):
        record({**x, **y}, R, W)

    def move(out, a, R, W):
        either(CP(out, a), ACT(out, a, F.Silu if isinstance(out, tuple) else F.Copy), R + " silu" * isinstance(out, tuple), W)

    def copy3(out, a, R, W):
        n = out.shape[1]
        record({**CP(out, a), **ACT(out, a, F.Copy), "g": (0.17 + 2 * n * CY, 0.0, lambda: g.affine_select(out, a, [[0, n]], A.is_ge, 0.0, 0, 0))}, R, W)

    def zero(out, W):
        n = out.shape[1]
        record({**CP(out, T.zer[:, 0:n]), **ACT(out, T.zer[:, 0:n], F.Copy),
                "g": (0.13 + 2 * n * CY, 0.0, lambda: g.iota(out, [[0, n]], 0, 0, allow_small_or_imprecise_dtypes=True))}, "zer", W)

    def plus(out, a, c, R, W):
        either(TS(out, a, c, A.add), ACT(out, a, F.Identity, bias=c), R, W)

    def ms(a, c, W):
        record({"v": (cost("v", a, a), 0.0, lambda: v.memset(a, c))}, "", W)

    def scan(out, a, b, init, o0, o1, R, W):
        record({"v": (cost("v", out, a, b), 0.0, lambda: v.tensor_tensor_scan(out, a, b, init, o0, o1))}, R, W)

    def turned(out, a, R, W):
        record({"v": (cost("v", out, a), 0.0, lambda: v.transpose(out, a))}, R, W)

    def iota(out, pat, base, cm, W, flt=True):
        kw = {"allow_small_or_imprecise_dtypes": True} if flt else {}
        record({"g": (0.13 + 2 * out.shape[1] * CY, 0.0, lambda: g.iota(out, pat, base, cm, **kw))}, "", W)

    def mms(items, R, W, left=None):
        def call():
            if left:
                left[0] -= 1
            for k, it in enumerate(items):
                last = g.tensor.matmul(*it[:4], it[4] if not left else left[0] == 0 and k == len(items) - 1)
            return last
        c = sum(max(64, it[2].shape[1]) * (4 if "32" in str(it[1].dtype) else 1) for it in items) * PE
        record({"t": (c, 0.0, call)}, R, "" if left else W, W if left else "")

    def mm(out, tl, R, W, first=True, end=True):
        mms([(out, l, r, first and k == 0, end and k == len(tl) - 1) for k, (l, r) in enumerate(tl)], R, W)

    def more(out, tl, R, W, left):
        mms([(out, l, r, False, False) for l, r in tl], R, W, left)

    nd, nx = [0], [0]

    def dma(pairs, R, W, kb, q="y"):
        s = "d%d" % nd[0]
        nd[0] += 1

        def call():
            for o, i in pairs:
                Q[q].dma_start(o, i).then_inc(T.sem[s], 16)
            return [(s, 16 * len(pairs))]
        record({q: (0.05 * len(pairs), (2.0 + kb / 200.0) * DM, call)}, R, W)

    def engines_of(src):
        peers = [c for c in T.cores if c != src]
        far = [c for c in peers if topo.chip(c) != topo.chip(src)]
        near = [c for c in peers if topo.chip(c) == topo.chip(src)]
        out, used = {}, set()
        for k, c in enumerate(far):
            free = [e for e in topo.engines(src, c) if e not in used]
            n = len(free) // (len(far) - k)
            while n & (n - 1):
                n -= 1
            out[c] = free[:n]
            used.update(free[:n])
        for c in near:
            free = [e for e in topo.engines(src, c) if e not in used]
            out[c] = free[::len(free) // n][:n]
            used.update(out[c])
        return out

    def exchange(src, s0, dst, d0, sign, R, W):
        k = nx[0]
        nx[0] += 1

        def call():
            mine = engines_of(core)
            tr, tot, arr = [], 0, 0
            for h in range(1, N):
                c = T.cores[(rank + sign * h) % N]
                rid, pid = topo.addr(c)[:2]
                tr.append(RemoteDMATransfer(dst_ids=[DstId(rid=rid, pnc=pid)], dma_engine_mask=sum(1 << e for e in mine[c]), remote_sem=T.sem["ar%d" % k],
                                            src=src[:, s0 + (h - 1) * 256:s0 + h * 256], dst=dst[:, d0 + (h - 1) * 256:d0 + h * 256]))
                tot += len(mine[c])
                arr += len(engines_of(c)[core])
            g.remote_dma_fused(tr, local_sem=T.sem["lo%d" % k])
            return [("lo%d" % k, tot), ("ar%d" % k, arr)]
        record({"g": (0.6 + 3.0 * (k == 0), 4.5 * DM, call)}, R, W)

    def terms(Z, rhs):
        return [(Z[:, 15 - r:143 - r], rhs(r)) for r in range(16)]

    def conv(out, Z, rhs, R, W):
        mm(out, terms(Z, rhs), R, W)

    row, row1 = slice(0, 128, 16), slice(1, 128, 16)
    SH, AND = A.arith_shift_right, A.bitwise_and
    Pq = [T.P0, T.P1, T.P2, T.P3]
    pf, col, pc = T.pf, T.col, T.pc
    Y0 = PL + 16
    yv = [lambda a, b, s=1: T.xw0[:, Y0 + a:Y0 + b:s], lambda a, b, s=1: T.xw1[:, 16 + a:16 + b:s]]
    YP = "yp0 yp1 yp2 yp3"
    LK = slice(128, 176)
    AXL = T.AX[:, 8256:11328:4]
    one = (T.cb[0:1, 512:640], T.cb[0:1, 0:512])
    sel15 = T.ch[0:1, 704:832]

    def xn(b):
        return " ".join("x%d_%d" % (b, q) for q in range(4))

    def own(a, b):
        return T.xw0[:, 16 + a:16 + b]

    def pl(B, j, a=0, b=128):
        return B[:, 176 * j + a:176 * j + b]

    def clear(bank, n):
        mm(T[bank][:, 0:n], [(T.Zq[0:1, 16:144], T.cb[0:1, 0:n])], "Zq cb0", bank, True, False)

    def refill(L, n):
        plus(L[:, 0:1024], T.zer[:], pf[:, 10:11], "zer pf10", n)
        plus(L[:, 1024:1088], T.zer[:, 0:64], pf[:, 10:11], "zer pf10", n)

    dma([(T.axoi[:], T.axo[:])], "", "axoi", 256)
    dma([(T.AI[:, 0:512], T.den[:])], "", "AI", 512, q="s")
    dma([(yv[0](0, 2048), T.x0[:])], "", xn(0), 1024)
    dma([(T.pari[0:8, 0:7], T.par[:])], "", "pari", 0, q="s")
    iota(T.pi[:, 0:1], [[0, 1]], 0, 1, "pi0", flt=False)
    iota(T.yrow[:], [[1, 144]], 0, 0, "yrow")
    iota(T.wb[0:32, 0:592], [[1, 592]], 0, 0, "wb")
    iota(T.f1[:, 0:64], [[1, 32], [0, 2]], 0, 0, "f1")
    iota(T.dumA[:], [[176, 3], [1, 48]], 304, 0, "dumA")
    iota(T.dumK[:], [[4, 48], [1, 3]], 8257, 0, "dumK")
    iota(T.hiF[0:8, :], [[1, 8], [0, 16]], 0, -1, "hiF")
    iota(T.RV[:], [[0, 2048]], -32, 0, "RV")
    record({"g": (0.17 + 4096 * CY, 0.0, lambda: g.affine_select(T.RV[:], T.RV[:], [[-1, 16], [-16, 8], [0, 16]], A.is_equal, 0.0, 0, 1))}, "RV", "RV")
    iota(AXL, [[0, 768]], 64, 0, "AXl")
    ms(T.zer[:], 0.0, "zer")
    iota(T.dT[:], [[0, 1088]], 64, 0, "dT")
    ts(T.pi[:, 1:2], T.pi[:, 0:1], 15, AND, "pi0", "pi1")
    ts(T.pi[:, 2:3], T.pi[:, 0:1], 112, AND, "pi0", "pi2")
    ts(T.pi[:, 3:4], T.pi[:, 0:1], 3, AND, "pi0", "pi3")
    ts(T.pi[:, 4:5], T.pi[:, 0:1], 2, SH, "pi0", "pi4", 3, AND)
    ts(T.pi[:, 5:6], T.pi[:, 0:1], 31, AND, "pi0", "pi5")
    cp(pf[:, 0:6], T.pi[:, 0:6], "pi0 pi1 pi2 pi3 pi4 pi5", "pfa")
    ts(pf[:, 6:7], pf[:, 2:3], 15.0, A.add, "pfa", "pf6")
    ts(pf[:, 7:8], pf[:, 1:2], 0.0, A.is_equal, "pfa", "pf7")
    ts(pf[:, 8:9], pf[:, 1:2], 15.0, A.is_equal, "pfa", "pf8")
    ms(T.cumG[:, 0:1], 0.0, "cumG0")
    ms(T.cumT[:, 0:1], 0.0, "cumT0")
    ts(pf[:, 9:10], pf[:, 8:9], 16.0 + 1.0 / 32, A.mult, "pf8", "pf9", -1.0 / 32, A.add)
    ts(pf[:, 10:11], pf[:, 8:9], 965.0 - 32783.5, A.mult, "pf8", "pf10", 32783.5, A.add)
    ts(pf[:, 11:12], pf[:, 8:9], -1.0, A.add, "pf8", "pf11")
    refill(T.La, "La")
    ts(T.g1[:, 0:128], T.yrow[:, 0:128], pf[:, 6:7], A.is_le, "yrow pf6", "g1")
    ts(T.f2[:, 0:128], T.yrow[:, 0:128], pf[:, 2:3], A.is_ge, "yrow pfa", "f2 f2b")
    ts(T.f3[:, 0:128], T.yrow[:, 0:128], pf[:, 0:1], A.is_ge, "yrow pfa", "f3")
    ts(T.f4[:, 0:128], T.yrow[:, 0:128], pf[:, 6:7], A.is_lt, "yrow pf6", "f4 f4b")
    tt(T.BOh[:], T.g1[:, 0:128], T.f2[:, 0:128], A.mult, "g1 f2 f2b", "BOh")
    tt(T.TRI[:], T.g1[:, 0:128], T.f3[:, 0:128], A.mult, "g1 f3", "TRI")
    tt(T.TRp[:], T.f4[:, 0:128], T.f3[:, 0:128], A.mult, "f4 f4b f3", "TRp")
    ts(T.TRe[:], T.TRI[:], 64.0, A.mult, "TRI", "TRe")
    ts(T.gam[:, 0:68], T.yrow[:, 0:68], 16.0, A.mult, "yrow pfa", "gam", pf[:, 1:2], A.add)
    cp(T.ch[0:32, 0:592], T.wb[0:32, 0:592], "wb", "ch")
    ts(T.ch[0:32, 592:704], T.wb[0:32, 0:112], 592.0, A.add, "wb", "ch1")
    ms(T.ch[0:32, 704:832], 0.0, "ch2")
    ms(T.ch[0:32, 719:832:16], 1.0, "ch2")
    ts(T.Dc[:], T.gam[:, 0:40], 1088.0, A.add, "gam", "Dc")
    record({"s": (1.4 + 768 * CY, 0.0, lambda: g.scalar.activation(T.Lb[:, 0:768], T.zer[:, 0:768], F.Silu))}, "zer", "Lb silu")
    plus(T.DEC[:, 0:1024], T.zer[:], pf[:, 11:12], "zer pf11", "DEC")
    plus(T.DEC[:, 1024:1160], T.zer[:, 0:136], pf[:, 11:12], "zer pf11", "DEC1 DEC2")
    zero(T.snd[:, 0:768], "snd")
    zero(T.D[:], "D DL")
    zero(T.dG[:, 768:1088], "dG1")
    for a in (0, PL, W0 - 16):
        ms(T.xw0[:, a:a + 16], 0.0, "vac")
    ms(T.xw1[:, 0:16], 0.0, "vac1")
    ts(pf[:, 23:24], pf[:, 7:8], 1024.0, A.mult, "pf7", "pf23")
    ts(pf[:, 24:25], pf[:, 8:9], 17.0, A.mult, "pf8", "pf24", -16.0, A.add)
    for Z, w, n, R in ((T.Zh, 1.0, "Zh", ""), (T.Zc, pf[:, 9:10], "Zc", "pf9"), (T.Zb, 1.0, "Zb", ""), (T.Zt, pf[:, 24:25], "Zt", "pf24")):
        ts(Z[:], T.yrow[:], pf[:, 6:7], A.is_equal, "yrow pf6 " + R, n, w, A.mult)
    ts(T.Zk[:], T.Zb[:], 65536.0, A.mult, "Zb", "Zk")
    ts(T.Zq[:], T.Zb[:], pf[:, 23:24], A.mult, "Zb pf23", "Zq")
    for I, w, n in ((T.Ie, 1.0 / 128, "Ie"), (T.Ib, 1.0, "Ib")):
        ts(I[:], T.yrow[:, 0:128], pf[:, 0:1], A.is_equal, "yrow pfa", n, w, A.mult)
    for I, w, n in ((T.In, -1.0, "In"), (T.If, 1.0, "If"), (T.Ig, -65536.0, "Ig"), (T.I4, 4.0, "I4"), (T.I8, 0.125, "I8")):
        ts(I[:], T.Ib[:], w, A.mult, "Ib", n)
    ms(T.cb[0:32, 0:512], 1.0, "cb0")
    ms(T.cb[0:32, 512:640], 3072.0, "cb1")
    ms(T.cb[0:32, 896:976], -832.0, "cb6")
    ms(T.cb[0:32, 640:768], 65536.0, "cb2")
    ms(T.cb[0:32, 768:896], -16384.0, "cb2")
    for j in range(4):
        ts(pf[:, 14 + j:15 + j], pf[:, 3:4], float(j), A.is_equal, "pfa", "pm%d" % j)
        ts(pf[:, 18 + j:19 + j], pf[:, 4:5], float(j), A.is_equal, "pfa", "pn%d" % j)
    ts(pf[:, 12:13], pf[:, 1:2], 704.0, A.mult, "pfa", "pf12")
    ts(T.dumA[:], T.dumA[:], pf[:, 12:13], A.add, "dumA pf12", "dumA")
    ts(pf[:, 13:14], pf[:, 2:3], pf[:, 4:5], A.add, "pfa", "pf13", 12.0, A.add)
    ts(pf[:, 25:26], pf[:, 3:4], 4.0, A.mult, "pfa pf6", "pf25", pf[:, 6:7], A.add)
    ts(pf[:, 25:26], pf[:, 25:26], -12.0, A.add, "pf25", "pf25")
    ts(T.Zp[:, 0:144], T.yrow[:], pf[:, 13:14], A.is_equal, "yrow pf13", "Zp0")
    ts(T.Zp[:, 144:288], T.yrow[:], pf[:, 25:26], A.is_equal, "yrow pf25", "Zp1")
    for j in range(4):
        ts(T.Pf[:, 144 * j:144 * j + 144], T.Zp[:, 0:144], pf[:, 14 + j:15 + j], A.mult, "Zp0 pm%d" % j, "Pf")
        ts(T.Qh[:, 144 * j:144 * j + 144], T.Zp[:, 144:288], pf[:, 18 + j:19 + j], A.mult, "Zp1 pn%d" % j, "Qh")
    ts(pf[:, 26:27], pf[:, 1:2], 192.0, A.mult, "pfa", "pf26")
    ts(T.dumK[:], T.dumK[:], pf[:, 26:27], A.add, "dumK pf26", "dumK")
    tt(T.TRs[:], T.TRI[:], T.Ib[:], A.subtract, "TRI Ib", "TRs")
    ts(T.CL[:, 0:37], T.Dc[:, 0:37], 1088.0 + 527.5, A.is_ge, "Dc", "CL", 64.0, A.mult)
    ts(T.CL[:, 0:37], T.CL[:, 0:37], 1024.0, A.add, "CL", "CL")
    move(T.CL[:, 37:74], T.CL[:, 0:37], "CL", "CL")
    ts(col[:, 19:20], pf[:, 17:18], 1.0 / 32, A.mult, "pm3", "c19")
    ts(col[:, 20:21], pf[:, 8:9], 4.0 + 1.0 / 32, A.mult, "pf8 c19", "c20", col[:, 19:20], A.subtract)
    ts(T.Wv[:, 0:128], T.BOh[:], col[:, 20:21], A.mult, "BOh c20", "Wv")
    ts(T.Wv[:, 128:256], T.BOh[:], col[:, 20:21], A.mult, "BOh c20", "Wv1", -1.0, A.mult)
    ts(col[:, 22:23], pf[:, 1:2], 68.0, A.mult, "pfa", "c22")
    ts(T.gam[:, 68:136], T.yrow[:, 0:68], col[:, 22:23], A.add, "yrow c22", "gam2")
    ms(T.flT[:, 512:528], 0.0, "flT1")
    cp(T.parf[0:8, 0:7], T.pari[0:8, 0:7], "pari", "parf")
    ts(T.hiF[0:8, :], T.hiF[0:8, :], 0.0, A.is_equal, "hiF", "hiF")

    def heads(cum, cn, nb, lim, se, sn, o1, on, bank):
        k = nb // 16
        conv(T[bank][:, 0:k], T.Zh, lambda r: cum[:, r:nb:16], "Zh " + cn, bank)
        conv(T[bank][:, k:2 * k], T.Zh, lambda r: cum[:, r + 1:nb + 1:16], "Zh " + cn, bank)
        if lim is None:
            ts(se[:, 0:2 * k], T[bank][:, 0:2 * k], 1088.0, A.min, bank, sn)
        else:
            tt(se[:, 0:2 * k], T[bank][:, 0:2 * k], lim, A.min, bank + " CL", sn)
        tt(se[:, k:2 * k], se[:, k:2 * k], se[:, 0:k], A.is_le, sn, sn)
        tt(se[:, k:2 * k], se[:, k:2 * k], T.Dc[:, 0:k], A.mult, sn + " Dc", sn)
        tt(se[:, 0:k], se[:, k:2 * k], se[:, 0:k], A.max, sn, sn)
        cp(o1[:, 0:k], se[:, 0:k], sn, on)

    def counts(fl, fn, nb, c1, wd, wn, ba, bb):
        mm(T[ba][:], [(T.TRp[:], fl[:, 0:512]), (sel15, T.ch[0:1, 0:512])], "TRp ch ch2 " + fn, ba)
        plus(wd[:, 0:512], T[ba][:], pf[:, 10:11], ba + " pf10", wn)
        if nb > 512:
            mm(T[bb][:, 0:nb - 512], [(T.TRp[:], fl[:, 512:nb]), (sel15, T.ch[0:1, c1:c1 + nb - 512])], "TRp ch ch1 ch2 " + fn, bb)
            plus(wd[:, 512:nb], T[bb][:, 0:nb - 512], pf[:, 10:11], bb + " pf10", wn + "1")

    def run_down(L, ln, cw, cn, n, d0=0, R=""):
        scan(cw[:, 0:n], T.DEC[:, d0:d0 + n], L[:, 0:n], 0.0, A.add, A.max, ln + " DEC DEC1 " + R, cn)

    def link_list(src, sn, fl, fn, cum, cn, se, sen, o1, on, bank, pb):
        ts(fl[:, 0:512], src, 8192.0, A.is_ge, sn, fn)
        ts(T.cwb[:, 0:512], src, -8192.0, A.add, sn, "cwb", 0.0, A.max)
        scan(cum[:, 1:513], fl[:, 0:512], fl[:, 0:512], 0.0, A.add, A.max, fn, cn)
        heads(cum, cn + " " + cn + "0", 512, None, se, sen, o1, on, bank)
        mm(T[pb][:], [(T.TRe[:], fl[:, 0:512]), (T.Ie[:], T.cwb[:, 0:512])], "TRe Ie cwb " + fn, pb)
        move(T.wb[:, 0:512], T[pb][:], pb, "wb")
        move((T.Lb[:], o1[:, 0:32]), T.wb[:, 0:512], on + " wb", "Lb")
        scan(T.dG[:, 0:768], T.Lb[:, 0:768], T.dT[:, 0:768], 0.0, A.max, A.subtract, "Lb dT", "dG")
        ts(T.cwb[:, 0:768], T.dG[:, 0:768], 0.0, A.max, "dG", "cwb", 32.0, A.min)
        conv(T[bank][:, 64:112], T.Zh, lambda r: T.cwb[:, r:768:16], "Zh cwb", bank)

    link_list(T.axoi[:], "axoi", T.flG, "flG0 flG1", T.cumG, "cumG", T.sea, "sea", T.oa, "oa", "PX", "P1")
    counts(T.flG, "flG0", 512, 0, T.wa, "wa", "P0", "")
    mm(T.PY[:, 0:1], [(T.BOh[:], T.cumG[:, 512:513])], "BOh cumG", "PY")
    move((T.La[:], T.oa[:, 0:32]), T.wa[:, 0:512], "oa wa", "La")
    move(col[:, 0:1], T.PY[:, 0:1], "PY", "c0")
    run_down(T.La, "La", T.cwa, "cwa", 768)
    conv(T.PS[:, 0:48], T.Zc, lambda r: T.cwa[:, r:768:16], "Zc cwa", "PS")
    ts(T.oS[:, 0:48], T.PS[:, 0:48], 0.25, A.mult, "PS", "oS", -0.625, A.add)
    conv(T.PS[:, 64:112], T.Zc, lambda r: T.cwa[:, 48 * r:48 * r + 48], "Zc cwa", "PS")
    move(T.M[:, 0:768], (T.xw0[:, PL:Y0 + 2048], T.oS[:, 0:48]), "oS vac " + xn(0), "rr0 rr1")
    ts(T.inv[:, 0:48], T.gam[:, 0:48], col[:, 0:1], A.is_ge, "gam c0", "inv")
    ts(T.f3[:, 0:48], T.gam[:, 0:48], 768.0, A.add, "gam", "f3")
    ts(T.i1[:, 0:48], T.PX[:, 64:112], 32.0, A.mult, "PX", "i1")
    tt(T.f3[:, 0:48], T.f3[:, 0:48], T.inv[:, 0:48], A.mult, "f3 inv", "f3")
    ts(T.i1[:, 0:48], T.i1[:, 0:48], 1023, AND, "i1", "i1")
    tt(T.f3[:, 0:48], T.f3[:, 0:48], T.i1[:, 0:48], A.max, "f3 i1", "f3")
    cp(T.oL[:], T.f3[:, 0:48], "f3", "oL")
    cp((T.snd[:], T.oL[:]), T.M[:, 0:768], "oL rr0 rr1", "snd snd1 msS")
    exchange(T.snd, 0, T.xw0, Y0 + 2048, 1, "snd snd1", "xl0")
    plus(T.valG[:, 0:48], T.PS[:, 64:112], -1.0, "PS", "valG")
    zero(T.Lb[:, 0:768], "Lb")
    ts(T.i2[:, 0:48], T.i1[:, 0:48], 15, AND, "i1", "i2")
    ts(T.i2[:, 68:116], T.i1[:, 0:48], 4, SH, "i1", "i3")
    ts(T.f4[:, 68:116], T.i2[:, 0:48], 704.0, A.mult, "i2", "f4b", 128.0, A.add)
    tt(T.f4[:, 0:48], T.f4[:, 68:116], T.i2[:, 68:116], A.add, "f4b i3", "f4")
    tt(T.dA[:, 0:48], T.dumA[:, 48:96], T.f4[:, 0:48], A.subtract, "dumA f4", "dA")
    tt(T.dA[:, 0:48], T.dA[:, 0:48], T.inv[:, 0:48], A.mult, "dA inv", "dA")
    tt(T.dA[:, 0:48], T.dA[:, 0:48], T.f4[:, 0:48], A.add, "dA f4", "dA")
    cp(T.oT[:, 0:48], T.dA[:, 0:48], "dA", "oT")
    cp(T.Fb[:], T.AI[:, 0:512], "AI", "Fb")
    for j in range(4):
        mm(T.PK[:, 128 * j:128 * j + 128], [(T.Pf[:, 144 * j + 12 - 4 * b:144 * j + 140 - 4 * b], T.Fb[:, b:512:4]) for b in range(4)], "Pf Fb", "PK")
    for j in range(4):
        plus(pl(T.D, j), T.PK[:, 128 * j:128 * j + 128], 64.0, "PK", "D")
    ts(T.off[:], T.D[:], 0.25, A.mult, "D DL", "off offL", -0.375, A.add)
    dma([(T.UA[row, :], T.D[:])], "D DL", "UA", 360)
    link_list(T.AI[:, 0:512], "AI", T.flT, "flT0", T.cumT, "cumT", T.seb, "seb", T.ob, "ob", "PX", "PS")
    dma([(T.dG[row, 0:768], T.valG[:, 0:48])], "valG", "dG", 30)
    move((T.UA[:], T.oT[:, 0:48]), T.dG[:, 0:768], "oT dG", "UA")
    mm(T.PY[:, 0:1], [(T.BOh[:], T.cumT[:, 512:513])], "BOh cumT", "PY")
    move(col[:, 1:2], T.PY[:, 0:1], "PY", "c1")
    mm(T.PY[:, 0:7], [(T.hiF[0:8, :], T.parf[0:8, 0:7])], "hiF parf", "PY")
    move(pc[:, 0:7], T.PY[:, 0:7], "PY", "pc")
    ts(pc[:, 8:11], pc[:, 0:3], 256.0, A.add, "pc", "pc2")
    ts(pc[:, 11:12], pc[:, 0:1], -64.0, A.mult, "pc", "pc3", -255.0 * 64, A.add)
    ts(pc[:, 12:13], pc[:, 2:3], -2.0 ** 25, A.mult, "pc", "pc3", -255.0 * 2 ** 25, A.add)
    ts(pc[:, 7:8], pc[:, 1:2], -1.0, A.mult, "pc", "pc5", -255.0, A.add)
    ts(pc[:, 13:16], pc[:, 4:7], pc[:, 3:4], A.subtract, "pc", "pc4")
    ts(T.inv[:, 68:116], T.gam[:, 0:48], col[:, 1:2], A.is_ge, "gam c1", "invX")
    ts(T.i1[:, 0:48], T.PX[:, 64:112], 32.0, A.mult, "PX", "i1")
    ts(T.i1[:, 0:48], T.i1[:, 0:48], 1023, AND, "i1", "i1")
    ts(T.i1[:, 0:48], T.i1[:, 0:48], 4.0, A.mult, "i1", "i1", 8256.0, A.add)
    refill(T.La, "La")
    refill(T.Lb, "Lb")
    dma([(T.D[:], T.UA[row, :])], "UA", "D DL", 360)

    def prefetch(k, win, off, R):
        move(T.VA[:, 1024 * k:1024 * k + 1024], (win, off), R, "W%d" % k)

    def sums(q, end):
        mm(Pq[q][:], [one, (T.Ib[:], yv[0](512 * q, 512 * q + 512))], "cb0 cb1 Ib x0_%d" % q, "P%d" % q, True, False)
        left = [4 if end else 5]
        for j in range(4):
            more(Pq[q][:], [(T.Ib[:], T.VA[:, 2048 * j + 512 * q:2048 * j + 512 * q + 512])], "Ib W%d" % (2 * j + q // 2), "P%d" % q, left)
        return left

    for k in (0, 2, 4, 6, 1, 3, 5, 7):
        prefetch(k, T.xw0[:, PL:W0 - 16], pl(T.off, k // 2, 64 * (k % 2), 64 * (k % 2) + 64), "vac xl0 off " + xn(0))
    for q in range(4):
        sums(q, True)

    def turn(out, on, ta, tan, tb, tbn):
        move(ta, (out, T.lpre[:]), on + " lpre", tan)
        turned(tb, ta, tan, tbn)
        move(out, (tb, T.lpost[:]), tbn + " lpost", on)

    ts(pf[:, 22:23], pf[:, 1:2], 32.0, A.mult, "pfa", "pf22")
    ts(T.lpost[:], T.yrow[:, 0:32], 32.0, A.mult, "yrow pfa", "lpost", pf[:, 5:6], A.add)
    ts(T.lpre[:], T.f1[:, 0:64], pf[:, 22:23], A.add, "f1 pf22", "lpre")
    ts(T.Eb[:], T.axoi[:], 64.0, A.add, "axoi", "Eb")
    turn(T.Eb[:], "Eb", T.AX[:, 64:1088], "AXa", T.AX[:, 1088:2112], "AXb")
    ts(T.Fb[:], T.Eb[:], 63.5, A.is_ge, "Eb", "Fb", 64.0, A.mult)
    cp(T.j1[:, 0:1], pc[:, 3:4], "pc", "j1")
    ts(T.f2[:, 0:16], T.yrow[:, 0:16], -1.0, A.mult, "yrow pfa", "f2", pf[:, 1:2], A.add)
    ts(T.j1[:, 0:1], T.j1[:, 0:1], 15, AND, "j1", "j1")
    cp(col[:, 23:24], T.j1[:, 0:1], "j1", "c23")
    ts(T.f2[:, 0:16], T.f2[:, 0:16], col[:, 23:24], A.mult, "f2 c23", "f2", col[:, 23:24], A.mult)
    ts(T.j1[:, 0:16], T.f2[:, 0:16], col[:, 23:24], A.mult, "f2 c23", "j1", 65536.0, A.add)
    for b in range(4):
        ts(T.j2[:, 16 * b:16 * b + 16], T.j1[:, 0:16], b, SH, "j1", "j2%d" % b, 1, AND)
    for b in range(4):
        ts(T.g2[:, 16 * b:16 * b + 16], T.j2[:, 16 * b:16 * b + 16], float(2 ** 2 ** b - 1), A.mult, "j20 j21 j2%d" % b, "g2", 1.0, A.add)
    tt(T.g2[:, 0:32], T.g2[:, 0:32], T.g2[:, 32:64], A.mult, "g2", "g2")
    tt(T.Ut[:], T.g2[:, 0:16], T.g2[:, 16:32], A.mult, "g2", "Ut")
    ts(T.f3[:, 0:48], T.inv[:, 68:116], -1.0, A.mult, "invX", "f3", 1.0, A.add)
    tt(T.f3[:, 0:48], T.f3[:, 0:48], T.i1[:, 0:48], A.mult, "f3 i1", "f3")
    tt(T.f5[:, 0:48], T.inv[:, 68:116], T.dumK[:, 0:48], A.mult, "invX dumK", "f5")
    tt(T.f3[:, 0:48], T.f3[:, 0:48], T.f5[:, 0:48], A.add, "f3 f5", "f3")
    cp(T.oG[:, 0:48], T.f3[:, 0:48], "f3", "oG")
    move((T.AX[:], T.oG[:, 0:48]), T.zer[:, 0:768], "oG zer", "AX AXl AXa AXb")
    move(T.snd[:, 768:1536], AXL, "AX", "msS")
    iota(AXL, [[0, 768]], 64, 0, "AX")
    conv(T.PY[:, 0:48], T.Zq, lambda r: T.snd[:, 768 + r:1536:16], "Zq msS", "PY")
    ts(T.held[:], T.PY[:, 0:48], 1.0, A.is_lt, "PY", "held")
    dma([(T.AX[row, 64:8256], T.Eb[:]), (T.AX[row1, 64:8256], T.Fb[:])], "Eb Fb", "AX", 512)

    lo, th, hi, K = pc[:, 8:9], pc[:, 9:10], pc[:, 10:11], pc[:, 3:4]

    def mod16(b, q):
        o, n = T.M[:, 512 * (q % 2):512 * (q % 2) + 512], "rr%d" % (q % 2)
        if b:
            o, n = T.V[:, 4096 + 1024 * q:4608 + 1024 * q], "V%d%d" % (2 + q // 2, q % 2)
        plus(o, Pq[q][:], -23.5, "P%d" % q, n)
        tt(yv[b](512 * q, 512 * q + 512), Pq[q][:], o, A.subtract, "P%d %s" % (q, n), "x%d_%d" % (b, q))

    def send(win, R, dst, d0, W):
        for k in range(2):
            move(T.snd[:, 384 * k:384 * k + 384], (win, T.oN[:, 24 * k:24 * k + 24]), "oN " + R, ("snd", "snd1")[k])
        exchange(T.snd, 0, dst, d0, 1, "snd snd1", W)

    for t in range(RO):
        last = t == RO - 1
        for q in range(4):
            mod16(1, q)
        if t == 0:
            ts(T.oN[:], T.D[:, LK], 0.25, A.mult, "DL", "oN", -0.375, A.add)
        send(T.xw1[:, 0:2064], "vac1 " + xn(1), T.xw1, 2064, "xl1")
        for hq in range(2):
            copy3(own(1024 * hq, 1024 * hq + 1024), yv[1](1024 * hq, 1024 * hq + 1024), "x1_%d x1_%d" % (2 * hq, 2 * hq + 1), "yp%d yp%d" % (2 * hq, 2 * hq + 1))
        if t > 0:
            ts(T.off[:, 0:656], T.D[:, 0:656], 0.25, A.mult, "D DL", "off", -0.375, A.add)
            move((T.AX[:], T.oG[:]), T.dT[:], "oG dT", "AX")
        either(TS(T.vacm[:], T.D[:], 63.5, A.is_lt, 1e9, A.mult), ACT(T.vacm[:], T.D[:], F.Relu, scale=-134217728.0, bias=8522825728.0), "D DL", "vacm")
        ts(T.AI[:, 0:656], T.D[:, 0:656], -64.0, A.add, "D DL", "AI")
        ts(T.AI[:, 0:656], T.AI[:, 0:656], 8195, AND, "AI", "AI")
        ts(T.isT[:, 0:656], T.AI[:, 0:656], float(t), A.is_equal, "AI", "isT", -8256.0, A.mult)
        ts(T.i1[:, 0:48], T.D[:, LK], -64.0, A.add, "DL", "i1")
        ts(T.i1[:, 0:48], T.i1[:, 0:48], 8195, AND, "i1", "i1")
        ts(T.f5[:, 0:48], T.i1[:, 0:48], float(t), A.is_equal, "i1", "f5", -8256.0, A.mult)
        tt(T.f5[:, 0:48], T.D[:, LK], T.f5[:, 0:48], A.add, "DL f5", "f5")
        ts(T.oN[:], T.f5[:, 0:48], 0.25, A.mult, "f5", "oN", 2063.625, A.add)
        ts(T.f4[:, 0:48], T.D[:, LK], 63.5, A.is_lt, "DL", "f4")
        tt(T.f4[:, 0:48], T.f4[:, 0:48], T.dumK[:, 0:48], A.mult, "f4 dumK", "f4")
        tt(T.f4[:, 0:48], T.f4[:, 0:48], T.D[:, LK], A.max, "f4 DL", "f4")
        cp(T.oL[:], T.f4[:, 0:48], "f4", "oL")
        ts(T.j1[:, 0:32], T.gam[:, 0:32], K, A.mult, "gam pc", "j1", pc[:, 4 + t:5 + t], A.add)
        ts(T.j2[:, 0:32], T.j1[:, 0:32], 511, AND, "j1", "j20")
        ts(T.j2[:, 32:64], T.j1[:, 0:32], 9, SH, "j1", "j21", 15, AND)
        cp(T.oJ[:], T.j2[:, 0:64], "j20 j21", "oJ")
        move(T.TG[:, 0:512], (T.Ut[:], T.oJ[:, 32:64]), "Ut oJ", "Tt")
        if last:
            dma([(T.Eb[:], T.AX[row, 64:8256])], "AX", "Eb", 256)
            iota(T.wa[:, 0:64], [[16, 32], [0, 2]], 0, 0, "wa")
            iota(T.wa[:, 64:96], [[1, 16], [512, 2]], 0, 0, "wa")
            ts(pf[:, 22:23], pf[:, 1:2], 31.0, A.mult, "pfa", "pf22", pf[:, 5:6], A.add)
            ts(T.lpre[:], T.wa[:, 0:64], pf[:, 1:2], A.add, "wa pfa", "lpre")
            ts(T.lpost[:], T.wa[:, 64:96], pf[:, 22:23], A.add, "wa pf22", "lpost")
            ts(T.axoi[:], T.Eb[:], -64.0, A.add, "Eb", "axoi")
            ts(T.Eb[:], T.axoi[:], -1.0, A.max, "axoi", "Eb")
            turn(T.Eb[:], "Eb", T.UA[:, 8192:9216], "UA", T.UA[:, 9216:10240], "UAb")
        if t == RO - 2:
            iota(T.dG[:, 0:768], [[4, 768]], 8256 - 64, 0, "dG")
            ts(col[:, 18:19], pf[:, 7:8], 1.0 / 64, A.mult, "pf7", "c18")
            ts(T.dT[:, 0:768], T.dG[:, 0:768], col[:, 18:19], A.mult, "dG c18", "dT", 1.0, A.add)
        win = "vac1 xl1 off " + xn(1)
        for q in range(4):
            mm(Pq[q][:], [one, (T.I4[:], yv[1](512 * q, 512 * q + 512))], "cb0 cb1 I4 x1_%d" % q, "P%d" % q, True, False)
        mms([(T.PK[:], T.cb[0:1, 640:768], T.cb[0:1, 0:512], True, False)] +
            [(T.PK[:, 128 * j:512], T.cb[0:1, 768:896], T.cb[0:1, 128 * j:512], False, False) for j in range(1, 4)], "cb0 cb2", "PK")
        kl = [16]
        for j in range(4):
            more(T.PK[:, 128 * j:128 * j + 128], [(T.If[:], pl(T.D, j))], "If D", "PK", kl)
            more(T.PK[:, 128 * j:128 * j + 128], [(T.In[:], pl(T.vacm, j))], "In vacm", "PK", kl)
        clear("PY", 256)
        left, sl = [[4] for q in range(4)], [6]
        for hq in range(2):
            for j in (3, 0, 1, 2):
                c0, vn, wn = 2048 * j + 1024 * hq, "V%d%d" % (j, hq), "W%d" % (2 * j + hq)
                src = (T.xw1[:], pl(T.off, j, 64 * hq, 64 * hq + 64))
                if j == SP:
                    act(T.V[:, c0:c0 + 1024], src, F.Copy, win, vn)
                else:
                    tt(T.V[:, c0:c0 + 1024], src, own(1024 * hq, 1024 * hq + 1024), A.subtract, win + " yp%d yp%d" % (2 * hq, 2 * hq + 1), vn)
                    act(T.VA[:, c0:c0 + 1024], T.V[:, c0:c0 + 1024], F.Abs, vn, wn)
                for k in range(2):
                    q, c = 2 * hq + k, slice(c0 + 512 * k, c0 + 512 * k + 512)
                    more(Pq[q][:], [(T.Ib[:], T.V[:, c])], "Ib " + vn, "P%d" % q, left[q])
                    if j == SP:
                        bank = ("PS", "PX")[k]
                        mm(T[bank][:], [(T.In[:], yv[1](512 * q, 512 * q + 512))], "In x1_%d" % q, bank, True, False)
                        mm(T[bank][:], [(T.Ib[:], T.V[:, c])], "Ib " + vn, bank, False, True)
                        act(T.VA[:, c], T[bank][:], F.Abs, bank, wn)
                more(T.PK[:, 128 * j + 64 * hq:128 * j + 64 * hq + 64], terms(T.Zk, lambda r: T.VA[:, c0 + r:c0 + 1024:16]), "Zk " + wn, "PK", kl)
            for q in (2 * hq, 2 * hq + 1):
                mod16(0, q)
                more(T.PY[:, 128:256], [(T.Zb[:, 15 - r:143 - r], yv[0](128 * r, 128 * r + 128)) for r in range(4 * q, 4 * q + 4)], "Zb x0_%d" % q, "PY", sl)
            more(T.PY[:, 64 * hq:64 * hq + 64], terms(T.Zb, lambda r: yv[0](1024 * hq + r, 1024 * hq + 1024, 16)), "Zb x0_%d x0_%d" % (2 * hq, 2 * hq + 1), "PY", sl)
        SB, SL = T.PY[:, 128:256], T.PY[:, 0:128]
        either(TS(T.lostB[:], SB, lo, A.is_lt), ACT(T.lostB[:], SB, F.Relu, scale=-1.0, bias=lo), "PY pc2", "lostB")
        either(TS(T.keepB[:], SB, lo, A.is_ge, 64.0, A.mult), ACT(T.keepB[:], SB, F.Relu, scale=64.0, bias=pc[:, 11:12]), "PY pc2 pc3", "keepB")
        for q in range(4):
            mms([(Pq[q][:], T.Ib[:], yv[0](512 * q, 512 * q + 512), True, False)] +
                [(Pq[q][:, 128 * c:128 * c + 128], T.RV[:, 128 * (4 * q + c):128 * (4 * q + c) + 128], T.lostB[:], False, c == 3) for c in range(4)],
                "Ib RV lostB x0_%d" % q, "P%d" % q)
            o = own(512 * q, 512 * q + 512)
            either(TS(o, Pq[q][:], 0.0, A.max), ACT(o, Pq[q][:], F.Relu), "P%d" % q, "yp%d" % q)
        send(T.xw0[:, 0:Y0 + 2048], "vac " + YP + " " + xn(0), T.xw0, Y0 + 2048, "xl0")
        move(T.f1[:], T.PK[:, 0:256], "PK", "f1 f1b")
        tt(T.km[:], T.PK[:, 256:512], T.f1[:], A.max, "PK f1 f1b", "km")
        either(TS(T.hiF[:], SL, hi, A.is_ge, 2.0 ** 25, A.mult), ACT(T.hiF[:], SL, F.Relu, scale=2.0 ** 25, bias=pc[:, 12:13]), "PY pc2 pc3", "hiF")
        either(TS(T.thr[:], SL, th, A.is_ge), ACT(T.thr[:], SL, F.Relu, bias=pc[:, 7:8]), "PY pc2 pc5", "thr")
        tt(T.km[:, 0:128], T.km[:, 0:128], T.km[:, 128:256], A.max, "km", "km")
        tt(T.mg[:], T.km[:, 0:128], T.hiF[:], A.min, "km hiF", "mg")
        tt(T.i1[:, 0:128], T.mg[:], T.dumK[:, 0:128], A.max, "mg dumK", "i1")
        ts(T.i1[:, 0:128], T.i1[:, 0:128], 16383, AND, "i1", "i1")
        cp(T.oK[:], T.i1[:, 0:128], "i1", "oK")
        for k in range(2):
            move((T.AX[:], T.oK[:, 64 * k:64 * k + 64]), T.zer[:], "oK zer", "AX")
        for j in range(4):
            tt(T.TG[:, 512 + 128 * j:640 + 128 * j], T.PK[:, 128 * j:128 * j + 128], T.mg[:], A.is_equal, "PK mg Gj", "lost%d" % j)
            mm(T.PX[:, 128 * j:128 * j + 128], [(T.If[:], pl(T.D, j)), (T.Ib[:], pl(T.isT, j)), (T.Ig[:], T.TG[:, 512 + 128 * j:640 + 128 * j])],
               "If Ib Ig D isT lost%d" % j, "PX")
        ts(T.ofp[:], T.PX[:], 0.25, A.mult, "PX", "ofp", 2063.625, A.add)
        if last:
            plus(T.V[:, 0:2048], yv[0](0, 2048), -16.0, xn(0), "V00 V01")
            dma([(T.yx[:], T.V[:, 0:2048])], "V00 V01", "", 512)
        move(T.snd[:, 768:1536], AXL, "AX", "msS")
        exchange(T.snd, 768, T.msR, 0, -1, "msS", "msR")
        if not last:
            iota(AXL, [[0, 768]], 64, 0, "AX")
        clear("PS", 512)
        left = [9]
        mms([(T.PS[:, 128 * j:128 * j + 128], T.I8[:], T.thr[:], False, False) for j in range(4)], "I8 thr", "PS", left)
        for k in range(8):
            prefetch(k, T.xw0[:], T.ofp[:, 64 * k:64 * k + 64], "vac xl0 ofp " + YP + " " + xn(0))
            more(T.PS[:, 64 * k:64 * k + 64], terms(T.Zq, lambda r: T.VA[:, 1024 * k + r:1024 * k + 1024:16]), "Zq W%d" % k, "PS", left)
        conv(T.PY[:, 0:48], T.Zq, lambda r: T.snd[:, r:768:16], "Zq snd snd1", "PY")
        tt(T.D[:, LK], T.PY[:, 0:48], T.D[:, LK], A.min, "PY DL", "DL")
        conv(T.PY[:, 48:96], T.Zq, lambda r: T.xw0[:, Y0 + 2048 + r:Y0 + 2816:16], "Zq xl0", "PY")
        ts(T.alive[:], T.PY[:, 48:96], 1.0, A.is_ge, "PY", "alive")
        tt(T.flG[:, 0:48], T.alive[:], T.held[:], A.is_gt, "alive held", "flG0")
        scan(T.cumG[:, 1:49], T.flG[:, 0:48], T.flG[:, 0:48], 0.0, A.add, A.max, "flG0", "cumGa cumG")
        mm(T.PY[:, 0:48], [(T.BOh[:], T.cumG[:, 0:48]), (T.TRI[:], T.flG[:, 0:48])], "BOh TRI cumG0 cumGa flG0", "PY")
        mm(T.PY[:, 48:49], [(T.BOh[:], T.cumG[:, 48:49])], "BOh cumGa", "PY")
        move(T.g1[:, 0:49], T.PY[:, 0:49], "PY", "g1")
        nL = T.g1[:, 48:49]
        if not last:
            conv(T.PY[:, 0:48], T.Zq, lambda r: T.snd[:, 768 + r:1536:16], "Zq msS", "PY")
            tt(T.held[:], T.alive[:], T.held[:], A.mult, "alive held", "held")
            tt(T.held[:], T.PY[:, 0:48], T.held[:], A.min, "PY held", "held")
        if t == RO - 2:
            move(T.dG[:, 0:768], T.msR[:], "msR", "dG")
            tt((T.AX[:], T.oL[:]), T.dG[:, 0:768], T.dT[:, 0:768], A.mult, "oL dG dT", "AX")
            iota(T.dT[:, 0:768], [[0, 768]], 64, 0, "dT")
        else:
            cp((T.AX[:], T.oL[:]), T.msR[:], "oL msR", "AX")
        dma([(T.Fb[:], T.AX[row1, 64:8256])], "AX", "Fb", 256)
        conv(T.PY[:, 0:48], T.Zq, lambda r: T.msR[:, r:768:16], "Zq msR", "PY")
        tt(T.D[:, LK], T.PY[:, 0:48], T.D[:, LK], A.min, "PY DL", "DL")
        if not last:
            ts(T.oN[:], T.D[:, LK], 0.25, A.mult, "DL", "oN", -0.375, A.add)
        ts(T.isL[:], T.gam[:], nL, A.is_lt, "gam gam2 g1", "isL")
        ts(T.flE[:, 512:528], T.D[:, 128 + 16 * t:144 + 16 * t], 63.5, A.is_lt, "DL", "flEL")
        mms([(T.P1[:, b:64:4], T.Qh[:, 144 * b + 3:144 * b + 131], T.flE[:, 512:528], True, True) for b in range(4)], "Qh flEL", "P1")
        move(T.flT[:, 528:592], T.P1[:, 0:64], "P1", "flT2")
        tt(T.Fb[:, t:512:4], T.Fb[:, t:512:4], T.keepB[:], A.min, "Fb keepB", "Fb")
        tt(T.TG[:, 512:1024], (T.Fb[:], T.oJ[:, 0:32]), T.TG[:, 0:512], A.mult, "Fb oJ Tt", "Gj lost0 lost1 lost2 lost3")
        if not last:
            dma([(T.AX[row1, 64:8256], T.Fb[:])], "Fb", "AX", 256)
        conv(T.PK[:, 0:32], T.Zb, lambda r: T.TG[:, 512 + r:1024:16], "Zb Gj", "PK")
        ts(T.j1[:, 0:32], T.PK[:, 0:32], -1.0 / 64, A.mult, "PK", "j1", 65535.0, A.add)
        for b in range(4):
            ts(T.j2[:, 32 * b:32 * b + 32], T.j1[:, 0:32], b, SH, "j1", "j2%d" % b, 0x1111, AND)
        for k in range(4):
            ts(T.AI[:, 128 * k:128 * k + 128], T.j2[:, 0:128], 4 * k, SH, "j20 j21 j22 j23 isT", "AI%d" % k, 1, AND)
        cp(T.flG[:, 48:560], T.AI[:, 0:512], "AI0 AI1 AI2 AI3", "flG1 AI")
        scan(T.cumG[:, 49:561], T.flG[:, 48:560], T.flG[:, 48:560], T.cumG[:, 48:49], A.add, A.max, "flG1 cumGa", "cumG")
        heads(T.cumG, "cumG cumG0 cumGa", 560, None, T.seb, "seb", T.ob, "ob", "PK")
        counts(T.flG, "flG0 flG1", 560, 512, T.wb, "wb", "P2", "P3")
        move((T.Lb[:], T.ob[:, 0:35]), T.wb[:, 0:560], "ob wb wb1", "Lb")
        mm(T.PK[:, 256:257], [(T.BOh[:], T.cumG[:, 560:561])], "BOh cumG", "PK")
        move(col[:, 5:6], T.PK[:, 256:257], "PK", "c5")
        run_down(T.Lb, "Lb", T.cwb, "cwb", 1088)
        back = [(T.cb[0:1, 0:128], T.cb[0:1, 896:964])]
        mm(T.PK[:, 64:132], back + terms(T.Zc, lambda r: T.cwb[:, r:1088:16]), "cb0 cb6 Zc cwb", "PK")
        either(TS(T.flE[:, 0:512], T.PS[:], 0.0, A.is_equal), ACT(T.flE[:, 0:512], T.PS[:], F.Relu, scale=-8.0, bias=1.0), "PS", "flP")
        for j in range(4):
            tt(pl(T.D, j), T.PS[:, 128 * j:128 * j + 128], pl(T.D, j), A.min, "PS D", "D")
        for b in range(4):
            mm(T.P0[:, b:512:4], [(T.Qh[:, 144 * b + 3 - j:144 * b + 131 - j], T.flE[:, 128 * j:128 * j + 128]) for j in range(4)], "Qh flP", "P0")
        move(T.flT[:, 0:512], T.P0[:], "P0", "flT0")
        scan(T.cumT[:, 1:513], T.flT[:, 0:512], T.flT[:, 0:512], 0.0, A.add, A.max, "flT0", "cumT")
        mm(T.PY[:, 0:1], [(T.BOh[:], T.cumT[:, 512:513])], "BOh cumT", "PY")
        ts(col[:, 1:2], T.PY[:, 0:1], 1024.0, A.min, "PY g1", "c1", nL, A.max)
        ts(col[:, 0:1], T.PY[:, 0:1], 1024.0, A.min, "PY", "c0")
        ts(col[:, 4:5], T.PY[:, 0:1], 1024.0, A.is_gt, "PY", "c4", 64.0, A.mult)
        ts(col[:, 3:4], col[:, 1:2], pf[:, 7:8], A.mult, "c1 pf7", "c3")
        scan(T.cumT[:, 513:593], T.flT[:, 512:592], T.flT[:, 512:592], col[:, 3:4], A.add, A.max, "flT1 flT2 c3", "cumTa")
        heads(T.cumT, "cumT cumT0 cumTa", 592, T.CL[:, 0:74], T.sea, "sea", T.oa, "oa", "PX")
        counts(T.flT, "flT0 flT1 flT2", 592, 496 + 64 * t, T.wa, "wa", "P0", "P1")
        move((T.La[:], T.oa[:, 0:37]), T.wa[:, 0:592], "oa wa wa1", "La")
        mm(T.PY[:, 0:1], [(T.BOh[:], T.cumT[:, 592:593])], "BOh cumTa", "PY")
        ts(col[:, 6:7], col[:, 1:2], 64.0, A.add, "c1", "c6")
        ts(col[:, 2:3], T.PY[:, 0:1], col[:, 6:7], A.min, "PY c6", "c2")
        ts(col[:, 8:11], col[:, 0:3], col[:, 5:6], A.min, "c0 c1 c2 c5", "c8")
        ts(T.DEC[:, 1096:1097], col[:, 4:5], 1.0, A.add, "c4 pf11", "DEC2", pf[:, 11:12], A.mult)
        run_down(T.La, "La", T.cwa, "cwa", 1088, 72, "DEC2")
        CK = pc[:, 13 + t:14 + t]
        ts(T.j1[:, 0:68], T.PK[:, 64:132], K, A.mult, "PK pc pc4", "j1", CK, A.add)
        ts(T.f2[:, 0:64], T.PK[:, 64:128], 2815.0, A.add, "PK", "f2")
        mm(T.PK[:, 132:200], back + terms(T.Zc, lambda r: T.cwb[:, 68 * r:68 * r + 68]), "cb0 cb6 Zc cwb", "PK")
        ts(T.j1[:, 68:136], T.PK[:, 132:200], K, A.mult, "PK pc pc4", "j1b", CK, A.add)
        if not last:
            dma([(T.UA[row, :], T.D[:])], "D DL", "UA", 360)
            refill(T.Lb, "Lb")
            refill(T.La, "La")
            for k, TR in enumerate((T.TRI, T.TRs)):
                mm(T.PY[:, 128 + 128 * k:256 + 128 * k], [(T.BOh[:], T.cumT[:, 0:512:4])] +
                   [(TR[:], T.flE[:, 128 * j:128 * j + 128]) for j in range(4)], "BOh TRI TRs cumT cumT0 flP", "PY")
            act(T.f1[:, 0:128], T.PY[:, 256:384], F.Relu, "PY", "f1", scale=-1.0, bias=1024.0)
            act(T.f1[:, 128:256], T.PY[:, 128:256], F.Relu, "PY", "f1b", scale=-1.0, bias=1024.0)
            tt(T.f3[:, 0:128], T.f1[:, 0:128], T.f1[:, 128:256], A.subtract, "f1 f1b", "f3")
            ts(T.f1[:, 128:256], T.f1[:, 128:256], -1.0, A.mult, "f1b f3", "f1b", 1039.0, A.add)
            ts(T.f3[:, 0:128], T.f3[:, 0:128], 2048.0, A.mult, "f3", "f3")
            tt(T.f3[:, 0:128], T.f3[:, 0:128], T.f1[:, 128:256], A.min, "f1b f3", "f3")
            cp(T.oE[:], T.f3[:, 0:128], "f3", "oE")
            for k, bank in enumerate(("PS", "PY")):
                a = 512 * k + (k == 0)
                o, p = T.TG[:, a:512 * k + 512], T[bank][:, a - 512 * k:512]
                mm(p, [(T.Wv[:, 0:128], T.cwa[:, a:512 * k + 512]), (T.Wv[:, 128:256], T.cwa[:, a - 1:512 * k + 511])], "Wv Wv1 cwa", bank)
                either(TS(o, p, 0.0, A.is_equal), ACT(o, p, F.Relu, scale=-1.0, bias=1.0), bank, ("Tt", "Gj")[k])
            left = [sums(q, False) for q in range(4)]
            ts(T.pre[:], T.gam[:, 0:64], col[:, 5:6], A.is_ge, "gam c5", "pre", float(W0 - 32 - PL), A.mult)
            ts(T.j2[:, 0:64], T.j1[:, 0:64], 2, SH, "j1", "j20 j21", 2047, AND)
            tt(T.f2[:, 0:64], T.f2[:, 0:64], T.isL[:, 0:64], A.mult, "f2 isL", "f2")
            tt(T.pre[:], T.pre[:], T.j2[:, 0:64], A.max, "pre j20 j21", "pre")
            tt(T.f2[:, 0:64], T.f2[:, 0:64], T.pre[:], A.max, "f2 pre", "f2")
            ts(T.oS[:], T.f2[:, 0:64], 16.0, A.add, "f2", "oS")
            for k in range(2):
                move(T.M[:, 512 * k:512 * k + 512], (T.xw0[:, PL:W0], T.oS[:, 32 * k:32 * k + 32]), "oS vac xl0 " + xn(0), "rr%d" % k)
            scan(T.xw0[:, 16:1040], T.TG[:], T.M[:], 0.0, A.mult, A.add, "Tt Gj rr0 rr1", "yp0 yp1")
            for q in range(4):
                c, vn = T.V[:, 1024 * q:1024 * q + 512], "V%d%d" % (q // 2, q % 2)
                move(c, (T.xw0[:, 0:1040], T.oE[:, 32 * q:32 * q + 32]), "yp0 yp1 vac oE", vn)
                more(Pq[q][:], [(T.Ib[:], c)], "Ib " + vn, "P%d" % q, left[q])
        conv(T.PX[:, 128:196], T.Zt if last else T.Zc, lambda r: T.cwa[:, r:1088:16], "Zc Zt cwa", "PX")
        conv(T.PX[:, 196:264], T.Zc, lambda r: T.cwa[:, 68 * r:68 * r + 68], "Zc cwa", "PX")
        ts(T.g2[:, 0:68], T.PK[:, 132:200], 4.0, A.mult, "PK", "g2", 11260.0, A.add)
        ts(T.j1[:, 68:136], T.j1[:, 68:136], 8191, AND, "j1b", "j1b")
        ts(T.j1[:, 0:68], T.j1[:, 0:68], 8191, AND, "j1", "j1")
        tt(T.g2[:, 0:68], T.g2[:, 0:68], T.isL[:, 68:136], A.mult, "g2 isL", "g2")
        tt(T.valG[:], T.g2[:, 0:68], T.j1[:, 68:136], A.max, "g2 j1b", "valG")
        if not last:
            plus(T.valG[:], T.valG[:], 64.0, "valG", "valG")
        dma([(T.dG[row, :], T.valG[:])], "valG", "dG dG1", 40)
        plus(T.valT[:], T.PX[:, 196:264], -65.0 if last else -1.0, "PX", "valT")
        dma([(T.dT[row, :], T.valT[:])], "valT", "dT", 40)
        inv, invX = T.inv[:, 0:68], T.inv[:, 68:136]
        ts(inv, T.gam[:, 0:68], col[:, 8:9], A.is_ge, "gam c8", "inv")
        ts(T.f2[:, 68:136], T.gam[:, 0:68], col[:, 9:10], A.is_lt, "gam c8", "f2b")
        ts(T.f5[:, 0:68], T.gam[:, 0:68], col[:, 10:11], A.is_ge, "gam c8", "f5")
        tt(invX, inv, T.f2[:, 68:136], A.mult, "inv f2b", "invX")
        tt(invX, invX, T.f5[:, 0:68], A.max, "invX f5", "invX")
        if not last:
            ts(T.i1[:, 0:68], T.PX[:, 128:196], 1.0 / 64, A.mult, "PX", "i1", -96.5 / 64, A.add)
            ts(T.posT[:], T.PX[:, 128:196], 176.0, A.mult, "PX", "posT", -65.0 * 176, A.add)
            ts(T.f4[:, 68:136], T.i1[:, 0:68], -11263.0, A.mult, "i1", "f4b")
            tt(T.dA[:], invX, T.dumA[:, 0:68], A.mult, "invX dumA", "dA")
            ts(T.f5[:, 68:136], invX, -20000.0, A.mult, "invX", "f5b", 20000.0, A.add)
            tt(T.posT[:], T.posT[:], T.f4[:, 68:136], A.add, "posT f4b", "posT")
            tt(T.posT[:], T.posT[:], T.f5[:, 68:136], A.min, "posT f5b", "posT")
            tt(T.posT[:], T.posT[:], T.dA[:], A.max, "posT dA", "posT")
            cp(T.oT[:], T.posT[:], "posT", "oT")
            move((T.UA[:], T.oT[:]), T.dG[:], "oT dG dG1", "UA")
            dma([(T.D[:], T.UA[row, :])], "UA", "D DL", 360)
            tt(invX, invX, T.isL[:, 0:68], A.max, "invX isL", "invX")
            tt(T.dX[:], invX, T.dumK[:, 72:140], A.mult, "invX dumK", "dX")
            tt(T.f2[:, 68:136], T.j1[:, 0:68], T.dX[:], A.max, "j1 dX", "f2b")
            ts(T.oG[:], T.f2[:, 68:136], 64.0, A.add, "f2b", "oG")
            ts(T.f4[:, 0:48], T.g1[:, 0:48], col[:, 0:1], A.is_le, "g1 c0", "f4")
            tt(T.f4[:, 0:48], T.f4[:, 0:48], T.flG[:, 0:48], A.mult, "f4 flG0", "f4")
            tt(T.held[:], T.held[:], T.f4[:, 0:48], A.add, "held f4", "held")
        else:
            ts(T.dA[:], T.gam[:, 0:68], 8448.0, A.add, "gam", "dA")
            ts(T.posT[:], T.PX[:, 128:196], 16.0 * 15 * 32800 - 965, A.add, "PX", "posT")
            tt(T.dX[:], T.dA[:], inv, A.mult, "dA inv", "dX")
            tt(T.posT[:], T.posT[:], T.dX[:], A.max, "posT dX", "posT")
            cp(T.oT[:], T.posT[:], "posT", "oT")
            ts(T.AI[:], T.D[:], -64.0, A.add, "D DL", "AI AI0 AI1 AI2 AI3", -1.0, A.max)
            move(T.Pf[:], T.Qh[:], "Qh", "Pf")
            cp(T.D[:], T.AI[:], "AI", "D DL")
            for b in range(4):
                mm(T.PS[:, b:512:4], [(T.Pf[:, 144 * b + 3 - j:144 * b + 131 - j], pl(T.D, j)) for j in range(4)], "Pf D", "PS")
            move(T.D[:, 0:512], T.PS[:], "PS", "D DL")
            ta, tb = T.V[:, 4096:5120], T.V[:, 6144:7168]
            move(ta, (T.Fb[:], T.lpre[:]), "Fb lpre", "V20")
            turned(tb, ta, "V20", "V30")
            either(TS(T.Fb[:], (tb, T.lpost[:]), 256.0, A.mult, -1.0, A.add), ACT(T.Fb[:], (tb, T.lpost[:]), F.Identity, scale=256.0, bias=-1.0), "V30 lpost", "Fb")
            tt(T.Eb[:], T.Eb[:], T.Fb[:], A.min, "Eb Fb", "Eb")
            dma([(T.UA[row, 0:8192], T.D[:, 0:512])], "D", "UAn", 256)
            dma([(T.AX[row, 0:8192], T.Eb[:])], "Eb", "AX", 256)
            tt(invX, invX, T.isL[:, 0:68], A.max, "invX isL", "invX")
            ts(T.i2[:, 0:68], T.j1[:, 0:68], 15, AND, "j1", "i2")
            ts(T.i2[:, 68:136], T.j1[:, 0:68], 4, SH, "j1", "i3")
            tt(T.dX[:], invX, T.dA[:], A.mult, "invX dA", "dX")
            ts(T.f2[:, 0:68], T.i2[:, 0:68], 512.0, A.mult, "i2", "f2")
            tt(T.f2[:, 0:68], T.f2[:, 0:68], T.i2[:, 68:136], A.add, "f2 i3", "f2")
            tt(T.f2[:, 0:68], T.f2[:, 0:68], T.dX[:], A.max, "f2 dX", "f2")
            cp(T.oG[:], T.f2[:, 0:68], "f2", "oG")
            cp((T.AX[:], T.oG[:]), T.dT[:], "oG dT", "AX")
            dma([(T.ya[:], T.AX[row, 0:8192])], "AX", "", 256)
            cp((T.UA[:], T.oT[:, 0:64]), T.dG[:, 0:1024], "oT dG dG1", "UA UAb UAn")
            dma([(T.yd[:], T.UA[row, 0:8192])], "UA", "", 256, q="s")

    if "order" not in PLAN:
        PLAN["order"] = schedule(ops)
    toks, at, cnt, known, seen = {}, {}, {}, {}, {q: {} for q in Q}

    def wait(q, need):
        for s, n in need:
            if seen[q].get(s, 0) < n and not q == "t" == s[1]:
                Q[q].wait_ge(T.sem[s], n)
                seen[q][s] = n
                for a, b in known.get((s, n), {}).items():
                    seen[q][a] = max(seen[q].get(a, 0), b)
    for i, q in PLAN["order"]:
        wait(q, [tok for p in sorted(ops[i][0], key=lambda p: -at[p]) for tok in toks[p]])
        at[i] = len(at)
        got = calls[i][q]()
        if not isinstance(got, list):
            s = "q" + q
            got.then_inc(T.sem[s], 1)
            got = [(s, cnt.get(s, 0) + 1)]
        toks[i] = got
        known[got[0]] = dict(seen[q])
        cnt.update(got)
    wait("g", list(cnt.items()))
